import numpy as np
import ml_dtypes


def mxq(x, axis, fmt="e4m3"):
    dtype, down = {"e4m3": (ml_dtypes.float8_e4m3fn, 7), "e5m2": (ml_dtypes.float8_e5m2, 14)}[fmt]
    v = np.moveaxis(np.asarray(x, np.float32).astype(ml_dtypes.bfloat16).astype(np.float64), axis, -1)
    blocks = v.reshape(v.shape[:-1] + (-1, 32))
    amax = np.abs(blocks).max(-1, keepdims=True)
    byte = np.maximum(np.where(amax > 0, np.frexp(amax)[1] - 1 + 127, 0) - down, 1)
    scale = np.exp2(byte - 127.0)
    codes = (blocks / scale).astype(np.float32).astype(dtype).astype(np.float64)
    return np.moveaxis((codes * scale).reshape(v.shape), -1, axis)


WIDE = False


def mx_kscale(k):
    if not WIDE:
        return np.ones(k)
    levels = np.array([10, -10, 5, -5, 0])
    if k % 512:
        return np.exp2(np.random.permutation(np.resize(levels, k // 32))).repeat(32)
    a = np.empty((k // 512, 16))
    for p in range(k // 512):
        a[p, :8] = np.random.permutation(np.resize(levels, 8))
        for g in range(8):
            far = levels[np.abs(levels - a[p, g]) >= 10]
            a[p, g + 8] = far[np.random.randint(len(far))]
    return np.exp2(a.ravel()).repeat(32)


def f64(x):
    return np.asarray(x).astype(np.float64)


def striped(idx):
    return np.tile(idx.reshape(-1, 16).T, (8, 1)).astype(np.uint16)


def unstriped(offs):
    return offs[:16].T.reshape(-1).astype(np.int64)


E2M1 = np.array([0.0, 0.5, 1.0, 1.5, 2.0, 3.0, 4.0, 6.0, -0.0, -0.5, -1.0, -1.5, -2.0, -3.0, -4.0, -6.0])


def pack_weight(w, fmt):
    k, n = w.shape
    w = f64(np.asarray(w, np.float32).astype(ml_dtypes.bfloat16)).reshape(k // 32, 32, n)
    amax = np.abs(w).max(1)
    if fmt == "e4m3":
        byte = np.frexp(amax)[1] - 1 + 127 - 7
    else:
        mant, ex = np.frexp(amax / 6.0)
        byte = np.where(mant > 0.5, ex, ex - 1) + 127
    byte = np.clip(np.where(amax > 0, byte, 1), 1, 254)
    scaled = (w * np.exp2(127.0 - byte)[:, None, :]).reshape(k, n).astype(np.float32)
    by_word = np.ascontiguousarray(scaled.reshape(k // 512, 128, 4, n).transpose(0, 1, 3, 2))
    if fmt == "e4m3":
        words = by_word.astype(ml_dtypes.float8_e4m3fn).view(np.uint8)
    else:
        c = by_word.astype(ml_dtypes.float4_e2m1fn).view(np.uint8) & 0xF
        words = (c[..., 0::2] | (c[..., 1::2] << 4)).reshape(k // 512, 128, 2 * n)
    return np.ascontiguousarray(words), np.ascontiguousarray(byte.astype(np.uint8).reshape(k // 512, 16, n))


def unpack_weight(words, scales, fmt):
    g, _, n = scales.shape
    words = np.ascontiguousarray(words).reshape(g, 128, n, -1)
    if fmt == "e4m3":
        vals = words.view(ml_dtypes.float8_e4m3fn).astype(np.float64)
    else:
        nib = np.empty((g, 128, n, 4), np.uint8)
        nib[..., 0::2] = words & 0xF
        nib[..., 1::2] = words >> 4
        vals = E2M1[nib]
    vals = vals * np.repeat(np.exp2(scales.astype(np.float64) - 127.0), 8, axis=1)[..., None]
    return vals.transpose(0, 1, 3, 2).reshape(g * 512, n)


def gelu(v):
    return 0.5 * v * (1.0 + np.tanh(np.sqrt(2.0 / np.pi) * (v + 0.044715 * v**3)))


K, H, N, T, S = 512, 1024, 384, 4096, 1024


def setup_inputs():
    n = np.random.standard_normal
    s = mx_kscale(K)[:, None]
    u = mx_kscale(H)[:, None]
    tab_words, tab_scales = pack_weight(n((K, T)) * s, "e4m3")
    wm_words, wm_scales = pack_weight(n((K, H)) / np.sqrt(K) / s * u.T, "e2m1")
    wd_words, wd_scales = pack_weight(n((K, H)) / np.sqrt(K) / s * u.T, "e4m3")
    return {
        "tab_words": tab_words, "tab_scales": tab_scales,
        "offs": striped(np.random.permutation(T)[:S]),
        "offs2": striped(np.random.permutation(T)[:S]),
        "offs3": striped(np.random.permutation(T)[:S]),
        "wp": (n((K, H)) / np.sqrt(K) / s * u.T).astype(np.float32),
        "wm_words": wm_words, "wm_scales": wm_scales,
        "wd_words": wd_words, "wd_scales": wd_scales,
        "wo": (n((H, N)) / np.sqrt(H) / u).astype(np.float32),
        "bo": (0.5 * n(N)).astype(np.float32),
    }


def reference(tab_words, tab_scales, offs, offs2, offs3, wp, wm_words, wm_scales, wd_words, wd_scales, wo, bo):
    vp = unpack_weight(tab_words, tab_scales, "e4m3")[:, unstriped(offs)]
    vm = unpack_weight(tab_words, tab_scales, "e4m3")[:, unstriped(offs2)]
    vd = unpack_weight(tab_words, tab_scales, "e4m3")[:, unstriped(offs3)]
    p = mxq(f64(wp), 0, "e4m3").T @ vp
    m = unpack_weight(wm_words, wm_scales, "e2m1").T @ vm
    d = unpack_weight(wd_words, wd_scales, "e4m3").T @ vd
    h = np.maximum(np.abs(p), np.abs(m)) - d
    y = mxq(f64(wo), 0, "e4m3").T @ mxq(h, 0, "e4m3")
    return y + f64(bo)[:, None]

@@ -1,0 +1,267 @@
+from contextlib import ExitStack
+
+import concourse.mybir as mybir
+
+K, H, N, T, S = 512, 1024, 384, 4096, 1024
+FLOPS = 2 * S * (3 * K * H + H * N)
+
+F32 = mybir.dt.float32
+BF16 = mybir.dt.bfloat16
+I32 = mybir.dt.int32
+U32 = mybir.dt.uint32
+U16 = mybir.dt.uint16
+U8 = mybir.dt.uint8
+FP8X4 = mybir.dt.float8_e4m3fn_x4
+FP4X4 = mybir.dt.float4_e2m1fn_x4
+ALU = mybir.AluOpType
+ACT = mybir.ActivationFunctionType
+
+P = 128
+PACK = 4
+PASSES = H // (P * PACK)
+HALF = 512
+CHUNK = 128
+N_TILES = N // P
+GROUPS = (256, 256, 256, 128, 128)
+
+
+def tile_list_payment_fraud_decoder_kernel(
+    tc, tab_words, tab_scales, offs, offs2, offs3, wp, wm_words, wm_scales, wd_words, wd_scales, wo, bo, out
+):
+    nc = tc.nc
+    with ExitStack() as ctx:
+        keep = ctx.enter_context(tc.tile_pool(name="keep", bufs=1))
+        ring = ctx.enter_context(tc.tile_pool(name="ring", bufs=1))
+        psum = ctx.enter_context(tc.psum_pool(name="psum", bufs=2))
+
+        lists = {}
+        for role, src in (("p", offs), ("m", offs2), ("d", offs3)):
+            lists[role] = keep.tile([P, S // 16], U16, name="list_" + role)
+            nc.sync.dma_start(lists[role][:], src)
+
+        tab_sc = keep.tile([P, T], U8, align_bytes=64)
+        for q in range(4):
+            rows = tab_scales[0, 4 * q : 4 * q + 4, :].bitcast(I32)
+            nc.sync.dma_start(
+                out=tab_sc[32 * q : 32 * q + 32, :].bitcast(I32),
+                in_=rows.unsqueeze(0).to_broadcast([8, 4, T // 4]),
+            )
+        wp_view = wp.rearrange("(p j) c -> p j c", j=PACK)
+        wp_raw = [keep.tile([P, PACK, 512], F32, name="wp_raw%d" % b) for b in range(PASSES)]
+        for b in range(PASSES):
+            nc.sync.dma_start(out=wp_raw[b][:], in_=wp_view[:, :, 512 * b : 512 * (b + 1)])
+        tab = keep.tile([P, T], I32, align_bytes=64)
+        nc.sync.dma_start(out=tab[:], in_=tab_words[0].rearrange("p n t -> p (n t)").bitcast(I32))
+
+        def load_scales(src, name):
+            raw = keep.tile([P, H], U8, align_bytes=64, name=name)
+            nc.gpsimd.memset(raw[:].bitcast(I32), 0)
+            for q in range(4):
+                nc.sync.dma_start(
+                    out=raw[32 * q : 32 * q + 4, :].bitcast(I32), in_=src[0, 4 * q : 4 * q + 4, :].bitcast(I32)
+                )
+            return raw
+
+        wm_raw = keep.tile([P, 2 * H], U8, align_bytes=64)
+        nc.sync.dma_start(out=wm_raw[:].bitcast(I32), in_=wm_words[0].bitcast(I32))
+        wm_sc_raw = load_scales(wm_scales, "wm_sc_raw")
+        wd_raw = keep.tile([P, H], I32, align_bytes=64)
+        nc.sync.dma_start(out=wd_raw[:], in_=wd_words[0].rearrange("p n t -> p (n t)").bitcast(I32))
+        wd_sc_raw = load_scales(wd_scales, "wd_sc_raw")
+        wo_view = wo.rearrange("(b q t i) n -> b t q i n", b=PASSES, t=PACK, i=8)
+        wo_raw = keep.tile([P, PASSES, PACK, N], F32)
+        for b in range(PASSES):
+            for t in range(PACK):
+                nc.sync.dma_start(out=wo_raw[:, b, t, :], in_=wo_view[b, t])
+        bias = keep.tile([P, N_TILES], F32)
+        with nc.allow_non_contiguous_dma(reason="one bias value a partition"):
+            nc.sync.dma_start(out=bias[:], in_=bo.rearrange("(c p) -> p c", p=P))
+
+        picked = {}
+        picked_sc = {}
+
+        def gather_scales(role, half):
+            dst = keep.tile([P, HALF], U8, align_bytes=64, name="picked_sc_%s%d" % (role, half))
+            cols = slice(half * HALF // 16, (half + 1) * HALF // 16)
+            nc.vector.tensor_copy(dst[:], tab_sc[:].indirect(lists[role][:, cols]))
+            picked_sc[role, half] = dst
+
+        def gather_words(role, half):
+            dst = keep.tile([P, HALF], U32, align_bytes=64, name="picked_%s%d" % (role, half))
+            cols = slice(half * HALF // 16, (half + 1) * HALF // 16)
+            nc.vector.tensor_copy(dst[:], tab[:].bitcast(U32).indirect(lists[role][:, cols]))
+            picked[role, half] = dst
+
+        def reorder(dst, src):
+            nc.vector.tensor_copy(
+                out=dst.rearrange("p (b t q i) -> p b t q i", b=PASSES, t=PACK, q=16),
+                in_=src.rearrange("p (b q t i) -> p b t q i", b=PASSES, t=PACK, q=16),
+            )
+
+        wm_codes = keep.tile([P, 2 * H], U8, align_bytes=64)
+        wd_codes = keep.tile([P, H], I32, align_bytes=64)
+        wm_sc = keep.tile([P, H], U8, align_bytes=64)
+        wd_sc = keep.tile([P, H], U8, align_bytes=64)
+        wp_bf = [keep.tile([P, PACK, P, PACK], BF16, align_bytes=64, name="wp_bf%d" % b) for b in range(PASSES)]
+        wp_codes = [keep.tile([P, 512], U32, align_bytes=64, name="wp_codes%d" % b) for b in range(PASSES)]
+        wp_sc = [keep.tile([P, 512], U8, align_bytes=64, name="wp_sc%d" % b) for b in range(PASSES)]
+
+        def round_wp(b):
+            src = wp_raw[b][:].rearrange("p j (q t i) -> p t q i j", t=PACK, i=8)
+            for t in range(PACK):
+                nc.scalar.copy(out=wp_bf[b][:, t].rearrange("p (q i) j -> p q i j", i=8), in_=src[:, t])
+
+        def quantize_wp(b):
+            nc.vector.quantize_mx(
+                out=wp_codes[b][:].bitcast(FP8X4),
+                scales=wp_sc[b][:],
+                in_=wp_bf[b][:].rearrange("p t c j -> p (t c j)"),
+            )
+
+        wo_bf = keep.tile([P, PASSES * N, PACK], BF16, align_bytes=64)
+        wo_codes = keep.tile([P, PASSES * N], U32, align_bytes=64)
+        wo_sc = keep.tile([P, PASSES * N], U8, align_bytes=64)
+
+        def round_wo(b):
+            nc.scalar.copy(out=wo_bf[:, b * N : (b + 1) * N, :], in_=wo_raw[:, b].rearrange("p t n -> p n t"))
+
+        def quantize_wo():
+            for c0, c1 in ((0, 512), (512, 768)):
+                nc.vector.quantize_mx(
+                    out=wo_codes[:, c0:c1].bitcast(FP8X4),
+                    scales=wo_sc[:, c0:c1],
+                    in_=wo_bf[:, c0:c1, :].rearrange("p c j -> p (c j)"),
+                )
+
+        def stationary(role, b, t):
+            cols = slice((b * PACK + t) * P, (b * PACK + t + 1) * P)
+            if role == "p":
+                local = slice(t * P, (t + 1) * P)
+                return wp_codes[b][:, local].bitcast(FP8X4), wp_sc[b][:, local]
+            if role == "m":
+                return wm_codes[:, 2 * cols.start : 2 * cols.stop].bitcast(FP4X4), wm_sc[:, cols]
+            return wd_codes[:, cols].bitcast(FP8X4), wd_sc[:, cols]
+
+        def project(role, b, j0):
+            half, c0 = divmod(j0, HALF)
+            bank = psum.tile([P, PACK, CHUNK], F32, name="bank_" + role)
+            for t in range(PACK):
+                codes, scales = stationary(role, b, t)
+                nc.tensor.matmul_mx(
+                    out=bank[:, t, :],
+                    lhsT=codes,
+                    lhsT_scale=scales,
+                    rhs=picked[role, half][:, c0 : c0 + CHUNK].bitcast(FP8X4),
+                    rhs_scale=picked_sc[role, half][:, c0 : c0 + CHUNK],
+                    start=True,
+                    stop=True,
+                )
+            return bank[:].rearrange("p t n -> p n t")
+
+        units = []
+        j0 = 0
+        for g, width in enumerate(GROUPS):
+            for b in range(PASSES):
+                for c0 in range(0, width, CHUNK):
+                    units.append((g, j0, width, b, c0))
+            j0 += width
+
+        h_bf, h_codes, h_sc, larger, d_bank = {}, {}, {}, {}, {}
+
+        def front(unit):
+            g, j0, width, b, c0 = unit
+            mags = []
+            for role in "pm":
+                bank = project(role, b, j0 + c0)
+                mag = ring.tile([P, CHUNK, PACK], F32, name="mag_" + role, bufs=8)
+                nc.scalar.activation(out=mag[:], in_=bank, func=ACT.Abs)
+                mags.append(mag)
+            d_bank[unit] = project("d", b, j0 + c0)
+            larger[unit] = ring.tile([P, CHUNK, PACK], F32, name="larger", bufs=3)
+            nc.vector.tensor_tensor(out=larger[unit][:], in0=mags[0][:], in1=mags[1][:], op=ALU.max)
+
+        def subtract(unit):
+            g, j0, width, b, c0 = unit
+            if c0 == 0:
+                h_bf[g, b] = keep.tile([P, width, PACK], BF16, align_bytes=64, name="h_bf%d_%d" % (g, b))
+            nc.vector.tensor_tensor(
+                out=h_bf[g, b][:, c0 : c0 + CHUNK, :], in0=larger[unit][:], in1=d_bank[unit], op=ALU.subtract
+            )
+
+        def quantize_h(unit):
+            g, j0, width, b, c0 = unit
+            if c0 + CHUNK < width:
+                return
+            h_codes[g, b] = keep.tile([P, width], U32, align_bytes=64, name="h_codes%d_%d" % (g, b))
+            h_sc[g, b] = keep.tile([P, width], U8, align_bytes=64, name="h_sc%d_%d" % (g, b))
+            nc.vector.quantize_mx(
+                out=h_codes[g, b][:].bitcast(FP8X4),
+                scales=h_sc[g, b][:],
+                in_=h_bf[g, b][:].rearrange("p c j -> p (c j)"),
+            )
+            if b == PASSES - 1:
+                decode(g, j0, width)
+
+        out_view = out.rearrange("(c p) j -> p c j", p=P)
+
+        def decode(g, j0, width):
+            last = g == len(GROUPS) - 1
+            if last:
+                acc = [psum.tile([P, width], F32, name="bank_" + role)[:] for role in "pmd"]
+                order = [(n, b) for b in range(PASSES) for n in range(N_TILES)]
+            else:
+                both = psum.tile([P, 4, 256], F32, name="bank_y", bufs=1)
+                acc = [both[:, n, 0:width] for n in range(N_TILES)]
+                order = [(n, b) for n in range(N_TILES) for b in range(PASSES)]
+            result = keep.tile([P, N_TILES, width], F32, name="result%d" % g)
+            for n, b in order:
+                cols = slice(b * N + n * P, b * N + (n + 1) * P)
+                nc.tensor.matmul_mx(
+                    out=acc[n],
+                    lhsT=wo_codes[:, cols].bitcast(FP8X4),
+                    lhsT_scale=wo_sc[:, cols],
+                    rhs=h_codes[g, b][:].bitcast(FP8X4),
+                    rhs_scale=h_sc[g, b][:],
+                    start=(b == 0),
+                    stop=(b == PASSES - 1),
+                )
+            for n in range(N_TILES):
+                if last and n == 1:
+                    nc.vector.tensor_scalar(
+                        out=result[:, n, :], in0=acc[n], scalar1=bias[:, n : n + 1], scalar2=None, op0=ALU.add
+                    )
+                else:
+                    nc.scalar.activation(out=result[:, n, :], in_=acc[n], func=ACT.Identity, bias=bias[:, n : n + 1])
+            nc.sync.dma_start(out=out_view[:, :, j0 : j0 + width], in_=result[:])
+
+        for role in "pmd":
+            gather_scales(role, 0)
+        round_wp(0)
+        round_wp(1)
+        gather_scales("p", 1)
+        quantize_wp(0)
+        gather_scales("m", 1)
+        gather_scales("d", 1)
+        quantize_wp(1)
+        gather_words("p", 0)
+        reorder(wm_codes[:].bitcast(I32), wm_raw[:].bitcast(I32))
+        reorder(wm_sc[:].bitcast(I32), wm_sc_raw[:].bitcast(I32))
+        gather_words("m", 0)
+        gather_words("d", 0)
+        reorder(wd_codes[:], wd_raw[:])
+        reorder(wd_sc[:].bitcast(I32), wd_sc_raw[:].bitcast(I32))
+
+        extra = {1: "p", 3: "m", 5: "d"}
+        for i in range(len(units) + 2):
+            if i < len(units):
+                front(units[i])
+            if i in extra:
+                gather_words(extra[i], 1)
+            if i in (1, 2):
+                round_wo(i - 1)
+            if i == 4:
+                quantize_wo()
+            if 0 <= i - 1 < len(units):
+                subtract(units[i - 1])
+            if 0 <= i - 2 < len(units):
+                quantize_h(units[i - 2])

@@ -22,7 +22,17 @@ PASSES = H // (P * PACK)
 HALF = 512
 CHUNK = 128
 N_TILES = N // P
+WO_STEP = 96
 GROUPS = (256, 256, 256, 128, 128)
+GROUP_ORDER = ((0,0),(0,1),(1,0),(1,1),(2,0),(2,1),(3,0),(3,1),(4,0),(4,1))
+ON_GPSIMD = ()
+ROUND_ON_GPSIMD = ""
+SINGLE_FROM = 0
+MAG_BUFS = 8
+LARGER_BUFS = 3
+MOVED_BUFS = 2
+LOADS = "lp lm tt ld wp0 wp1 wm sm tab wo0 wd sd wo1 bo"
+STEPS = "gsp2 rp0 rp1 gsm2 qp0 gsd2 xm qp1 gwp0 gwm0 gwp1 gwm1 gwd2 xd f0 f1 ro0 s0 f2 s1 q0 f3 ro1 s2 q1 f4 qo s3 q2 f5 s4 q3 f6 s5 q4 f7 s6 q5 f8 s7 q6 f9 s8 q7 f10 s9 q8 f11 s10 q9 f12 s11 q10 f13 s12 q11 f14 s13 q12 f15 s14 q13 s15 q14 q15"
 
 
 def tile_list_payment_fraud_decoder_kernel(
@@ -34,59 +44,81 @@ def tile_list_payment_fraud_decoder_kernel(
         ring = ctx.enter_context(tc.tile_pool(name="ring", bufs=1))
         psum = ctx.enter_context(tc.psum_pool(name="psum", bufs=2))
 
-        lists = {}
-        for role, src in (("p", offs), ("m", offs2), ("d", offs3)):
-            lists[role] = keep.tile([P, S // 16], U16, name="list_" + role)
-            nc.sync.dma_start(lists[role][:], src)
-
-        tab_sc = keep.tile([P, T], U8, align_bytes=64)
-        for q in range(4):
-            rows = tab_scales[0, 4 * q : 4 * q + 4, :].bitcast(I32)
-            nc.sync.dma_start(
-                out=tab_sc[32 * q : 32 * q + 32, :].bitcast(I32),
-                in_=rows.unsqueeze(0).to_broadcast([8, 4, T // 4]),
-            )
+        lists = {role: keep.tile([P, S // 16], U16, name="list_" + role) for role in "pmd"}
+        tab_sc = keep.tile([P, T], U8, align_bytes=64, name="tab_sc")
+        tab = keep.tile([P, T], I32, align_bytes=64, name="tab")
         wp_view = wp.rearrange("(p j) c -> p j c", j=PACK)
         wp_raw = [keep.tile([P, PACK, 512], F32, name="wp_raw%d" % b) for b in range(PASSES)]
-        for b in range(PASSES):
-            nc.sync.dma_start(out=wp_raw[b][:], in_=wp_view[:, :, 512 * b : 512 * (b + 1)])
-        tab = keep.tile([P, T], I32, align_bytes=64)
-        nc.sync.dma_start(out=tab[:], in_=tab_words[0].rearrange("p n t -> p (n t)").bitcast(I32))
-
-        def load_scales(src, name):
-            raw = keep.tile([P, H], U8, align_bytes=64, name=name)
-            nc.gpsimd.memset(raw[:].bitcast(I32), 0)
-            for q in range(4):
-                nc.sync.dma_start(
-                    out=raw[32 * q : 32 * q + 4, :].bitcast(I32), in_=src[0, 4 * q : 4 * q + 4, :].bitcast(I32)
-                )
-            return raw
-
-        wm_raw = keep.tile([P, 2 * H], U8, align_bytes=64)
-        nc.sync.dma_start(out=wm_raw[:].bitcast(I32), in_=wm_words[0].bitcast(I32))
-        wm_sc_raw = load_scales(wm_scales, "wm_sc_raw")
-        wd_raw = keep.tile([P, H], I32, align_bytes=64)
-        nc.sync.dma_start(out=wd_raw[:], in_=wd_words[0].rearrange("p n t -> p (n t)").bitcast(I32))
-        wd_sc_raw = load_scales(wd_scales, "wd_sc_raw")
+        wm_raw = keep.tile([P, 2 * H], U8, align_bytes=64, name="wm_raw")
+        wd_raw = keep.tile([P, H], I32, align_bytes=64, name="wd_raw")
+        sc_raw = {role: keep.tile([P, H], U8, align_bytes=64, name="sc_raw_" + role) for role in "md"}
         wo_view = wo.rearrange("(b q t i) n -> b t q i n", b=PASSES, t=PACK, i=8)
-        wo_raw = keep.tile([P, PASSES, PACK, N], F32)
-        for b in range(PASSES):
-            for t in range(PACK):
-                nc.sync.dma_start(out=wo_raw[:, b, t, :], in_=wo_view[b, t])
-        bias = keep.tile([P, N_TILES], F32)
-        with nc.allow_non_contiguous_dma(reason="one bias value a partition"):
-            nc.sync.dma_start(out=bias[:], in_=bo.rearrange("(c p) -> p c", p=P))
+        wo_raw = keep.tile([P, PASSES, PACK, N], F32, name="wo_raw")
+        bias = keep.tile([P, N_TILES], F32, name="bias")
+        if "tt" in LOADS:
+            nc.vector.memset(tab_sc[:].bitcast(I32), 0)
+        for role in "md":
+            nc.gpsimd.memset(sc_raw[role][:].bitcast(I32), 0)
+
+        def load_scale_rows(plane, src):
+            rows = src[0].rearrange("(q r) n -> r q n", r=4)
+            for r in range(4):
+                nc.sync.dma_start(out=plane[r:P:32, :].bitcast(I32), in_=rows[r].bitcast(I32))
+
+        def load(what):
+            if what[0] == "l":
+                nc.sync.dma_start(lists[what[1]][:], {"p": offs, "m": offs2, "d": offs3}[what[1]])
+            elif what == "ts":
+                for q in range(4):
+                    rows = tab_scales[0, 4 * q : 4 * q + 4, :].bitcast(I32)
+                    nc.sync.dma_start(
+                        out=tab_sc[32 * q : 32 * q + 32, :].bitcast(I32),
+                        in_=rows.unsqueeze(0).to_broadcast([8, 4, T // 4]),
+                    )
+            elif what == "tt":
+                load_scale_rows(tab_sc, tab_scales)
+            elif what == "tab":
+                nc.sync.dma_start(out=tab[:], in_=tab_words[0].rearrange("p n t -> p (n t)").bitcast(I32))
+            elif what[:2] == "wp":
+                b = int(what[2])
+                nc.sync.dma_start(out=wp_raw[b][:], in_=wp_view[:, :, 512 * b : 512 * (b + 1)])
+            elif what == "wm":
+                nc.sync.dma_start(out=wm_raw[:].bitcast(I32), in_=wm_words[0].bitcast(I32))
+            elif what == "wd":
+                nc.sync.dma_start(out=wd_raw[:], in_=wd_words[0].rearrange("p n t -> p (n t)").bitcast(I32))
+            elif what[0] == "s":
+                load_scale_rows(sc_raw[what[1]], {"m": wm_scales, "d": wd_scales}[what[1]])
+            elif what[:2] == "wo":
+                b = int(what[2])
+                for t in range(PACK):
+                    nc.sync.dma_start(out=wo_raw[:, b, t, :], in_=wo_view[b, t])
+            else:
+                with nc.allow_non_contiguous_dma(reason="one bias value a partition"):
+                    nc.sync.dma_start(out=bias[:], in_=bo.rearrange("(c p) -> p c", p=P))
+
+        for what in LOADS.split():
+            load(what)
 
         picked = {}
         picked_sc = {}
 
         def gather_scales(role, half):
+            if half == 2:
+                dst = keep.tile([P, S], U8, align_bytes=64, name="picked_sc_" + role)
+                nc.vector.tensor_copy(dst[:], tab_sc[:].indirect(lists[role][:]))
+                picked_sc[role, 0], picked_sc[role, 1] = dst[:, 0:HALF], dst[:, HALF:S]
+                return
             dst = keep.tile([P, HALF], U8, align_bytes=64, name="picked_sc_%s%d" % (role, half))
             cols = slice(half * HALF // 16, (half + 1) * HALF // 16)
             nc.vector.tensor_copy(dst[:], tab_sc[:].indirect(lists[role][:, cols]))
             picked_sc[role, half] = dst
 
         def gather_words(role, half):
+            if half == 2:
+                dst = keep.tile([P, S], U32, align_bytes=64, name="picked_" + role)
+                nc.vector.tensor_copy(dst[:], tab[:].bitcast(U32).indirect(lists[role][:]))
+                picked[role, 0], picked[role, 1] = dst[:, 0:HALF], dst[:, HALF:S]
+                return
             dst = keep.tile([P, HALF], U32, align_bytes=64, name="picked_%s%d" % (role, half))
             cols = slice(half * HALF // 16, (half + 1) * HALF // 16)
             nc.vector.tensor_copy(dst[:], tab[:].bitcast(U32).indirect(lists[role][:, cols]))
@@ -98,10 +130,12 @@ def tile_list_payment_fraud_decoder_kernel(
                 in_=src.rearrange("p (b q t i) -> p b t q i", b=PASSES, t=PACK, q=16),
             )
 
-        wm_codes = keep.tile([P, 2 * H], U8, align_bytes=64)
-        wd_codes = keep.tile([P, H], I32, align_bytes=64)
-        wm_sc = keep.tile([P, H], U8, align_bytes=64)
-        wd_sc = keep.tile([P, H], U8, align_bytes=64)
+        wm_codes = keep.tile([P, 2 * H], U8, align_bytes=64, name="wm_codes")
+        wm_sc = keep.tile([P, H], U8, align_bytes=64, name="wm_sc")
+        wd_codes = keep.tile([P, H], I32, align_bytes=64, name="wd_codes")
+        wd_sc = keep.tile([P, H], U8, align_bytes=64, name="wd_sc")
+        wo_codes = keep.tile([P, PASSES * N], U32, align_bytes=64, name="wo_codes")
+        wo_sc = keep.tile([P, PASSES * N], U8, align_bytes=64, name="wo_sc")
         wp_bf = [keep.tile([P, PACK, P, PACK], BF16, align_bytes=64, name="wp_bf%d" % b) for b in range(PASSES)]
         wp_codes = [keep.tile([P, 512], U32, align_bytes=64, name="wp_codes%d" % b) for b in range(PASSES)]
         wp_sc = [keep.tile([P, 512], U8, align_bytes=64, name="wp_sc%d" % b) for b in range(PASSES)]
@@ -109,7 +143,11 @@ def tile_list_payment_fraud_decoder_kernel(
         def round_wp(b):
             src = wp_raw[b][:].rearrange("p j (q t i) -> p t q i j", t=PACK, i=8)
             for t in range(PACK):
-                nc.scalar.copy(out=wp_bf[b][:, t].rearrange("p (q i) j -> p q i j", i=8), in_=src[:, t])
+                dst = wp_bf[b][:, t].rearrange("p (q i) j -> p q i j", i=8)
+                if "p%d" % b not in ROUND_ON_GPSIMD:
+                    nc.scalar.copy(out=dst, in_=src[:, t])
+                else:
+                    nc.gpsimd.tensor_scalar(out=dst, in0=src[:, t], scalar1=1.0, scalar2=0.0, op0=ALU.mult, op1=ALU.add)
 
         def quantize_wp(b):
             nc.vector.quantize_mx(
@@ -118,12 +156,25 @@ def tile_list_payment_fraud_decoder_kernel(
                 in_=wp_bf[b][:].rearrange("p t c j -> p (t c j)"),
             )
 
-        wo_bf = keep.tile([P, PASSES * N, PACK], BF16, align_bytes=64)
-        wo_codes = keep.tile([P, PASSES * N], U32, align_bytes=64)
-        wo_sc = keep.tile([P, PASSES * N], U8, align_bytes=64)
+        wo_bf = keep.tile([P, PASSES * N, PACK], BF16, align_bytes=64, name="wo_bf")
 
         def round_wo(b):
-            nc.scalar.copy(out=wo_bf[:, b * N : (b + 1) * N, :], in_=wo_raw[:, b].rearrange("p t n -> p n t"))
+            if "o%d" % b not in ROUND_ON_GPSIMD:
+                for c0 in range(0, N, P):
+                    nc.scalar.copy(
+                        out=wo_bf[:, b * N + c0 : b * N + c0 + P, :].rearrange("p (c i) t -> p c t i", i=4),
+                        in_=wo_raw[:, b, :, c0 : c0 + P].rearrange("p t (c i) -> p c t i", i=4),
+                    )
+                return
+            for c0 in range(0, N, WO_STEP):
+                nc.gpsimd.tensor_scalar(
+                    out=wo_bf[:, b * N + c0 : b * N + c0 + WO_STEP, :],
+                    in0=wo_raw[:, b, :, c0 : c0 + WO_STEP].rearrange("p t n -> p n t"),
+                    scalar1=1.0,
+                    scalar2=0.0,
+                    op0=ALU.mult,
+                    op1=ALU.add,
+                )
 
         def quantize_wo():
             for c0, c1 in ((0, 512), (512, 768)):
@@ -142,9 +193,9 @@ def tile_list_payment_fraud_decoder_kernel(
                 return wm_codes[:, 2 * cols.start : 2 * cols.stop].bitcast(FP4X4), wm_sc[:, cols]
             return wd_codes[:, cols].bitcast(FP8X4), wd_sc[:, cols]
 
-        def project(role, b, j0):
+        def project(role, b, j0, tag):
             half, c0 = divmod(j0, HALF)
-            bank = psum.tile([P, PACK, CHUNK], F32, name="bank_" + role)
+            bank = psum.tile([P, PACK, CHUNK], F32, name="bank_" + tag)
             for t in range(PACK):
                 codes, scales = stationary(role, b, t)
                 nc.tensor.matmul_mx(
@@ -158,46 +209,68 @@ def tile_list_payment_fraud_decoder_kernel(
                 )
             return bank[:].rearrange("p t n -> p n t")
 
-        units = []
-        j0 = 0
-        for g, width in enumerate(GROUPS):
-            for b in range(PASSES):
-                for c0 in range(0, width, CHUNK):
-                    units.append((g, j0, width, b, c0))
-            j0 += width
+        starts = [sum(GROUPS[:g]) for g in range(len(GROUPS))]
+        units = [
+            (g, starts[g], GROUPS[g], b, c0) for g, b in GROUP_ORDER for c0 in range(0, GROUPS[g], CHUNK)
+        ]
 
         h_bf, h_codes, h_sc, larger, d_bank = {}, {}, {}, {}, {}
 
-        def front(unit):
-            g, j0, width, b, c0 = unit
-            mags = []
+        def device(i):
+            g, j0, width, b, c0 = units[i]
+            bank = project("d", b, j0 + c0, "d")
+            if i in ON_GPSIMD:
+                moved = ring.tile([P, CHUNK, PACK], F32, name="moved", bufs=MOVED_BUFS)
+                nc.scalar.copy(out=moved[:], in_=bank)
+                bank = moved[:]
+            d_bank[i] = bank
+
+        mags = {}
+
+        def front(i):
+            g, j0, width, b, c0 = units[i]
+            span = 1 if i >= SINGLE_FROM else 2
+            k = i % span
             for role in "pm":
-                bank = project(role, b, j0 + c0)
-                mag = ring.tile([P, CHUNK, PACK], F32, name="mag_" + role, bufs=8)
-                nc.scalar.activation(out=mag[:], in_=bank, func=ACT.Abs)
-                mags.append(mag)
-            d_bank[unit] = project("d", b, j0 + c0)
-            larger[unit] = ring.tile([P, CHUNK, PACK], F32, name="larger", bufs=3)
-            nc.vector.tensor_tensor(out=larger[unit][:], in0=mags[0][:], in1=mags[1][:], op=ALU.max)
+                bank = project(role, b, j0 + c0, role)
+                if k == 0:
+                    mags[role] = ring.tile([P, span, CHUNK, PACK], F32, name="mag_" + role, bufs=MAG_BUFS)
+                nc.scalar.activation(out=mags[role][:, k], in_=bank, func=ACT.Abs)
+            if i not in d_bank:
+                device(i)
+            if k == span - 1:
+                both = ring.tile([P, span, CHUNK, PACK], F32, name="larger", bufs=LARGER_BUFS)
+                flat = "p s c j -> p (s c j)"
+                nc.vector.tensor_tensor(
+                    out=both[:].rearrange(flat),
+                    in0=mags["p"][:].rearrange(flat),
+                    in1=mags["m"][:].rearrange(flat),
+                    op=ALU.max,
+                )
+                for kk in range(span):
+                    larger[i - k + kk] = both[:, kk]
 
-        def subtract(unit):
-            g, j0, width, b, c0 = unit
-            if c0 == 0:
-                h_bf[g, b] = keep.tile([P, width, PACK], BF16, align_bytes=64, name="h_bf%d_%d" % (g, b))
-            nc.vector.tensor_tensor(
-                out=h_bf[g, b][:, c0 : c0 + CHUNK, :], in0=larger[unit][:], in1=d_bank[unit], op=ALU.subtract
-            )
+        def subtract(i):
+            g, j0, width, b, c0 = units[i]
+            if g not in h_bf:
+                h_bf[g] = keep.tile([P, PASSES, width, PACK], BF16, align_bytes=64, name="h_bf%d" % g)
+                h_codes[g] = keep.tile([P, PASSES, width], U32, align_bytes=64, name="h_codes%d" % g)
+                h_sc[g] = keep.tile([P, PASSES, width], U8, align_bytes=64, name="h_sc%d" % g)
+            engine = nc.gpsimd if i in ON_GPSIMD else nc.vector
+            engine.tensor_tensor(out=h_bf[g][:, b, c0 : c0 + CHUNK, :], in0=larger[i], in1=d_bank[i], op=ALU.subtract)
 
-        def quantize_h(unit):
-            g, j0, width, b, c0 = unit
+        def quantize_h(i):
+            g, j0, width, b, c0 = units[i]
             if c0 + CHUNK < width:
                 return
-            h_codes[g, b] = keep.tile([P, width], U32, align_bytes=64, name="h_codes%d_%d" % (g, b))
-            h_sc[g, b] = keep.tile([P, width], U8, align_bytes=64, name="h_sc%d_%d" % (g, b))
+            last = g == len(GROUPS) - 1
+            if b < PASSES - 1 and not last:
+                return
+            which = slice(b, b + 1) if last else slice(0, PASSES)
             nc.vector.quantize_mx(
-                out=h_codes[g, b][:].bitcast(FP8X4),
-                scales=h_sc[g, b][:],
-                in_=h_bf[g, b][:].rearrange("p c j -> p (c j)"),
+                out=h_codes[g][:, which].rearrange("p b c -> p (b c)").bitcast(FP8X4),
+                scales=h_sc[g][:, which].rearrange("p b c -> p (b c)"),
+                in_=h_bf[g][:, which].rearrange("p b c j -> p (b c j)"),
             )
             if b == PASSES - 1:
                 decode(g, j0, width)
@@ -220,8 +293,8 @@ def tile_list_payment_fraud_decoder_kernel(
                     out=acc[n],
                     lhsT=wo_codes[:, cols].bitcast(FP8X4),
                     lhsT_scale=wo_sc[:, cols],
-                    rhs=h_codes[g, b][:].bitcast(FP8X4),
-                    rhs_scale=h_sc[g, b][:],
+                    rhs=h_codes[g][:, b].bitcast(FP8X4),
+                    rhs_scale=h_sc[g][:, b],
                     start=(b == 0),
                     stop=(b == PASSES - 1),
                 )
@@ -234,34 +307,24 @@ def tile_list_payment_fraud_decoder_kernel(
                     nc.scalar.activation(out=result[:, n, :], in_=acc[n], func=ACT.Identity, bias=bias[:, n : n + 1])
             nc.sync.dma_start(out=out_view[:, :, j0 : j0 + width], in_=result[:])
 
-        for role in "pmd":
-            gather_scales(role, 0)
-        round_wp(0)
-        round_wp(1)
-        gather_scales("p", 1)
-        quantize_wp(0)
-        gather_scales("m", 1)
-        gather_scales("d", 1)
-        quantize_wp(1)
-        gather_words("p", 0)
-        reorder(wm_codes[:].bitcast(I32), wm_raw[:].bitcast(I32))
-        reorder(wm_sc[:].bitcast(I32), wm_sc_raw[:].bitcast(I32))
-        gather_words("m", 0)
-        gather_words("d", 0)
-        reorder(wd_codes[:], wd_raw[:])
-        reorder(wd_sc[:].bitcast(I32), wd_sc_raw[:].bitcast(I32))
-
-        extra = {1: "p", 3: "m", 5: "d"}
-        for i in range(len(units) + 2):
-            if i < len(units):
-                front(units[i])
-            if i in extra:
-                gather_words(extra[i], 1)
-            if i in (1, 2):
-                round_wo(i - 1)
-            if i == 4:
+        for step in STEPS.split():
+            if step[:2] == "gs":
+                gather_scales(step[2], int(step[3]))
+            elif step[:2] == "gw":
+                gather_words(step[2], int(step[3]))
+            elif step[:2] == "rp":
+                round_wp(int(step[2]))
+            elif step[:2] == "qp":
+                quantize_wp(int(step[2]))
+            elif step[:2] == "ro":
+                round_wo(int(step[2]))
+            elif step == "qo":
                 quantize_wo()
-            if 0 <= i - 1 < len(units):
-                subtract(units[i - 1])
-            if 0 <= i - 2 < len(units):
-                quantize_h(units[i - 2])
+            elif step == "xm":
+                reorder(wm_codes[:].bitcast(I32), wm_raw[:].bitcast(I32))
+                reorder(wm_sc[:].bitcast(I32), sc_raw["m"][:].bitcast(I32))
+            elif step == "xd":
+                reorder(wd_codes[:], wd_raw[:])
+                reorder(wd_sc[:].bitcast(I32), sc_raw["d"][:].bitcast(I32))
+            else:
+                {"f": front, "s": subtract, "q": quantize_h, "d": device}[step[0]](int(step[1:]))

@@ -18,21 +18,20 @@ ACT = mybir.ActivationFunctionType
 
 P = 128
 PACK = 4
-PASSES = H // (P * PACK)
-HALF = 512
+PASS = P * PACK
+PASSES = H // PASS
+RUN = 8
+QUADRANT = 32
+LIST_ROWS = 16
+HALF = S // 2
 CHUNK = 128
 N_TILES = N // P
-WO_STEP = 96
 GROUPS = (256, 256, 256, 128, 128)
-GROUP_ORDER = ((0,0),(0,1),(1,0),(1,1),(2,0),(2,1),(3,0),(3,1),(4,0),(4,1))
-ON_GPSIMD = ()
-ROUND_ON_GPSIMD = ""
-SINGLE_FROM = 0
-MAG_BUFS = 8
-LARGER_BUFS = 3
-MOVED_BUFS = 2
-LOADS = "lp lm tt ld wp0 wp1 wm sm tab wo0 wd sd wo1 bo"
-STEPS = "gsp2 rp0 rp1 gsm2 qp0 gsd2 xm qp1 gwp0 gwm0 gwp1 gwm1 gwd2 xd f0 f1 ro0 s0 f2 s1 q0 f3 ro1 s2 q1 f4 qo s3 q2 f5 s4 q3 f6 s5 q4 f7 s6 q5 f8 s7 q6 f9 s8 q7 f10 s9 q8 f11 s10 q9 f12 s11 q10 f13 s12 q11 f14 s13 q12 f15 s14 q13 s15 q14 q15"
+MAGNITUDE_BUFS = 6
+LARGER_BUFS = 4
+WO_ROUND_AFTER = {1: 0, 3: 1}
+WO_QUANTIZE_AFTER = 4
+WO_QUANTIZE_COLUMNS = ((0, 512), (512, 768))
 
 
 def tile_list_payment_fraud_decoder_kernel(
@@ -44,90 +43,68 @@ def tile_list_payment_fraud_decoder_kernel(
         ring = ctx.enter_context(tc.tile_pool(name="ring", bufs=1))
         psum = ctx.enter_context(tc.psum_pool(name="psum", bufs=2))
 
-        lists = {role: keep.tile([P, S // 16], U16, name="list_" + role) for role in "pmd"}
+        lists = {role: keep.tile([P, S // LIST_ROWS], U16, name="list_" + role) for role in "pmd"}
         tab_sc = keep.tile([P, T], U8, align_bytes=64, name="tab_sc")
         tab = keep.tile([P, T], I32, align_bytes=64, name="tab")
-        wp_view = wp.rearrange("(p j) c -> p j c", j=PACK)
-        wp_raw = [keep.tile([P, PACK, 512], F32, name="wp_raw%d" % b) for b in range(PASSES)]
+        wp_raw = [keep.tile([P, PACK, PASS], F32, name="wp_raw%d" % b) for b in range(PASSES)]
         wm_raw = keep.tile([P, 2 * H], U8, align_bytes=64, name="wm_raw")
         wd_raw = keep.tile([P, H], I32, align_bytes=64, name="wd_raw")
         sc_raw = {role: keep.tile([P, H], U8, align_bytes=64, name="sc_raw_" + role) for role in "md"}
-        wo_view = wo.rearrange("(b q t i) n -> b t q i n", b=PASSES, t=PACK, i=8)
         wo_raw = keep.tile([P, PASSES, PACK, N], F32, name="wo_raw")
         bias = keep.tile([P, N_TILES], F32, name="bias")
-        if "tt" in LOADS:
-            nc.vector.memset(tab_sc[:].bitcast(I32), 0)
+
+        nc.vector.memset(tab_sc[:].bitcast(I32), 0)
         for role in "md":
             nc.gpsimd.memset(sc_raw[role][:].bitcast(I32), 0)
 
-        def load_scale_rows(plane, src):
+        def load_scale_rows(dst, src):
             rows = src[0].rearrange("(q r) n -> r q n", r=4)
             for r in range(4):
-                nc.sync.dma_start(out=plane[r:P:32, :].bitcast(I32), in_=rows[r].bitcast(I32))
+                nc.sync.dma_start(out=dst[r:P:QUADRANT, :].bitcast(I32), in_=rows[r].bitcast(I32))
 
-        def load(what):
-            if what[0] == "l":
-                nc.sync.dma_start(lists[what[1]][:], {"p": offs, "m": offs2, "d": offs3}[what[1]])
-            elif what == "ts":
-                for q in range(4):
-                    rows = tab_scales[0, 4 * q : 4 * q + 4, :].bitcast(I32)
-                    nc.sync.dma_start(
-                        out=tab_sc[32 * q : 32 * q + 32, :].bitcast(I32),
-                        in_=rows.unsqueeze(0).to_broadcast([8, 4, T // 4]),
-                    )
-            elif what == "tt":
-                load_scale_rows(tab_sc, tab_scales)
-            elif what == "tab":
-                nc.sync.dma_start(out=tab[:], in_=tab_words[0].rearrange("p n t -> p (n t)").bitcast(I32))
-            elif what[:2] == "wp":
-                b = int(what[2])
-                nc.sync.dma_start(out=wp_raw[b][:], in_=wp_view[:, :, 512 * b : 512 * (b + 1)])
-            elif what == "wm":
-                nc.sync.dma_start(out=wm_raw[:].bitcast(I32), in_=wm_words[0].bitcast(I32))
-            elif what == "wd":
-                nc.sync.dma_start(out=wd_raw[:], in_=wd_words[0].rearrange("p n t -> p (n t)").bitcast(I32))
-            elif what[0] == "s":
-                load_scale_rows(sc_raw[what[1]], {"m": wm_scales, "d": wd_scales}[what[1]])
-            elif what[:2] == "wo":
-                b = int(what[2])
-                for t in range(PACK):
-                    nc.sync.dma_start(out=wo_raw[:, b, t, :], in_=wo_view[b, t])
-            else:
-                with nc.allow_non_contiguous_dma(reason="one bias value a partition"):
-                    nc.sync.dma_start(out=bias[:], in_=bo.rearrange("(c p) -> p c", p=P))
+        def load_wp(b):
+            rows = wp.rearrange("(p j) c -> p j c", j=PACK)
+            nc.sync.dma_start(out=wp_raw[b][:], in_=rows[:, :, PASS * b : PASS * (b + 1)])
 
-        for what in LOADS.split():
-            load(what)
+        def load_wo(b):
+            rows = wo.rearrange("(b q t i) n -> b t q i n", b=PASSES, t=PACK, i=RUN)
+            for t in range(PACK):
+                nc.sync.dma_start(out=wo_raw[:, b, t, :], in_=rows[b, t])
 
-        picked = {}
-        picked_sc = {}
+        nc.sync.dma_start(lists["p"][:], offs)
+        nc.sync.dma_start(lists["m"][:], offs2)
+        nc.sync.dma_start(out=wm_raw[:].bitcast(I32), in_=wm_words[0].bitcast(I32))
+        load_scale_rows(tab_sc, tab_scales)
+        load_wp(0)
+        nc.sync.dma_start(lists["d"][:], offs3)
+        load_scale_rows(sc_raw["m"], wm_scales)
+        load_wp(1)
+        nc.sync.dma_start(out=tab[:], in_=tab_words[0].rearrange("p n t -> p (n t)").bitcast(I32))
+        load_wo(0)
+        nc.sync.dma_start(out=wd_raw[:], in_=wd_words[0].rearrange("p n t -> p (n t)").bitcast(I32))
+        with nc.allow_non_contiguous_dma(reason="one bias value a partition"):
+            nc.sync.dma_start(out=bias[:], in_=bo.rearrange("(c p) -> p c", p=P))
+        load_scale_rows(sc_raw["d"], wd_scales)
+        load_wo(1)
 
-        def gather_scales(role, half):
-            if half == 2:
-                dst = keep.tile([P, S], U8, align_bytes=64, name="picked_sc_" + role)
-                nc.vector.tensor_copy(dst[:], tab_sc[:].indirect(lists[role][:]))
-                picked_sc[role, 0], picked_sc[role, 1] = dst[:, 0:HALF], dst[:, HALF:S]
-                return
-            dst = keep.tile([P, HALF], U8, align_bytes=64, name="picked_sc_%s%d" % (role, half))
-            cols = slice(half * HALF // 16, (half + 1) * HALF // 16)
-            nc.vector.tensor_copy(dst[:], tab_sc[:].indirect(lists[role][:, cols]))
-            picked_sc[role, half] = dst
+        picked, picked_sc = {}, {}
 
-        def gather_words(role, half):
-            if half == 2:
-                dst = keep.tile([P, S], U32, align_bytes=64, name="picked_" + role)
-                nc.vector.tensor_copy(dst[:], tab[:].bitcast(U32).indirect(lists[role][:]))
-                picked[role, 0], picked[role, 1] = dst[:, 0:HALF], dst[:, HALF:S]
-                return
-            dst = keep.tile([P, HALF], U32, align_bytes=64, name="picked_%s%d" % (role, half))
-            cols = slice(half * HALF // 16, (half + 1) * HALF // 16)
-            nc.vector.tensor_copy(dst[:], tab[:].bitcast(U32).indirect(lists[role][:, cols]))
-            picked[role, half] = dst
+        def gather_scales(role):
+            picked_sc[role] = keep.tile([P, S], U8, align_bytes=64, name="picked_sc_" + role)
+            nc.vector.tensor_copy(picked_sc[role][:], tab_sc[:].indirect(lists[role][:]))
+
+        def gather_words(role, halves):
+            first, count = halves[0] * HALF, len(halves) * HALF
+            dst = keep.tile([P, count], U32, align_bytes=64, name="picked_%s%d" % (role, halves[0]))
+            offsets = lists[role][:, first // LIST_ROWS : (first + count) // LIST_ROWS]
+            nc.vector.tensor_copy(dst[:], tab[:].bitcast(U32).indirect(offsets))
+            for n, half in enumerate(halves):
+                picked[role, half] = dst[:, n * HALF : (n + 1) * HALF]
 
         def reorder(dst, src):
             nc.vector.tensor_copy(
-                out=dst.rearrange("p (b t q i) -> p b t q i", b=PASSES, t=PACK, q=16),
-                in_=src.rearrange("p (b q t i) -> p b t q i", b=PASSES, t=PACK, q=16),
+                out=dst.rearrange("p (b t q i) -> p b t q i", b=PASSES, t=PACK, q=P // RUN),
+                in_=src.rearrange("p (b q t i) -> p b t q i", b=PASSES, t=PACK, q=P // RUN),
             )
 
         wm_codes = keep.tile([P, 2 * H], U8, align_bytes=64, name="wm_codes")
@@ -137,17 +114,14 @@ def tile_list_payment_fraud_decoder_kernel(
         wo_codes = keep.tile([P, PASSES * N], U32, align_bytes=64, name="wo_codes")
         wo_sc = keep.tile([P, PASSES * N], U8, align_bytes=64, name="wo_sc")
         wp_bf = [keep.tile([P, PACK, P, PACK], BF16, align_bytes=64, name="wp_bf%d" % b) for b in range(PASSES)]
-        wp_codes = [keep.tile([P, 512], U32, align_bytes=64, name="wp_codes%d" % b) for b in range(PASSES)]
-        wp_sc = [keep.tile([P, 512], U8, align_bytes=64, name="wp_sc%d" % b) for b in range(PASSES)]
+        wp_codes = [keep.tile([P, PASS], U32, align_bytes=64, name="wp_codes%d" % b) for b in range(PASSES)]
+        wp_sc = [keep.tile([P, PASS], U8, align_bytes=64, name="wp_sc%d" % b) for b in range(PASSES)]
+        wo_bf = keep.tile([P, PASSES * N, PACK], BF16, align_bytes=64, name="wo_bf")
 
         def round_wp(b):
-            src = wp_raw[b][:].rearrange("p j (q t i) -> p t q i j", t=PACK, i=8)
+            src = wp_raw[b][:].rearrange("p j (q t i) -> p t q i j", t=PACK, i=RUN)
             for t in range(PACK):
-                dst = wp_bf[b][:, t].rearrange("p (q i) j -> p q i j", i=8)
-                if "p%d" % b not in ROUND_ON_GPSIMD:
-                    nc.scalar.copy(out=dst, in_=src[:, t])
-                else:
-                    nc.gpsimd.tensor_scalar(out=dst, in0=src[:, t], scalar1=1.0, scalar2=0.0, op0=ALU.mult, op1=ALU.add)
+                nc.scalar.copy(out=wp_bf[b][:, t].rearrange("p (q i) j -> p q i j", i=RUN), in_=src[:, t])
 
         def quantize_wp(b):
             nc.vector.quantize_mx(
@@ -156,28 +130,15 @@ def tile_list_payment_fraud_decoder_kernel(
                 in_=wp_bf[b][:].rearrange("p t c j -> p (t c j)"),
             )
 
-        wo_bf = keep.tile([P, PASSES * N, PACK], BF16, align_bytes=64, name="wo_bf")
-
         def round_wo(b):
-            if "o%d" % b not in ROUND_ON_GPSIMD:
-                for c0 in range(0, N, P):
-                    nc.scalar.copy(
-                        out=wo_bf[:, b * N + c0 : b * N + c0 + P, :].rearrange("p (c i) t -> p c t i", i=4),
-                        in_=wo_raw[:, b, :, c0 : c0 + P].rearrange("p t (c i) -> p c t i", i=4),
-                    )
-                return
-            for c0 in range(0, N, WO_STEP):
-                nc.gpsimd.tensor_scalar(
-                    out=wo_bf[:, b * N + c0 : b * N + c0 + WO_STEP, :],
-                    in0=wo_raw[:, b, :, c0 : c0 + WO_STEP].rearrange("p t n -> p n t"),
-                    scalar1=1.0,
-                    scalar2=0.0,
-                    op0=ALU.mult,
-                    op1=ALU.add,
+            for c0 in range(0, N, P):
+                nc.scalar.copy(
+                    out=wo_bf[:, b * N + c0 : b * N + c0 + P, :].rearrange("p (c i) t -> p c t i", i=4),
+                    in_=wo_raw[:, b, :, c0 : c0 + P].rearrange("p t (c i) -> p c t i", i=4),
                 )
 
         def quantize_wo():
-            for c0, c1 in ((0, 512), (512, 768)):
+            for c0, c1 in WO_QUANTIZE_COLUMNS:
                 nc.vector.quantize_mx(
                     out=wo_codes[:, c0:c1].bitcast(FP8X4),
                     scales=wo_sc[:, c0:c1],
@@ -193,9 +154,9 @@ def tile_list_payment_fraud_decoder_kernel(
                 return wm_codes[:, 2 * cols.start : 2 * cols.stop].bitcast(FP4X4), wm_sc[:, cols]
             return wd_codes[:, cols].bitcast(FP8X4), wd_sc[:, cols]
 
-        def project(role, b, j0, tag):
-            half, c0 = divmod(j0, HALF)
-            bank = psum.tile([P, PACK, CHUNK], F32, name="bank_" + tag)
+        def project(role, b, j):
+            half, c0 = divmod(j, HALF)
+            bank = psum.tile([P, PACK, CHUNK], F32, name="bank_" + role)
             for t in range(PACK):
                 codes, scales = stationary(role, b, t)
                 nc.tensor.matmul_mx(
@@ -203,94 +164,65 @@ def tile_list_payment_fraud_decoder_kernel(
                     lhsT=codes,
                     lhsT_scale=scales,
                     rhs=picked[role, half][:, c0 : c0 + CHUNK].bitcast(FP8X4),
-                    rhs_scale=picked_sc[role, half][:, c0 : c0 + CHUNK],
+                    rhs_scale=picked_sc[role][:, j : j + CHUNK],
                     start=True,
                     stop=True,
                 )
             return bank[:].rearrange("p t n -> p n t")
 
         starts = [sum(GROUPS[:g]) for g in range(len(GROUPS))]
-        units = [
-            (g, starts[g], GROUPS[g], b, c0) for g, b in GROUP_ORDER for c0 in range(0, GROUPS[g], CHUNK)
-        ]
+        last_group = len(GROUPS) - 1
+        units = [(g, b, c0) for g in range(len(GROUPS)) for b in range(PASSES) for c0 in range(0, GROUPS[g], CHUNK)]
+        h_bf, h_codes, h_sc, larger, device = {}, {}, {}, {}, {}
 
-        h_bf, h_codes, h_sc, larger, d_bank = {}, {}, {}, {}, {}
-
-        def device(i):
-            g, j0, width, b, c0 = units[i]
-            bank = project("d", b, j0 + c0, "d")
-            if i in ON_GPSIMD:
-                moved = ring.tile([P, CHUNK, PACK], F32, name="moved", bufs=MOVED_BUFS)
-                nc.scalar.copy(out=moved[:], in_=bank)
-                bank = moved[:]
-            d_bank[i] = bank
-
-        mags = {}
-
-        def front(i):
-            g, j0, width, b, c0 = units[i]
-            span = 1 if i >= SINGLE_FROM else 2
-            k = i % span
+        def take_maximum(u):
+            g, b, c0 = units[u]
+            magnitude = {}
             for role in "pm":
-                bank = project(role, b, j0 + c0, role)
-                if k == 0:
-                    mags[role] = ring.tile([P, span, CHUNK, PACK], F32, name="mag_" + role, bufs=MAG_BUFS)
-                nc.scalar.activation(out=mags[role][:, k], in_=bank, func=ACT.Abs)
-            if i not in d_bank:
-                device(i)
-            if k == span - 1:
-                both = ring.tile([P, span, CHUNK, PACK], F32, name="larger", bufs=LARGER_BUFS)
-                flat = "p s c j -> p (s c j)"
-                nc.vector.tensor_tensor(
-                    out=both[:].rearrange(flat),
-                    in0=mags["p"][:].rearrange(flat),
-                    in1=mags["m"][:].rearrange(flat),
-                    op=ALU.max,
-                )
-                for kk in range(span):
-                    larger[i - k + kk] = both[:, kk]
+                bank = project(role, b, starts[g] + c0)
+                magnitude[role] = ring.tile([P, CHUNK, PACK], F32, name="magnitude_" + role, bufs=MAGNITUDE_BUFS)
+                nc.scalar.activation(out=magnitude[role][:], in_=bank, func=ACT.Abs)
+            device[u] = project("d", b, starts[g] + c0)
+            larger[u] = ring.tile([P, CHUNK, PACK], F32, name="larger", bufs=LARGER_BUFS)
+            nc.vector.tensor_tensor(out=larger[u][:], in0=magnitude["p"][:], in1=magnitude["m"][:], op=ALU.max)
 
-        def subtract(i):
-            g, j0, width, b, c0 = units[i]
+        def subtract(u):
+            g, b, c0 = units[u]
             if g not in h_bf:
-                h_bf[g] = keep.tile([P, PASSES, width, PACK], BF16, align_bytes=64, name="h_bf%d" % g)
-                h_codes[g] = keep.tile([P, PASSES, width], U32, align_bytes=64, name="h_codes%d" % g)
-                h_sc[g] = keep.tile([P, PASSES, width], U8, align_bytes=64, name="h_sc%d" % g)
-            engine = nc.gpsimd if i in ON_GPSIMD else nc.vector
-            engine.tensor_tensor(out=h_bf[g][:, b, c0 : c0 + CHUNK, :], in0=larger[i], in1=d_bank[i], op=ALU.subtract)
-
-        def quantize_h(i):
-            g, j0, width, b, c0 = units[i]
-            if c0 + CHUNK < width:
-                return
-            last = g == len(GROUPS) - 1
-            if b < PASSES - 1 and not last:
-                return
-            which = slice(b, b + 1) if last else slice(0, PASSES)
-            nc.vector.quantize_mx(
-                out=h_codes[g][:, which].rearrange("p b c -> p (b c)").bitcast(FP8X4),
-                scales=h_sc[g][:, which].rearrange("p b c -> p (b c)"),
-                in_=h_bf[g][:, which].rearrange("p b c j -> p (b c j)"),
+                h_bf[g] = keep.tile([P, PASSES, GROUPS[g], PACK], BF16, align_bytes=64, name="h_bf%d" % g)
+                h_codes[g] = keep.tile([P, PASSES, GROUPS[g]], U32, align_bytes=64, name="h_codes%d" % g)
+                h_sc[g] = keep.tile([P, PASSES, GROUPS[g]], U8, align_bytes=64, name="h_sc%d" % g)
+            nc.vector.tensor_tensor(
+                out=h_bf[g][:, b, c0 : c0 + CHUNK, :], in0=larger[u][:], in1=device[u], op=ALU.subtract
             )
-            if b == PASSES - 1:
-                decode(g, j0, width)
 
-        out_view = out.rearrange("(c p) j -> p c j", p=P)
+        def quantize_h(u):
+            g, b, c0 = units[u]
+            closes_group = b == PASSES - 1 and c0 + CHUNK == GROUPS[g]
+            if g == last_group or closes_group:
+                which = slice(b, b + 1) if g == last_group else slice(0, PASSES)
+                nc.vector.quantize_mx(
+                    out=h_codes[g][:, which].rearrange("p b c -> p (b c)").bitcast(FP8X4),
+                    scales=h_sc[g][:, which].rearrange("p b c -> p (b c)"),
+                    in_=h_bf[g][:, which].rearrange("p b c j -> p (b c j)"),
+                )
+            if closes_group:
+                decode(g)
 
-        def decode(g, j0, width):
-            last = g == len(GROUPS) - 1
-            if last:
-                acc = [psum.tile([P, width], F32, name="bank_" + role)[:] for role in "pmd"]
+        def decode(g):
+            width = GROUPS[g]
+            if g == last_group:
+                sums = [psum.tile([P, width], F32, name="bank_" + role)[:] for role in "pmd"]
                 order = [(n, b) for b in range(PASSES) for n in range(N_TILES)]
             else:
-                both = psum.tile([P, 4, 256], F32, name="bank_y", bufs=1)
-                acc = [both[:, n, 0:width] for n in range(N_TILES)]
+                banks = psum.tile([P, 4, max(GROUPS)], F32, name="bank_y", bufs=1)
+                sums = [banks[:, n, 0:width] for n in range(N_TILES)]
                 order = [(n, b) for n in range(N_TILES) for b in range(PASSES)]
             result = keep.tile([P, N_TILES, width], F32, name="result%d" % g)
             for n, b in order:
                 cols = slice(b * N + n * P, b * N + (n + 1) * P)
                 nc.tensor.matmul_mx(
-                    out=acc[n],
+                    out=sums[n],
                     lhsT=wo_codes[:, cols].bitcast(FP8X4),
                     lhsT_scale=wo_sc[:, cols],
                     rhs=h_codes[g][:, b].bitcast(FP8X4),
@@ -298,33 +230,43 @@ def tile_list_payment_fraud_decoder_kernel(
                     start=(b == 0),
                     stop=(b == PASSES - 1),
                 )
+            rows = out.rearrange("(c p) j -> p c j", p=P)[:, :, starts[g] : starts[g] + width]
             for n in range(N_TILES):
-                if last and n == 1:
+                if g == last_group and n == 1:
                     nc.vector.tensor_scalar(
-                        out=result[:, n, :], in0=acc[n], scalar1=bias[:, n : n + 1], scalar2=None, op0=ALU.add
+                        out=result[:, n, :], in0=sums[n], scalar1=bias[:, n : n + 1], scalar2=None, op0=ALU.add
                     )
                 else:
-                    nc.scalar.activation(out=result[:, n, :], in_=acc[n], func=ACT.Identity, bias=bias[:, n : n + 1])
-            nc.sync.dma_start(out=out_view[:, :, j0 : j0 + width], in_=result[:])
+                    nc.scalar.activation(out=result[:, n, :], in_=sums[n], func=ACT.Identity, bias=bias[:, n : n + 1])
+                if g == last_group:
+                    nc.sync.dma_start(out=rows[:, n, :], in_=result[:, n, :])
+            if g != last_group:
+                nc.sync.dma_start(out=rows, in_=result[:])
 
-        for step in STEPS.split():
-            if step[:2] == "gs":
-                gather_scales(step[2], int(step[3]))
-            elif step[:2] == "gw":
-                gather_words(step[2], int(step[3]))
-            elif step[:2] == "rp":
-                round_wp(int(step[2]))
-            elif step[:2] == "qp":
-                quantize_wp(int(step[2]))
-            elif step[:2] == "ro":
-                round_wo(int(step[2]))
-            elif step == "qo":
+        gather_scales("p")
+        round_wp(0)
+        round_wp(1)
+        gather_scales("m")
+        quantize_wp(0)
+        gather_scales("d")
+        reorder(wm_codes[:].bitcast(I32), wm_raw[:].bitcast(I32))
+        reorder(wm_sc[:].bitcast(I32), sc_raw["m"][:].bitcast(I32))
+        quantize_wp(1)
+        for half in range(2):
+            gather_words("p", [half])
+            gather_words("m", [half])
+        gather_words("d", [0, 1])
+        reorder(wd_codes[:], wd_raw[:])
+        reorder(wd_sc[:].bitcast(I32), sc_raw["d"][:].bitcast(I32))
+
+        for u in range(len(units) + 2):
+            if u < len(units):
+                take_maximum(u)
+            if u in WO_ROUND_AFTER:
+                round_wo(WO_ROUND_AFTER[u])
+            if u == WO_QUANTIZE_AFTER:
                 quantize_wo()
-            elif step == "xm":
-                reorder(wm_codes[:].bitcast(I32), wm_raw[:].bitcast(I32))
-                reorder(wm_sc[:].bitcast(I32), sc_raw["m"][:].bitcast(I32))
-            elif step == "xd":
-                reorder(wd_codes[:], wd_raw[:])
-                reorder(wd_sc[:].bitcast(I32), sc_raw["d"][:].bitcast(I32))
-            else:
-                {"f": front, "s": subtract, "q": quantize_h, "d": device}[step[0]](int(step[1:]))
+            if 1 <= u <= len(units):
+                subtract(u - 1)
+            if u >= 2:
+                quantize_h(u - 2)

@@ -131,11 +131,10 @@ def tile_list_payment_fraud_decoder_kernel(
             )
 
         def round_wo(b):
-            for c0 in range(0, N, P):
-                nc.scalar.copy(
-                    out=wo_bf[:, b * N + c0 : b * N + c0 + P, :].rearrange("p (c i) t -> p c t i", i=4),
-                    in_=wo_raw[:, b, :, c0 : c0 + P].rearrange("p t (c i) -> p c t i", i=4),
-                )
+            nc.scalar.copy(
+                out=wo_bf[:, b * N : (b + 1) * N, :].rearrange("p (c i) t -> p c t i", i=4),
+                in_=wo_raw[:, b].rearrange("p t (c i) -> p c t i", i=4),
+            )
 
         def quantize_wo():
             for c0, c1 in WO_QUANTIZE_COLUMNS:

@@ -27,8 +27,8 @@ HALF = S // 2
 CHUNK = 128
 N_TILES = N // P
 GROUPS = (256, 256, 256, 128, 128)
-MAGNITUDE_BUFS = 6
-LARGER_BUFS = 4
+MAGNITUDE_BUFS = 8
+LARGER_BUFS = 6
 WO_ROUND_AFTER = {1: 0, 3: 1}
 WO_QUANTIZE_AFTER = 4
 WO_QUANTIZE_COLUMNS = ((0, 512), (512, 768))
@@ -82,10 +82,10 @@ def tile_list_payment_fraud_decoder_kernel(
         nc.sync.dma_start(out=tab[:], in_=tab_words[0].rearrange("p n t -> p (n t)").bitcast(I32))
         load_wo(0)
         nc.sync.dma_start(out=wd_raw[:], in_=wd_words[0].rearrange("p n t -> p (n t)").bitcast(I32))
-        with nc.allow_non_contiguous_dma(reason="one bias value a partition"):
-            nc.sync.dma_start(out=bias[:], in_=bo.rearrange("(c p) -> p c", p=P))
         load_scale_rows(sc_raw["d"], wd_scales)
         load_wo(1)
+        with nc.allow_non_contiguous_dma(reason="one bias value a partition"):
+            nc.sync.dma_start(out=bias[:], in_=bo.rearrange("(c p) -> p c", p=P))
 
         picked, picked_sc = {}, {}
 
@@ -119,9 +119,9 @@ def tile_list_payment_fraud_decoder_kernel(
         wo_bf = keep.tile([P, PASSES * N, PACK], BF16, align_bytes=64, name="wo_bf")
 
         def round_wp(b):
-            src = wp_raw[b][:].rearrange("p j (q t i) -> p t q i j", t=PACK, i=RUN)
+            src = wp_raw[b][:].rearrange("p j (q t c i) -> p t q c j i", t=PACK, c=2, i=4)
             for t in range(PACK):
-                nc.scalar.copy(out=wp_bf[b][:, t].rearrange("p (q i) j -> p q i j", i=RUN), in_=src[:, t])
+                nc.scalar.copy(out=wp_bf[b][:, t].rearrange("p (q c i) j -> p q c j i", c=2, i=4), in_=src[:, t])
 
         def quantize_wp(b):
             nc.vector.quantize_mx(
@@ -131,9 +131,13 @@ def tile_list_payment_fraud_decoder_kernel(
             )
 
         def round_wo(b):
-            nc.scalar.copy(
+            nc.gpsimd.tensor_scalar(
                 out=wo_bf[:, b * N : (b + 1) * N, :].rearrange("p (c i) t -> p c t i", i=4),
-                in_=wo_raw[:, b].rearrange("p t (c i) -> p c t i", i=4),
+                in0=wo_raw[:, b].rearrange("p t (c i) -> p c t i", i=4),
+                scalar1=1.0,
+                scalar2=0.0,
+                op0=ALU.mult,
+                op1=ALU.add,
             )
 
         def quantize_wo():

@@ -27,11 +27,10 @@ HALF = S // 2
 CHUNK = 128
 N_TILES = N // P
 GROUPS = (256, 256, 256, 128, 128)
-MAGNITUDE_BUFS = 8
-LARGER_BUFS = 6
-WO_ROUND_AFTER = {1: 0, 3: 1}
-WO_QUANTIZE_AFTER = 4
-WO_QUANTIZE_COLUMNS = ((0, 512), (512, 768))
+SHARED_GROUPS = (0, 1, 2)
+MAGNITUDE_BUFS = 6
+LARGER_BUFS = 2
+WO_QUANTIZE_COLUMNS = ((0, 256), (256, 768))
 
 
 def tile_list_payment_fraud_decoder_kernel(
@@ -48,9 +47,9 @@ def tile_list_payment_fraud_decoder_kernel(
         tab = keep.tile([P, T], I32, align_bytes=64, name="tab")
         wp_raw = [keep.tile([P, PACK, PASS], F32, name="wp_raw%d" % b) for b in range(PASSES)]
         wm_raw = keep.tile([P, 2 * H], U8, align_bytes=64, name="wm_raw")
-        wd_raw = keep.tile([P, H], I32, align_bytes=64, name="wd_raw")
+        wd_raw = keep.tile([P, H], I32, align_bytes=64, name="wd_raw", tag="late")
         sc_raw = {role: keep.tile([P, H], U8, align_bytes=64, name="sc_raw_" + role) for role in "md"}
-        wo_raw = keep.tile([P, PASSES, PACK, N], F32, name="wo_raw")
+        wo_raw = [keep.tile([P, PACK, N], F32, name="wo_raw%d" % b) for b in range(PASSES)]
         bias = keep.tile([P, N_TILES], F32, name="bias")
 
         nc.vector.memset(tab_sc[:].bitcast(I32), 0)
@@ -69,7 +68,7 @@ def tile_list_payment_fraud_decoder_kernel(
         def load_wo(b):
             rows = wo.rearrange("(b q t i) n -> b t q i n", b=PASSES, t=PACK, i=RUN)
             for t in range(PACK):
-                nc.sync.dma_start(out=wo_raw[:, b, t, :], in_=rows[b, t])
+                nc.sync.dma_start(out=wo_raw[b][:, t, :], in_=rows[b, t])
 
         nc.sync.dma_start(lists["p"][:], offs)
         nc.sync.dma_start(lists["m"][:], offs2)
@@ -79,11 +78,11 @@ def tile_list_payment_fraud_decoder_kernel(
         nc.sync.dma_start(lists["d"][:], offs3)
         load_scale_rows(sc_raw["m"], wm_scales)
         load_wp(1)
+        load_scale_rows(sc_raw["d"], wd_scales)
         nc.sync.dma_start(out=tab[:], in_=tab_words[0].rearrange("p n t -> p (n t)").bitcast(I32))
         load_wo(0)
-        nc.sync.dma_start(out=wd_raw[:], in_=wd_words[0].rearrange("p n t -> p (n t)").bitcast(I32))
-        load_scale_rows(sc_raw["d"], wd_scales)
         load_wo(1)
+        nc.sync.dma_start(out=wd_raw[:], in_=wd_words[0].rearrange("p n t -> p (n t)").bitcast(I32))
         with nc.allow_non_contiguous_dma(reason="one bias value a partition"):
             nc.sync.dma_start(out=bias[:], in_=bo.rearrange("(c p) -> p c", p=P))
 
@@ -93,13 +92,11 @@ def tile_list_payment_fraud_decoder_kernel(
             picked_sc[role] = keep.tile([P, S], U8, align_bytes=64, name="picked_sc_" + role)
             nc.vector.tensor_copy(picked_sc[role][:], tab_sc[:].indirect(lists[role][:]))
 
-        def gather_words(role, halves):
-            first, count = halves[0] * HALF, len(halves) * HALF
-            dst = keep.tile([P, count], U32, align_bytes=64, name="picked_%s%d" % (role, halves[0]))
-            offsets = lists[role][:, first // LIST_ROWS : (first + count) // LIST_ROWS]
+        def gather_words(role, half):
+            dst = keep.tile([P, HALF], U32, align_bytes=64, name="picked_%s%d" % (role, half))
+            offsets = lists[role][:, half * HALF // LIST_ROWS : (half + 1) * HALF // LIST_ROWS]
             nc.vector.tensor_copy(dst[:], tab[:].bitcast(U32).indirect(offsets))
-            for n, half in enumerate(halves):
-                picked[role, half] = dst[:, n * HALF : (n + 1) * HALF]
+            picked[role, half] = dst
 
         def reorder(dst, src):
             nc.vector.tensor_copy(
@@ -108,9 +105,8 @@ def tile_list_payment_fraud_decoder_kernel(
             )
 
         wm_codes = keep.tile([P, 2 * H], U8, align_bytes=64, name="wm_codes")
-        wm_sc = keep.tile([P, H], U8, align_bytes=64, name="wm_sc")
+        w_sc = {role: keep.tile([P, H], U8, align_bytes=64, name="w_sc_" + role) for role in "md"}
         wd_codes = keep.tile([P, H], I32, align_bytes=64, name="wd_codes")
-        wd_sc = keep.tile([P, H], U8, align_bytes=64, name="wd_sc")
         wo_codes = keep.tile([P, PASSES * N], U32, align_bytes=64, name="wo_codes")
         wo_sc = keep.tile([P, PASSES * N], U8, align_bytes=64, name="wo_sc")
         wp_bf = [keep.tile([P, PACK, P, PACK], BF16, align_bytes=64, name="wp_bf%d" % b) for b in range(PASSES)]
@@ -132,8 +128,8 @@ def tile_list_payment_fraud_decoder_kernel(
 
         def round_wo(b):
             nc.gpsimd.tensor_scalar(
-                out=wo_bf[:, b * N : (b + 1) * N, :].rearrange("p (c i) t -> p c t i", i=4),
-                in0=wo_raw[:, b].rearrange("p t (c i) -> p c t i", i=4),
+                out=wo_bf[:, b * N : (b + 1) * N, :],
+                in0=wo_raw[b][:].rearrange("p t c -> p c t"),
                 scalar1=1.0,
                 scalar2=0.0,
                 op0=ALU.mult,
@@ -154,16 +150,19 @@ def tile_list_payment_fraud_decoder_kernel(
                 local = slice(t * P, (t + 1) * P)
                 return wp_codes[b][:, local].bitcast(FP8X4), wp_sc[b][:, local]
             if role == "m":
-                return wm_codes[:, 2 * cols.start : 2 * cols.stop].bitcast(FP4X4), wm_sc[:, cols]
-            return wd_codes[:, cols].bitcast(FP8X4), wd_sc[:, cols]
+                return wm_codes[:, 2 * cols.start : 2 * cols.stop].bitcast(FP4X4), w_sc["m"][:, cols]
+            return wd_codes[:, cols].bitcast(FP8X4), w_sc["d"][:, cols]
 
         def project(role, b, j):
             half, c0 = divmod(j, HALF)
-            bank = psum.tile([P, PACK, CHUNK], F32, name="bank_" + role)
+            if role == "d":
+                bank = psum.tile([P, PACK * CHUNK], F32, name="bank_d", bufs=4)
+            else:
+                bank = psum.tile([P, PACK * CHUNK], F32, name="bank_pm", bufs=4)
             for t in range(PACK):
                 codes, scales = stationary(role, b, t)
                 nc.tensor.matmul_mx(
-                    out=bank[:, t, :],
+                    out=bank[:, t * CHUNK : (t + 1) * CHUNK],
                     lhsT=codes,
                     lhsT_scale=scales,
                     rhs=picked[role, half][:, c0 : c0 + CHUNK].bitcast(FP8X4),
@@ -171,55 +170,60 @@ def tile_list_payment_fraud_decoder_kernel(
                     start=True,
                     stop=True,
                 )
-            return bank[:].rearrange("p t n -> p n t")
+            return bank[:].rearrange("p (t n) -> p n t", t=PACK)
 
         starts = [sum(GROUPS[:g]) for g in range(len(GROUPS))]
         last_group = len(GROUPS) - 1
-        units = [(g, b, c0) for g in range(len(GROUPS)) for b in range(PASSES) for c0 in range(0, GROUPS[g], CHUNK)]
-        h_bf, h_codes, h_sc, larger, device = {}, {}, {}, {}, {}
+        magnitude, larger, h_bf, h_codes, h_sc = {}, {}, {}, {}, {}
 
-        def take_maximum(u):
-            g, b, c0 = units[u]
-            magnitude = {}
+        def take_magnitudes(g, b):
             for role in "pm":
-                bank = project(role, b, starts[g] + c0)
-                magnitude[role] = ring.tile([P, CHUNK, PACK], F32, name="magnitude_" + role, bufs=MAGNITUDE_BUFS)
-                nc.scalar.activation(out=magnitude[role][:], in_=bank, func=ACT.Abs)
-            device[u] = project("d", b, starts[g] + c0)
-            larger[u] = ring.tile([P, CHUNK, PACK], F32, name="larger", bufs=LARGER_BUFS)
-            nc.vector.tensor_tensor(out=larger[u][:], in0=magnitude["p"][:], in1=magnitude["m"][:], op=ALU.max)
+                tile = ring.tile([P, GROUPS[g], PACK], F32, name="magnitude_" + role, bufs=MAGNITUDE_BUFS)
+                magnitude[role, g, b] = tile
+                for c0 in range(0, GROUPS[g], CHUNK):
+                    nc.scalar.activation(
+                        out=tile[:, c0 : c0 + CHUNK, :], in_=project(role, b, starts[g] + c0), func=ACT.Abs
+                    )
 
-        def subtract(u):
-            g, b, c0 = units[u]
-            if g not in h_bf:
-                h_bf[g] = keep.tile([P, PASSES, GROUPS[g], PACK], BF16, align_bytes=64, name="h_bf%d" % g)
-                h_codes[g] = keep.tile([P, PASSES, GROUPS[g]], U32, align_bytes=64, name="h_codes%d" % g)
-                h_sc[g] = keep.tile([P, PASSES, GROUPS[g]], U8, align_bytes=64, name="h_sc%d" % g)
+        def take_maximum(g, b):
+            if g > 0:
+                larger[g, b] = ring.tile([P, GROUPS[g], PACK], F32, name="larger", bufs=LARGER_BUFS)[:]
+            elif b == 0:
+                first = keep.tile([P, PASSES, GROUPS[g], PACK], F32, align_bytes=64, name="larger_first", tag="late")
+                larger.update({(g, c): first[:, c] for c in range(PASSES)})
             nc.vector.tensor_tensor(
-                out=h_bf[g][:, b, c0 : c0 + CHUNK, :], in0=larger[u][:], in1=device[u], op=ALU.subtract
+                out=larger[g, b], in0=magnitude["p", g, b][:], in1=magnitude["m", g, b][:], op=ALU.max
             )
 
-        def quantize_h(u):
-            g, b, c0 = units[u]
-            closes_group = b == PASSES - 1 and c0 + CHUNK == GROUPS[g]
-            if g == last_group or closes_group:
-                which = slice(b, b + 1) if g == last_group else slice(0, PASSES)
-                nc.vector.quantize_mx(
-                    out=h_codes[g][:, which].rearrange("p b c -> p (b c)").bitcast(FP8X4),
-                    scales=h_sc[g][:, which].rearrange("p b c -> p (b c)"),
-                    in_=h_bf[g][:, which].rearrange("p b c j -> p (b c j)"),
-                )
-            if closes_group:
-                decode(g)
+        def copy_device(g, b, c0):
+            device = keep.tile([P, CHUNK, PACK], F32, name="device%d" % g)
+            nc.scalar.copy(out=device[:], in_=project("d", b, starts[g] + c0))
+            return device[:]
+
+        def subtract(engine, g, b, c0, device):
+            engine.tensor_tensor(
+                out=h_bf[g][:, b, c0 : c0 + CHUNK, :],
+                in0=larger[g, b][:, c0 : c0 + CHUNK, :],
+                in1=device,
+                op=ALU.subtract,
+            )
+
+        def quantize_h(g, which):
+            nc.vector.quantize_mx(
+                out=h_codes[g][:, which].rearrange("p b c -> p (b c)").bitcast(FP8X4),
+                scales=h_sc[g][:, which].rearrange("p b c -> p (b c)"),
+                in_=h_bf[g][:, which].rearrange("p b c j -> p (b c j)"),
+            )
 
         def decode(g):
             width = GROUPS[g]
             if g == last_group:
-                sums = [psum.tile([P, width], F32, name="bank_" + role)[:] for role in "pmd"]
+                sums = [psum.tile([P, PACK * CHUNK], F32, name="bank_pm", bufs=4)[:, 0:width] for n in range(N_TILES)]
                 order = [(n, b) for b in range(PASSES) for n in range(N_TILES)]
             else:
-                banks = psum.tile([P, 4, max(GROUPS)], F32, name="bank_y", bufs=1)
-                sums = [banks[:, n, 0:width] for n in range(N_TILES)]
+                shared = PACK * CHUNK // width
+                banks = [psum.tile([P, PACK * CHUNK], F32, name="bank_pm", bufs=4) for n in range(0, N_TILES, shared)]
+                sums = [banks[n // shared][:, n % shared * width : (n % shared + 1) * width] for n in range(N_TILES)]
                 order = [(n, b) for n in range(N_TILES) for b in range(PASSES)]
             result = keep.tile([P, N_TILES, width], F32, name="result%d" % g)
             for n, b in order:
@@ -246,30 +250,46 @@ def tile_list_payment_fraud_decoder_kernel(
             if g != last_group:
                 nc.sync.dma_start(out=rows, in_=result[:])
 
+        reorder(wm_codes[:].bitcast(I32), wm_raw[:].bitcast(I32))
         gather_scales("p")
         round_wp(0)
         round_wp(1)
         gather_scales("m")
         quantize_wp(0)
         gather_scales("d")
-        reorder(wm_codes[:].bitcast(I32), wm_raw[:].bitcast(I32))
-        reorder(wm_sc[:].bitcast(I32), sc_raw["m"][:].bitcast(I32))
+        reorder(w_sc["m"][:].bitcast(I32), sc_raw["m"][:].bitcast(I32))
         quantize_wp(1)
         for half in range(2):
-            gather_words("p", [half])
-            gather_words("m", [half])
-        gather_words("d", [0, 1])
+            gather_words("p", half)
+            gather_words("m", half)
+        for half in range(2):
+            gather_words("d", half)
         reorder(wd_codes[:], wd_raw[:])
-        reorder(wd_sc[:].bitcast(I32), sc_raw["d"][:].bitcast(I32))
+        reorder(w_sc["d"][:].bitcast(I32), sc_raw["d"][:].bitcast(I32))
 
-        for u in range(len(units) + 2):
-            if u < len(units):
-                take_maximum(u)
-            if u in WO_ROUND_AFTER:
-                round_wo(WO_ROUND_AFTER[u])
-            if u == WO_QUANTIZE_AFTER:
+        for b in range(PASSES):
+            round_wo(b)
+        for g in range(len(GROUPS)):
+            h_bf[g] = keep.tile([P, PASSES, GROUPS[g], PACK], BF16, align_bytes=64, name="h_bf%d" % g)
+            h_codes[g] = keep.tile([P, PASSES, GROUPS[g]], U32, align_bytes=64, name="h_codes%d" % g)
+            h_sc[g] = keep.tile([P, PASSES, GROUPS[g]], U8, align_bytes=64, name="h_sc%d" % g)
+            units = [(b, c0) for b in range(PASSES) for c0 in range(0, GROUPS[g], CHUNK)]
+            for b in range(PASSES):
+                take_magnitudes(g, b)
+            if g in SHARED_GROUPS:
+                shared = units.pop()
+                device = copy_device(g, *shared)
+            for b in range(PASSES):
+                take_maximum(g, b)
+            if g > 0:
+                quantize_h(g - 1, slice(0, PASSES))
+            if g in SHARED_GROUPS:
+                subtract(nc.gpsimd, g, *shared, device)
+            for b, c0 in units:
+                subtract(nc.vector, g, b, c0, project("d", b, starts[g] + c0))
+            if g == 0:
                 quantize_wo()
-            if 1 <= u <= len(units):
-                subtract(u - 1)
-            if u >= 2:
-                quantize_h(u - 2)
+        for b in range(PASSES):
+            quantize_h(last_group, slice(b, b + 1))
+        for g in range(len(GROUPS)):
+            decode(g)

@@ -1,6 +1,7 @@
 from contextlib import ExitStack
 
 import concourse.mybir as mybir
+from concourse.masks import make_identity
 
 K, H, N, T, S = 512, 1024, 384, 4096, 1024
 FLOPS = 2 * S * (3 * K * H + H * N)
@@ -27,7 +28,7 @@ HALF = S // 2
 CHUNK = 128
 N_TILES = N // P
 GROUPS = (256, 256, 256, 128, 128)
-SHARED_GROUPS = (0, 1, 2)
+SHARED_GROUPS = (1, 2)
 MAGNITUDE_BUFS = 6
 LARGER_BUFS = 2
 WO_QUANTIZE_COLUMNS = ((0, 256), (256, 768))
@@ -52,9 +53,13 @@ def tile_list_payment_fraud_decoder_kernel(
         wo_raw = [keep.tile([P, PACK, N], F32, name="wo_raw%d" % b) for b in range(PASSES)]
         bias = keep.tile([P, N_TILES], F32, name="bias")
 
+        identity = keep.tile([P, P], F32, name="identity")
+
         nc.vector.memset(tab_sc[:].bitcast(I32), 0)
         for role in "md":
             nc.gpsimd.memset(sc_raw[role][:].bitcast(I32), 0)
+
+        make_identity(nc, identity[:])
 
         def load_scale_rows(dst, src):
             rows = src[0].rearrange("(q r) n -> r q n", r=4)
@@ -78,11 +83,11 @@ def tile_list_payment_fraud_decoder_kernel(
         nc.sync.dma_start(lists["d"][:], offs3)
         load_scale_rows(sc_raw["m"], wm_scales)
         load_wp(1)
-        load_scale_rows(sc_raw["d"], wd_scales)
         nc.sync.dma_start(out=tab[:], in_=tab_words[0].rearrange("p n t -> p (n t)").bitcast(I32))
+        load_scale_rows(sc_raw["d"], wd_scales)
         load_wo(0)
-        load_wo(1)
         nc.sync.dma_start(out=wd_raw[:], in_=wd_words[0].rearrange("p n t -> p (n t)").bitcast(I32))
+        load_wo(1)
         with nc.allow_non_contiguous_dma(reason="one bias value a partition"):
             nc.sync.dma_start(out=bias[:], in_=bo.rearrange("(c p) -> p c", p=P))
 
@@ -92,11 +97,13 @@ def tile_list_payment_fraud_decoder_kernel(
             picked_sc[role] = keep.tile([P, S], U8, align_bytes=64, name="picked_sc_" + role)
             nc.vector.tensor_copy(picked_sc[role][:], tab_sc[:].indirect(lists[role][:]))
 
-        def gather_words(role, half):
-            dst = keep.tile([P, HALF], U32, align_bytes=64, name="picked_%s%d" % (role, half))
-            offsets = lists[role][:, half * HALF // LIST_ROWS : (half + 1) * HALF // LIST_ROWS]
+        def gather_words(role, halves):
+            first, count = halves[0] * HALF, len(halves) * HALF
+            dst = keep.tile([P, count], U32, align_bytes=64, name="picked_%s%d" % (role, halves[0]))
+            offsets = lists[role][:, first // LIST_ROWS : (first + count) // LIST_ROWS]
             nc.vector.tensor_copy(dst[:], tab[:].bitcast(U32).indirect(offsets))
-            picked[role, half] = dst
+            for n, half in enumerate(halves):
+                picked[role, half] = dst[:, n * HALF : (n + 1) * HALF]
 
         def reorder(dst, src):
             nc.vector.tensor_copy(
@@ -126,10 +133,16 @@ def tile_list_payment_fraud_decoder_kernel(
                 in_=wp_bf[b][:].rearrange("p t c j -> p (t c j)"),
             )
 
-        def round_wo(b):
+        def round_wo_scalar(b, c0, c1):
+            nc.scalar.copy(
+                out=wo_bf[:, b * N + c0 : b * N + c1, :].rearrange("p (c i) t -> p c t i", i=4),
+                in_=wo_raw[b][:, :, c0:c1].rearrange("p t (c i) -> p c t i", i=4),
+            )
+
+        def round_wo(b, c0, c1):
             nc.gpsimd.tensor_scalar(
-                out=wo_bf[:, b * N : (b + 1) * N, :],
-                in0=wo_raw[b][:].rearrange("p t c -> p c t"),
+                out=wo_bf[:, b * N + c0 : b * N + c1, :],
+                in0=wo_raw[b][:, :, c0:c1].rearrange("p t c -> p c t"),
                 scalar1=1.0,
                 scalar2=0.0,
                 op0=ALU.mult,
@@ -176,14 +189,40 @@ def tile_list_payment_fraud_decoder_kernel(
         last_group = len(GROUPS) - 1
         magnitude, larger, h_bf, h_codes, h_sc = {}, {}, {}, {}, {}
 
+        def project_turned(role, b, j):
+            half, c0 = divmod(j, HALF)
+            cols = slice(b * PASS, (b + 1) * PASS)
+            if role == "p":
+                codes, scales = wp_codes[b][:].bitcast(FP8X4), wp_sc[b][:]
+            elif role == "m":
+                codes, scales = wm_codes[:, 2 * cols.start : 2 * cols.stop].bitcast(FP4X4), w_sc["m"][:, cols]
+            else:
+                codes, scales = wd_codes[:, cols].bitcast(FP8X4), w_sc["d"][:, cols]
+            if role == "d":
+                bank = psum.tile([P, PACK * CHUNK], F32, name="bank_d", bufs=4)
+            else:
+                bank = psum.tile([P, PACK * CHUNK], F32, name="bank_pm", bufs=4)
+            nc.tensor.matmul_mx(
+                out=bank[:],
+                lhsT=picked[role, half][:, c0 : c0 + CHUNK].bitcast(FP8X4),
+                lhsT_scale=picked_sc[role][:, j : j + CHUNK],
+                rhs=codes,
+                rhs_scale=scales,
+                start=True,
+                stop=True,
+            )
+            return bank[:].rearrange("p (n t) -> p n t", t=PACK)
+
+        def turned(g, b, c0):
+            return g in SHARED_GROUPS and (b, c0) == (0, 0)
+
         def take_magnitudes(g, b):
             for role in "pm":
                 tile = ring.tile([P, GROUPS[g], PACK], F32, name="magnitude_" + role, bufs=MAGNITUDE_BUFS)
                 magnitude[role, g, b] = tile
                 for c0 in range(0, GROUPS[g], CHUNK):
-                    nc.scalar.activation(
-                        out=tile[:, c0 : c0 + CHUNK, :], in_=project(role, b, starts[g] + c0), func=ACT.Abs
-                    )
+                    product = (project_turned if turned(g, b, c0) else project)(role, b, starts[g] + c0)
+                    nc.scalar.activation(out=tile[:, c0 : c0 + CHUNK, :], in_=product, func=ACT.Abs)
 
         def take_maximum(g, b):
             if g > 0:
@@ -197,8 +236,19 @@ def tile_list_payment_fraud_decoder_kernel(
 
         def copy_device(g, b, c0):
             device = keep.tile([P, CHUNK, PACK], F32, name="device%d" % g)
-            nc.scalar.copy(out=device[:], in_=project("d", b, starts[g] + c0))
+            nc.scalar.activation(out=device[:], in_=project_turned("d", b, starts[g] + c0), func=ACT.Copy, scale=-1.0)
             return device[:]
+
+        def subtract_turned(g, b, c0, device):
+            bank = psum.tile([P, PACK * CHUNK], F32, name="bank_d", bufs=4)
+            terms = [term.rearrange("p n t -> p (n t)") for term in (larger[g, b][:, c0 : c0 + CHUNK, :], device)]
+            for t in range(PACK):
+                cols = slice(t * P, (t + 1) * P)
+                for n, term in enumerate(terms):
+                    nc.tensor.matmul(
+                        out=bank[:, cols], lhsT=term[:, cols], rhs=identity[:], start=(n == 0), stop=(n == 1), is_transpose=True
+                    )
+            nc.scalar.copy(out=h_bf[g][:, b, c0 : c0 + CHUNK, :], in_=bank[:].rearrange("p (t n) -> p n t", t=PACK))
 
         def subtract(engine, g, b, c0, device):
             engine.tensor_tensor(
@@ -245,9 +295,9 @@ def tile_list_payment_fraud_decoder_kernel(
                     )
                 else:
                     nc.scalar.activation(out=result[:, n, :], in_=sums[n], func=ACT.Identity, bias=bias[:, n : n + 1])
-                if g == last_group:
+                if g >= 2:
                     nc.sync.dma_start(out=rows[:, n, :], in_=result[:, n, :])
-            if g != last_group:
+            if not g >= 2:
                 nc.sync.dma_start(out=rows, in_=result[:])
 
         reorder(wm_codes[:].bitcast(I32), wm_raw[:].bitcast(I32))
@@ -260,15 +310,14 @@ def tile_list_payment_fraud_decoder_kernel(
         reorder(w_sc["m"][:].bitcast(I32), sc_raw["m"][:].bitcast(I32))
         quantize_wp(1)
         for half in range(2):
-            gather_words("p", half)
-            gather_words("m", half)
-        for half in range(2):
-            gather_words("d", half)
+            gather_words("p", [half])
+            gather_words("m", [half])
+        gather_words("d", [0, 1])
         reorder(wd_codes[:], wd_raw[:])
         reorder(w_sc["d"][:].bitcast(I32), sc_raw["d"][:].bitcast(I32))
 
-        for b in range(PASSES):
-            round_wo(b)
+        round_wo(0, 0, N)
+        round_wo(1, 0, 192)
         for g in range(len(GROUPS)):
             h_bf[g] = keep.tile([P, PASSES, GROUPS[g], PACK], BF16, align_bytes=64, name="h_bf%d" % g)
             h_codes[g] = keep.tile([P, PASSES, GROUPS[g]], U32, align_bytes=64, name="h_codes%d" % g)
@@ -276,18 +325,21 @@ def tile_list_payment_fraud_decoder_kernel(
             units = [(b, c0) for b in range(PASSES) for c0 in range(0, GROUPS[g], CHUNK)]
             for b in range(PASSES):
                 take_magnitudes(g, b)
+            if g == 0:
+                round_wo_scalar(1, 192, N)
             if g in SHARED_GROUPS:
-                shared = units.pop()
+                shared = (0, 0)
+                units.remove(shared)
                 device = copy_device(g, *shared)
             for b in range(PASSES):
                 take_maximum(g, b)
             if g > 0:
                 quantize_h(g - 1, slice(0, PASSES))
             if g in SHARED_GROUPS:
-                subtract(nc.gpsimd, g, *shared, device)
+                subtract_turned(g, *shared, device)
             for b, c0 in units:
                 subtract(nc.vector, g, b, c0, project("d", b, starts[g] + c0))
-            if g == 0:
+            if g == 1:
                 quantize_wo()
         for b in range(PASSES):
             quantize_h(last_group, slice(b, b + 1))

@@ -28,7 +28,8 @@ HALF = S // 2
 CHUNK = 128
 N_TILES = N // P
 GROUPS = (256, 256, 256, 128, 128)
-SHARED_GROUPS = (1, 2)
+SHARED_GROUPS = (2,)
+DECODE_LAG = 3
 MAGNITUDE_BUFS = 6
 LARGER_BUFS = 2
 WO_QUANTIZE_COLUMNS = ((0, 256), (256, 768))
@@ -77,10 +78,10 @@ def tile_list_payment_fraud_decoder_kernel(
 
         nc.sync.dma_start(lists["p"][:], offs)
         nc.sync.dma_start(lists["m"][:], offs2)
+        nc.sync.dma_start(lists["d"][:], offs3)
         nc.sync.dma_start(out=wm_raw[:].bitcast(I32), in_=wm_words[0].bitcast(I32))
         load_scale_rows(tab_sc, tab_scales)
         load_wp(0)
-        nc.sync.dma_start(lists["d"][:], offs3)
         load_scale_rows(sc_raw["m"], wm_scales)
         load_wp(1)
         nc.sync.dma_start(out=tab[:], in_=tab_words[0].rearrange("p n t -> p (n t)").bitcast(I32))
@@ -141,8 +142,8 @@ def tile_list_payment_fraud_decoder_kernel(
 
         def round_wo(b, c0, c1):
             nc.gpsimd.tensor_scalar(
-                out=wo_bf[:, b * N + c0 : b * N + c1, :],
-                in0=wo_raw[b][:, :, c0:c1].rearrange("p t c -> p c t"),
+                out=wo_bf[:, b * N + c0 : b * N + c1, :].rearrange("p (c i) t -> p c t i", i=4),
+                in0=wo_raw[b][:, :, c0:c1].rearrange("p t (c i) -> p c t i", i=4),
                 scalar1=1.0,
                 scalar2=0.0,
                 op0=ALU.mult,
@@ -295,9 +296,9 @@ def tile_list_payment_fraud_decoder_kernel(
                     )
                 else:
                     nc.scalar.activation(out=result[:, n, :], in_=sums[n], func=ACT.Identity, bias=bias[:, n : n + 1])
-                if g >= 2:
+                if g >= 4:
                     nc.sync.dma_start(out=rows[:, n, :], in_=result[:, n, :])
-            if not g >= 2:
+            if not g >= 4:
                 nc.sync.dma_start(out=rows, in_=result[:])
 
         reorder(wm_codes[:].bitcast(I32), wm_raw[:].bitcast(I32))
@@ -317,7 +318,6 @@ def tile_list_payment_fraud_decoder_kernel(
         reorder(w_sc["d"][:].bitcast(I32), sc_raw["d"][:].bitcast(I32))
 
         round_wo(0, 0, N)
-        round_wo(1, 0, 192)
         for g in range(len(GROUPS)):
             h_bf[g] = keep.tile([P, PASSES, GROUPS[g], PACK], BF16, align_bytes=64, name="h_bf%d" % g)
             h_codes[g] = keep.tile([P, PASSES, GROUPS[g]], U32, align_bytes=64, name="h_codes%d" % g)
@@ -326,22 +326,24 @@ def tile_list_payment_fraud_decoder_kernel(
             for b in range(PASSES):
                 take_magnitudes(g, b)
             if g == 0:
-                round_wo_scalar(1, 192, N)
+                round_wo_scalar(1, 0, N)
             if g in SHARED_GROUPS:
                 shared = (0, 0)
                 units.remove(shared)
                 device = copy_device(g, *shared)
-            for b in range(PASSES):
-                take_maximum(g, b)
+            if g >= DECODE_LAG:
+                decode(g - DECODE_LAG)
+            take_maximum(g, 0)
             if g > 0:
                 quantize_h(g - 1, slice(0, PASSES))
+            take_maximum(g, 1)
             if g in SHARED_GROUPS:
                 subtract_turned(g, *shared, device)
             for b, c0 in units:
                 subtract(nc.vector, g, b, c0, project("d", b, starts[g] + c0))
-            if g == 1:
+            if g == 0:
                 quantize_wo()
         for b in range(PASSES):
             quantize_h(last_group, slice(b, b + 1))
-        for g in range(len(GROUPS)):
+        for g in range(len(GROUPS) - DECODE_LAG, len(GROUPS)):
             decode(g)

@@ -28,10 +28,13 @@ HALF = S // 2
 CHUNK = 128
 N_TILES = N // P
 GROUPS = (256, 256, 256, 128, 128)
-SHARED_GROUPS = (2,)
-DECODE_LAG = 3
-MAGNITUDE_BUFS = 6
-LARGER_BUFS = 2
+TURNED = ((1, 0), (2, 0), (3, 0))
+DECODE_LAG = 1
+EARLY_GROUPS = 4
+WO_GROUP = 0
+WO_LAG = 1
+SCALAR_BANKS = 4
+WO_GPSIMD = 256
 WO_QUANTIZE_COLUMNS = ((0, 256), (256, 768))
 
 
@@ -41,7 +44,6 @@ def tile_list_payment_fraud_decoder_kernel(
     nc = tc.nc
     with ExitStack() as ctx:
         keep = ctx.enter_context(tc.tile_pool(name="keep", bufs=1))
-        ring = ctx.enter_context(tc.tile_pool(name="ring", bufs=1))
         psum = ctx.enter_context(tc.psum_pool(name="psum", bufs=2))
 
         lists = {role: keep.tile([P, S // LIST_ROWS], U16, name="list_" + role) for role in "pmd"}
@@ -76,21 +78,21 @@ def tile_list_payment_fraud_decoder_kernel(
             for t in range(PACK):
                 nc.sync.dma_start(out=wo_raw[b][:, t, :], in_=rows[b, t])
 
-        nc.sync.dma_start(lists["p"][:], offs)
         nc.sync.dma_start(lists["m"][:], offs2)
-        nc.sync.dma_start(lists["d"][:], offs3)
+        nc.sync.dma_start(lists["p"][:], offs)
         nc.sync.dma_start(out=wm_raw[:].bitcast(I32), in_=wm_words[0].bitcast(I32))
-        load_scale_rows(tab_sc, tab_scales)
-        load_wp(0)
-        load_scale_rows(sc_raw["m"], wm_scales)
-        load_wp(1)
-        nc.sync.dma_start(out=tab[:], in_=tab_words[0].rearrange("p n t -> p (n t)").bitcast(I32))
-        load_scale_rows(sc_raw["d"], wd_scales)
-        load_wo(0)
-        nc.sync.dma_start(out=wd_raw[:], in_=wd_words[0].rearrange("p n t -> p (n t)").bitcast(I32))
-        load_wo(1)
         with nc.allow_non_contiguous_dma(reason="one bias value a partition"):
             nc.sync.dma_start(out=bias[:], in_=bo.rearrange("(c p) -> p c", p=P))
+        load_scale_rows(tab_sc, tab_scales)
+        nc.sync.dma_start(out=tab[:], in_=tab_words[0].rearrange("p n t -> p (n t)").bitcast(I32))
+        load_scale_rows(sc_raw["m"], wm_scales)
+        nc.sync.dma_start(lists["d"][:], offs3)
+        load_wp(0)
+        load_wp(1)
+        nc.sync.dma_start(out=wd_raw[:], in_=wd_words[0].rearrange("p n t -> p (n t)").bitcast(I32))
+        load_scale_rows(sc_raw["d"], wd_scales)
+        load_wo(0)
+        load_wo(1)
 
         picked, picked_sc = {}, {}
 
@@ -98,13 +100,12 @@ def tile_list_payment_fraud_decoder_kernel(
             picked_sc[role] = keep.tile([P, S], U8, align_bytes=64, name="picked_sc_" + role)
             nc.vector.tensor_copy(picked_sc[role][:], tab_sc[:].indirect(lists[role][:]))
 
-        def gather_words(role, halves):
-            first, count = halves[0] * HALF, len(halves) * HALF
-            dst = keep.tile([P, count], U32, align_bytes=64, name="picked_%s%d" % (role, halves[0]))
-            offsets = lists[role][:, first // LIST_ROWS : (first + count) // LIST_ROWS]
-            nc.vector.tensor_copy(dst[:], tab[:].bitcast(U32).indirect(offsets))
-            for n, half in enumerate(halves):
-                picked[role, half] = dst[:, n * HALF : (n + 1) * HALF]
+        def gather_words(halves, tag):
+            dst = keep.tile([P, len(halves), HALF], U32, align_bytes=64, name="picked_" + tag, tag=tag)
+            for n, (role, half) in enumerate(halves):
+                offsets = lists[role][:, half * HALF // LIST_ROWS : (half + 1) * HALF // LIST_ROWS]
+                nc.vector.tensor_copy(dst[:, n], tab[:].bitcast(U32).indirect(offsets))
+                picked[role, half] = dst[:, n]
 
         def reorder(dst, src):
             nc.vector.tensor_copy(
@@ -120,12 +121,21 @@ def tile_list_payment_fraud_decoder_kernel(
         wp_bf = [keep.tile([P, PACK, P, PACK], BF16, align_bytes=64, name="wp_bf%d" % b) for b in range(PASSES)]
         wp_codes = [keep.tile([P, PASS], U32, align_bytes=64, name="wp_codes%d" % b) for b in range(PASSES)]
         wp_sc = [keep.tile([P, PASS], U8, align_bytes=64, name="wp_sc%d" % b) for b in range(PASSES)]
-        wo_bf = keep.tile([P, PASSES * N, PACK], BF16, align_bytes=64, name="wo_bf")
 
         def round_wp(b):
             src = wp_raw[b][:].rearrange("p j (q t c i) -> p t q c j i", t=PACK, c=2, i=4)
             for t in range(PACK):
                 nc.scalar.copy(out=wp_bf[b][:, t].rearrange("p (q c i) j -> p q c j i", c=2, i=4), in_=src[:, t])
+
+        def round_wp_gpsimd(b):
+            nc.gpsimd.tensor_scalar(
+                out=wp_bf[b][:].rearrange("p t (q i) j -> p q t i j", i=RUN),
+                in0=wp_raw[b][:].rearrange("p j (q t i) -> p q t i j", t=PACK, i=RUN),
+                scalar1=1.0,
+                scalar2=0.0,
+                op0=ALU.mult,
+                op1=ALU.add,
+            )
 
         def quantize_wp(b):
             nc.vector.quantize_mx(
@@ -142,8 +152,8 @@ def tile_list_payment_fraud_decoder_kernel(
 
         def round_wo(b, c0, c1):
             nc.gpsimd.tensor_scalar(
-                out=wo_bf[:, b * N + c0 : b * N + c1, :].rearrange("p (c i) t -> p c t i", i=4),
-                in0=wo_raw[b][:, :, c0:c1].rearrange("p t (c i) -> p c t i", i=4),
+                out=wo_bf[:, b * N + c0 : b * N + c1, :],
+                in0=wo_raw[b][:, :, c0:c1].rearrange("p t c -> p c t"),
                 scalar1=1.0,
                 scalar2=0.0,
                 op0=ALU.mult,
@@ -170,9 +180,9 @@ def tile_list_payment_fraud_decoder_kernel(
         def project(role, b, j):
             half, c0 = divmod(j, HALF)
             if role == "d":
-                bank = psum.tile([P, PACK * CHUNK], F32, name="bank_d", bufs=4)
+                bank = psum.tile([P, PACK * CHUNK], F32, name="bank_d", bufs=8 - SCALAR_BANKS)
             else:
-                bank = psum.tile([P, PACK * CHUNK], F32, name="bank_pm", bufs=4)
+                bank = psum.tile([P, PACK * CHUNK], F32, name="bank_pm", bufs=SCALAR_BANKS)
             for t in range(PACK):
                 codes, scales = stationary(role, b, t)
                 nc.tensor.matmul_mx(
@@ -199,10 +209,7 @@ def tile_list_payment_fraud_decoder_kernel(
                 codes, scales = wm_codes[:, 2 * cols.start : 2 * cols.stop].bitcast(FP4X4), w_sc["m"][:, cols]
             else:
                 codes, scales = wd_codes[:, cols].bitcast(FP8X4), w_sc["d"][:, cols]
-            if role == "d":
-                bank = psum.tile([P, PACK * CHUNK], F32, name="bank_d", bufs=4)
-            else:
-                bank = psum.tile([P, PACK * CHUNK], F32, name="bank_pm", bufs=4)
+            bank = psum.tile([P, PACK * CHUNK], F32, name="bank_pm", bufs=SCALAR_BANKS)
             nc.tensor.matmul_mx(
                 out=bank[:],
                 lhsT=picked[role, half][:, c0 : c0 + CHUNK].bitcast(FP8X4),
@@ -215,33 +222,29 @@ def tile_list_payment_fraud_decoder_kernel(
             return bank[:].rearrange("p (n t) -> p n t", t=PACK)
 
         def turned(g, b, c0):
-            return g in SHARED_GROUPS and (b, c0) == (0, 0)
+            return (g, b) in TURNED and c0 == 0
 
-        def take_magnitudes(g, b):
-            for role in "pm":
-                tile = ring.tile([P, GROUPS[g], PACK], F32, name="magnitude_" + role, bufs=MAGNITUDE_BUFS)
+        def take_magnitudes(roles, g, b):
+            for role in roles:
+                tile = keep.tile([P, GROUPS[g], PACK], F32, name="magnitude_%s%d%d" % (role, g, b))
                 magnitude[role, g, b] = tile
                 for c0 in range(0, GROUPS[g], CHUNK):
                     product = (project_turned if turned(g, b, c0) else project)(role, b, starts[g] + c0)
                     nc.scalar.activation(out=tile[:, c0 : c0 + CHUNK, :], in_=product, func=ACT.Abs)
 
         def take_maximum(g, b):
-            if g > 0:
-                larger[g, b] = ring.tile([P, GROUPS[g], PACK], F32, name="larger", bufs=LARGER_BUFS)[:]
-            elif b == 0:
-                first = keep.tile([P, PASSES, GROUPS[g], PACK], F32, align_bytes=64, name="larger_first", tag="late")
-                larger.update({(g, c): first[:, c] for c in range(PASSES)})
+            larger[g, b] = magnitude["p", g, b][:]
             nc.vector.tensor_tensor(
                 out=larger[g, b], in0=magnitude["p", g, b][:], in1=magnitude["m", g, b][:], op=ALU.max
             )
 
         def copy_device(g, b, c0):
-            device = keep.tile([P, CHUNK, PACK], F32, name="device%d" % g)
+            device = keep.tile([P, CHUNK, PACK], F32, name="device%d%d" % (g, b))
             nc.scalar.activation(out=device[:], in_=project_turned("d", b, starts[g] + c0), func=ACT.Copy, scale=-1.0)
             return device[:]
 
         def subtract_turned(g, b, c0, device):
-            bank = psum.tile([P, PACK * CHUNK], F32, name="bank_d", bufs=4)
+            bank = psum.tile([P, PACK * CHUNK], F32, name="bank_pm", bufs=SCALAR_BANKS)
             terms = [term.rearrange("p n t -> p (n t)") for term in (larger[g, b][:, c0 : c0 + CHUNK, :], device)]
             for t in range(PACK):
                 cols = slice(t * P, (t + 1) * P)
@@ -269,11 +272,11 @@ def tile_list_payment_fraud_decoder_kernel(
         def decode(g):
             width = GROUPS[g]
             if g == last_group:
-                sums = [psum.tile([P, PACK * CHUNK], F32, name="bank_pm", bufs=4)[:, 0:width] for n in range(N_TILES)]
+                sums = [psum.tile([P, PACK * CHUNK], F32, name="bank_pm", bufs=SCALAR_BANKS)[:, 0:width] for n in range(N_TILES)]
                 order = [(n, b) for b in range(PASSES) for n in range(N_TILES)]
             else:
                 shared = PACK * CHUNK // width
-                banks = [psum.tile([P, PACK * CHUNK], F32, name="bank_pm", bufs=4) for n in range(0, N_TILES, shared)]
+                banks = [psum.tile([P, PACK * CHUNK], F32, name="bank_pm", bufs=SCALAR_BANKS) for n in range(0, N_TILES, shared)]
                 sums = [banks[n // shared][:, n % shared * width : (n % shared + 1) * width] for n in range(N_TILES)]
                 order = [(n, b) for n in range(N_TILES) for b in range(PASSES)]
             result = keep.tile([P, N_TILES, width], F32, name="result%d" % g)
@@ -302,48 +305,58 @@ def tile_list_payment_fraud_decoder_kernel(
                 nc.sync.dma_start(out=rows, in_=result[:])
 
         reorder(wm_codes[:].bitcast(I32), wm_raw[:].bitcast(I32))
-        gather_scales("p")
-        round_wp(0)
-        round_wp(1)
         gather_scales("m")
-        quantize_wp(0)
-        gather_scales("d")
+        gather_scales("p")
+        gather_words([("m", 0)], "first")
         reorder(w_sc["m"][:].bitcast(I32), sc_raw["m"][:].bitcast(I32))
-        quantize_wp(1)
-        for half in range(2):
-            gather_words("p", [half])
-            gather_words("m", [half])
-        gather_words("d", [0, 1])
+        gather_words([("m", 1), ("p", 0), ("p", 1)], "sc_raw_m")
+        gather_scales("d")
+        gather_words([("d", 0)], "third")
+        for b in range(PASSES):
+            round_wp_gpsimd(b)
+        for b in range(PASSES):
+            quantize_wp(b)
         reorder(wd_codes[:], wd_raw[:])
         reorder(w_sc["d"][:].bitcast(I32), sc_raw["d"][:].bitcast(I32))
+        gather_words([("d", 1)], "sc_raw_d")
 
-        round_wo(0, 0, N)
+        wo_bf = keep.tile([P, PASSES * N, PACK], BF16, align_bytes=64, name="wo_bf", tag="wp_bf1")
+        round_wo(0, 0, WO_GPSIMD)
+        for g in range(EARLY_GROUPS):
+            for b in range(PASSES):
+                take_magnitudes("m", g, b)
+        device = {}
+
+        def prepare(g):
+            for b in range(PASSES):
+                take_magnitudes("p" if g < EARLY_GROUPS else "pm", g, b)
+            device.update({(g, b): copy_device(g, b, 0) for b in range(PASSES) if turned(g, b, 0)})
+
+        prepare(0)
         for g in range(len(GROUPS)):
             h_bf[g] = keep.tile([P, PASSES, GROUPS[g], PACK], BF16, align_bytes=64, name="h_bf%d" % g)
             h_codes[g] = keep.tile([P, PASSES, GROUPS[g]], U32, align_bytes=64, name="h_codes%d" % g)
             h_sc[g] = keep.tile([P, PASSES, GROUPS[g]], U8, align_bytes=64, name="h_sc%d" % g)
-            units = [(b, c0) for b in range(PASSES) for c0 in range(0, GROUPS[g], CHUNK)]
-            for b in range(PASSES):
-                take_magnitudes(g, b)
-            if g == 0:
-                round_wo_scalar(1, 0, N)
-            if g in SHARED_GROUPS:
-                shared = (0, 0)
-                units.remove(shared)
-                device = copy_device(g, *shared)
-            if g >= DECODE_LAG:
-                decode(g - DECODE_LAG)
+            units = [(b, c0) for b in range(PASSES) for c0 in range(0, GROUPS[g], CHUNK) if not turned(g, b, c0)]
+            if g < last_group:
+                prepare(g + 1)
             take_maximum(g, 0)
             if g > 0:
                 quantize_h(g - 1, slice(0, PASSES))
             take_maximum(g, 1)
-            if g in SHARED_GROUPS:
-                subtract_turned(g, *shared, device)
+            for b in range(PASSES):
+                if turned(g, b, 0):
+                    subtract_turned(g, b, 0, device[g, b])
+            if g == WO_GROUP:
+                round_wo_scalar(0, WO_GPSIMD, N)
+                round_wo_scalar(1, 0, N)
             for b, c0 in units:
                 subtract(nc.vector, g, b, c0, project("d", b, starts[g] + c0))
-            if g == 0:
+            if g == WO_GROUP + WO_LAG:
                 quantize_wo()
+            if g > DECODE_LAG:
+                decode(g - DECODE_LAG - 1)
         for b in range(PASSES):
             quantize_h(last_group, slice(b, b + 1))
-        for g in range(len(GROUPS) - DECODE_LAG, len(GROUPS)):
+        for g in range(len(GROUPS) - DECODE_LAG - 1, len(GROUPS)):
             decode(g)

@@ -28,14 +28,14 @@ HALF = S // 2
 CHUNK = 128
 N_TILES = N // P
 GROUPS = (256, 256, 256, 128, 128)
-TURNED = ((1, 0), (2, 0), (3, 0))
-DECODE_LAG = 1
-EARLY_GROUPS = 4
-WO_GROUP = 0
-WO_LAG = 1
+TURNED = ((1, 0), (2, 0), (2, 1), (3, 0))
+DECODE_AT = (4, 6, 8, 10, 10)
+EARLY_STEPS = 8
 SCALAR_BANKS = 4
-WO_GPSIMD = 256
-WO_QUANTIZE_COLUMNS = ((0, 256), (256, 768))
+VECTOR_BIAS = ((4, 1),)
+AHEAD = 2
+WO_PARTS = 3
+WO_PART = PASSES * N // WO_PARTS
 
 
 def tile_list_payment_fraud_decoder_kernel(
@@ -53,7 +53,7 @@ def tile_list_payment_fraud_decoder_kernel(
         wm_raw = keep.tile([P, 2 * H], U8, align_bytes=64, name="wm_raw")
         wd_raw = keep.tile([P, H], I32, align_bytes=64, name="wd_raw", tag="late")
         sc_raw = {role: keep.tile([P, H], U8, align_bytes=64, name="sc_raw_" + role) for role in "md"}
-        wo_raw = [keep.tile([P, PACK, N], F32, name="wo_raw%d" % b) for b in range(PASSES)]
+        wo_raw = [keep.tile([P, PACK, N], F32, align_bytes=64, name="wo_raw%d" % b) for b in range(PASSES)]
         bias = keep.tile([P, N_TILES], F32, name="bias")
 
         identity = keep.tile([P, P], F32, name="identity")
@@ -116,8 +116,6 @@ def tile_list_payment_fraud_decoder_kernel(
         wm_codes = keep.tile([P, 2 * H], U8, align_bytes=64, name="wm_codes")
         w_sc = {role: keep.tile([P, H], U8, align_bytes=64, name="w_sc_" + role) for role in "md"}
         wd_codes = keep.tile([P, H], I32, align_bytes=64, name="wd_codes")
-        wo_codes = keep.tile([P, PASSES * N], U32, align_bytes=64, name="wo_codes")
-        wo_sc = keep.tile([P, PASSES * N], U8, align_bytes=64, name="wo_sc")
         wp_bf = [keep.tile([P, PACK, P, PACK], BF16, align_bytes=64, name="wp_bf%d" % b) for b in range(PASSES)]
         wp_codes = [keep.tile([P, PASS], U32, align_bytes=64, name="wp_codes%d" % b) for b in range(PASSES)]
         wp_sc = [keep.tile([P, PASS], U8, align_bytes=64, name="wp_sc%d" % b) for b in range(PASSES)]
@@ -144,28 +142,32 @@ def tile_list_payment_fraud_decoder_kernel(
                 in_=wp_bf[b][:].rearrange("p t c j -> p (t c j)"),
             )
 
-        def round_wo_scalar(b, c0, c1):
-            nc.scalar.copy(
-                out=wo_bf[:, b * N + c0 : b * N + c1, :].rearrange("p (c i) t -> p c t i", i=4),
-                in_=wo_raw[b][:, :, c0:c1].rearrange("p t (c i) -> p c t i", i=4),
-            )
+        wo_bf, wo_mx = {}, {}
 
-        def round_wo(b, c0, c1):
-            nc.gpsimd.tensor_scalar(
-                out=wo_bf[:, b * N + c0 : b * N + c1, :],
-                in0=wo_raw[b][:, :, c0:c1].rearrange("p t c -> p c t"),
-                scalar1=1.0,
-                scalar2=0.0,
-                op0=ALU.mult,
-                op1=ALU.add,
-            )
+        def round_wo(part, tag):
+            wo_bf[part] = keep.tile([P, WO_PART, PACK], BF16, align_bytes=64, name="wo_bf%d" % part, tag=tag)
+            first = part * WO_PART
+            for b in range(PASSES):
+                c0, c1 = max(first, b * N), min(first + WO_PART, (b + 1) * N)
+                if c0 < c1:
+                    nc.gpsimd.tensor_scalar(
+                        out=wo_bf[part][:, c0 - first : c1 - first, :],
+                        in0=wo_raw[b][:, :, c0 - b * N : c1 - b * N].rearrange("p t c -> p c t"),
+                        scalar1=1.0,
+                        scalar2=0.0,
+                        op0=ALU.mult,
+                        op1=ALU.add,
+                    )
 
         def quantize_wo():
-            for c0, c1 in WO_QUANTIZE_COLUMNS:
+            wo_mx["codes"] = keep.tile([P, PASSES * N], U32, align_bytes=64, name="wo_codes", tag="wo_raw1")
+            wo_mx["scales"] = keep.tile([P, PASSES * N], U8, align_bytes=64, name="wo_sc")
+            for part in range(WO_PARTS):
+                cols = slice(part * WO_PART, (part + 1) * WO_PART)
                 nc.vector.quantize_mx(
-                    out=wo_codes[:, c0:c1].bitcast(FP8X4),
-                    scales=wo_sc[:, c0:c1],
-                    in_=wo_bf[:, c0:c1, :].rearrange("p c j -> p (c j)"),
+                    out=wo_mx["codes"][:, cols].bitcast(FP8X4),
+                    scales=wo_mx["scales"][:, cols],
+                    in_=wo_bf[part][:].rearrange("p c j -> p (c j)"),
                 )
 
         def stationary(role, b, t):
@@ -226,7 +228,7 @@ def tile_list_payment_fraud_decoder_kernel(
 
         def take_magnitudes(roles, g, b):
             for role in roles:
-                tile = keep.tile([P, GROUPS[g], PACK], F32, name="magnitude_%s%d%d" % (role, g, b))
+                tile = keep.tile([P, GROUPS[g], PACK], F32, align_bytes=64, name="magnitude_%s%d%d" % (role, g, b))
                 magnitude[role, g, b] = tile
                 for c0 in range(0, GROUPS[g], CHUNK):
                     product = (project_turned if turned(g, b, c0) else project)(role, b, starts[g] + c0)
@@ -284,8 +286,8 @@ def tile_list_payment_fraud_decoder_kernel(
                 cols = slice(b * N + n * P, b * N + (n + 1) * P)
                 nc.tensor.matmul_mx(
                     out=sums[n],
-                    lhsT=wo_codes[:, cols].bitcast(FP8X4),
-                    lhsT_scale=wo_sc[:, cols],
+                    lhsT=wo_mx["codes"][:, cols].bitcast(FP8X4),
+                    lhsT_scale=wo_mx["scales"][:, cols],
                     rhs=h_codes[g][:, b].bitcast(FP8X4),
                     rhs_scale=h_sc[g][:, b],
                     start=(b == 0),
@@ -293,7 +295,7 @@ def tile_list_payment_fraud_decoder_kernel(
                 )
             rows = out.rearrange("(c p) j -> p c j", p=P)[:, :, starts[g] : starts[g] + width]
             for n in range(N_TILES):
-                if g == last_group and n == 1:
+                if (g, n) in VECTOR_BIAS:
                     nc.vector.tensor_scalar(
                         out=result[:, n, :], in0=sums[n], scalar1=bias[:, n : n + 1], scalar2=None, op0=ALU.add
                     )
@@ -320,43 +322,47 @@ def tile_list_payment_fraud_decoder_kernel(
         reorder(w_sc["d"][:].bitcast(I32), sc_raw["d"][:].bitcast(I32))
         gather_words([("d", 1)], "sc_raw_d")
 
-        wo_bf = keep.tile([P, PASSES * N, PACK], BF16, align_bytes=64, name="wo_bf", tag="wp_bf1")
-        round_wo(0, 0, WO_GPSIMD)
-        for g in range(EARLY_GROUPS):
-            for b in range(PASSES):
-                take_magnitudes("m", g, b)
+        round_wo(0, "wp_bf1")
+        early = [(g, b) for g in range(len(GROUPS)) for b in range(PASSES)][:EARLY_STEPS]
+        for g, b in early:
+            take_magnitudes("m", g, b)
         device = {}
 
         def prepare(g):
             for b in range(PASSES):
-                take_magnitudes("p" if g < EARLY_GROUPS else "pm", g, b)
+                take_magnitudes("p" if (g, b) in early else "pm", g, b)
             device.update({(g, b): copy_device(g, b, 0) for b in range(PASSES) if turned(g, b, 0)})
 
-        prepare(0)
+        for g in range(AHEAD):
+            prepare(g)
         for g in range(len(GROUPS)):
             h_bf[g] = keep.tile([P, PASSES, GROUPS[g], PACK], BF16, align_bytes=64, name="h_bf%d" % g)
             h_codes[g] = keep.tile([P, PASSES, GROUPS[g]], U32, align_bytes=64, name="h_codes%d" % g)
             h_sc[g] = keep.tile([P, PASSES, GROUPS[g]], U8, align_bytes=64, name="h_sc%d" % g)
             units = [(b, c0) for b in range(PASSES) for c0 in range(0, GROUPS[g], CHUNK) if not turned(g, b, c0)]
-            if g < last_group:
-                prepare(g + 1)
+            if g + AHEAD <= last_group:
+                prepare(g + AHEAD)
             take_maximum(g, 0)
+            if g == WO_PARTS - 1:
+                quantize_wo()
             if g > 0:
                 quantize_h(g - 1, slice(0, PASSES))
             take_maximum(g, 1)
+            for c in range(len(GROUPS)):
+                if DECODE_AT[c] == 2 * g:
+                    decode(c)
             for b in range(PASSES):
                 if turned(g, b, 0):
                     subtract_turned(g, b, 0, device[g, b])
-            if g == WO_GROUP:
-                round_wo_scalar(0, WO_GPSIMD, N)
-                round_wo_scalar(1, 0, N)
+            if g + 1 < WO_PARTS:
+                round_wo(g + 1, "magnitude_m%d1" % g)
             for b, c0 in units:
                 subtract(nc.vector, g, b, c0, project("d", b, starts[g] + c0))
-            if g == WO_GROUP + WO_LAG:
-                quantize_wo()
-            if g > DECODE_LAG:
-                decode(g - DECODE_LAG - 1)
+            for c in range(len(GROUPS)):
+                if DECODE_AT[c] == 2 * g + 1:
+                    decode(c)
         for b in range(PASSES):
             quantize_h(last_group, slice(b, b + 1))
-        for g in range(len(GROUPS) - DECODE_LAG - 1, len(GROUPS)):
-            decode(g)
+        for g in range(len(GROUPS)):
+            if DECODE_AT[g] == 10:
+                decode(g)

@@ -28,12 +28,11 @@ HALF = S // 2
 CHUNK = 128
 N_TILES = N // P
 GROUPS = (256, 256, 256, 128, 128)
-TURNED = ((1, 0), (2, 0), (2, 1), (3, 0))
-DECODE_AT = (4, 6, 8, 10, 10)
-EARLY_STEPS = 8
-SCALAR_BANKS = 4
-VECTOR_BIAS = ((4, 1),)
+TURNED_PASSES = ((), (0,), (0, 1), (0,), ())
+EARLY_GROUPS = 4
 AHEAD = 2
+DECODE_LAG = 2
+RING_BANKS = 4
 WO_PARTS = 3
 WO_PART = PASSES * N // WO_PARTS
 
@@ -44,14 +43,14 @@ def tile_list_payment_fraud_decoder_kernel(
     nc = tc.nc
     with ExitStack() as ctx:
         keep = ctx.enter_context(tc.tile_pool(name="keep", bufs=1))
-        psum = ctx.enter_context(tc.psum_pool(name="psum", bufs=2))
+        psum = ctx.enter_context(tc.psum_pool(name="psum", bufs=RING_BANKS))
 
         lists = {role: keep.tile([P, S // LIST_ROWS], U16, name="list_" + role) for role in "pmd"}
         tab_sc = keep.tile([P, T], U8, align_bytes=64, name="tab_sc")
         tab = keep.tile([P, T], I32, align_bytes=64, name="tab")
         wp_raw = [keep.tile([P, PACK, PASS], F32, name="wp_raw%d" % b) for b in range(PASSES)]
         wm_raw = keep.tile([P, 2 * H], U8, align_bytes=64, name="wm_raw")
-        wd_raw = keep.tile([P, H], I32, align_bytes=64, name="wd_raw", tag="late")
+        wd_raw = keep.tile([P, H], I32, align_bytes=64, name="wd_raw")
         sc_raw = {role: keep.tile([P, H], U8, align_bytes=64, name="sc_raw_" + role) for role in "md"}
         wo_raw = [keep.tile([P, PACK, N], F32, align_bytes=64, name="wo_raw%d" % b) for b in range(PASSES)]
         bias = keep.tile([P, N_TILES], F32, name="bias")
@@ -69,6 +68,9 @@ def tile_list_payment_fraud_decoder_kernel(
             for r in range(4):
                 nc.sync.dma_start(out=dst[r:P:QUADRANT, :].bitcast(I32), in_=rows[r].bitcast(I32))
 
+        def load_table(c0, c1):
+            nc.sync.dma_start(out=tab[:, c0:c1], in_=tab_words[0].rearrange("p n t -> p (n t)").bitcast(I32)[:, c0:c1])
+
         def load_wp(b):
             rows = wp.rearrange("(p j) c -> p j c", j=PACK)
             nc.sync.dma_start(out=wp_raw[b][:], in_=rows[:, :, PASS * b : PASS * (b + 1)])
@@ -84,8 +86,9 @@ def tile_list_payment_fraud_decoder_kernel(
         with nc.allow_non_contiguous_dma(reason="one bias value a partition"):
             nc.sync.dma_start(out=bias[:], in_=bo.rearrange("(c p) -> p c", p=P))
         load_scale_rows(tab_sc, tab_scales)
-        nc.sync.dma_start(out=tab[:], in_=tab_words[0].rearrange("p n t -> p (n t)").bitcast(I32))
+        load_table(0, T // 2)
         load_scale_rows(sc_raw["m"], wm_scales)
+        load_table(T // 2, T)
         nc.sync.dma_start(lists["d"][:], offs3)
         load_wp(0)
         load_wp(1)
@@ -120,19 +123,13 @@ def tile_list_payment_fraud_decoder_kernel(
         wp_codes = [keep.tile([P, PASS], U32, align_bytes=64, name="wp_codes%d" % b) for b in range(PASSES)]
         wp_sc = [keep.tile([P, PASS], U8, align_bytes=64, name="wp_sc%d" % b) for b in range(PASSES)]
 
-        def round_wp(b):
-            src = wp_raw[b][:].rearrange("p j (q t c i) -> p t q c j i", t=PACK, c=2, i=4)
-            for t in range(PACK):
-                nc.scalar.copy(out=wp_bf[b][:, t].rearrange("p (q c i) j -> p q c j i", c=2, i=4), in_=src[:, t])
+        def round_on_gpsimd(dst, src):
+            nc.gpsimd.tensor_scalar(out=dst, in0=src, scalar1=1.0, scalar2=0.0, op0=ALU.mult, op1=ALU.add)
 
-        def round_wp_gpsimd(b):
-            nc.gpsimd.tensor_scalar(
-                out=wp_bf[b][:].rearrange("p t (q i) j -> p q t i j", i=RUN),
-                in0=wp_raw[b][:].rearrange("p j (q t i) -> p q t i j", t=PACK, i=RUN),
-                scalar1=1.0,
-                scalar2=0.0,
-                op0=ALU.mult,
-                op1=ALU.add,
+        def round_wp(b):
+            round_on_gpsimd(
+                wp_bf[b][:].rearrange("p t (q i) j -> p q t i j", i=RUN),
+                wp_raw[b][:].rearrange("p j (q t i) -> p q t i j", t=PACK, i=RUN),
             )
 
         def quantize_wp(b):
@@ -150,13 +147,9 @@ def tile_list_payment_fraud_decoder_kernel(
             for b in range(PASSES):
                 c0, c1 = max(first, b * N), min(first + WO_PART, (b + 1) * N)
                 if c0 < c1:
-                    nc.gpsimd.tensor_scalar(
-                        out=wo_bf[part][:, c0 - first : c1 - first, :],
-                        in0=wo_raw[b][:, :, c0 - b * N : c1 - b * N].rearrange("p t c -> p c t"),
-                        scalar1=1.0,
-                        scalar2=0.0,
-                        op0=ALU.mult,
-                        op1=ALU.add,
+                    round_on_gpsimd(
+                        wo_bf[part][:, c0 - first : c1 - first, :],
+                        wo_raw[b][:, :, c0 - b * N : c1 - b * N].rearrange("p t c -> p c t"),
                     )
 
         def quantize_wo():
@@ -179,12 +172,12 @@ def tile_list_payment_fraud_decoder_kernel(
                 return wm_codes[:, 2 * cols.start : 2 * cols.stop].bitcast(FP4X4), w_sc["m"][:, cols]
             return wd_codes[:, cols].bitcast(FP8X4), w_sc["d"][:, cols]
 
+        def next_bank(ring="bank"):
+            return psum.tile([P, PACK * CHUNK], F32, name=ring)
+
         def project(role, b, j):
             half, c0 = divmod(j, HALF)
-            if role == "d":
-                bank = psum.tile([P, PACK * CHUNK], F32, name="bank_d", bufs=8 - SCALAR_BANKS)
-            else:
-                bank = psum.tile([P, PACK * CHUNK], F32, name="bank_pm", bufs=SCALAR_BANKS)
+            bank = next_bank("bank_d" if role == "d" else "bank")
             for t in range(PACK):
                 codes, scales = stationary(role, b, t)
                 nc.tensor.matmul_mx(
@@ -200,7 +193,7 @@ def tile_list_payment_fraud_decoder_kernel(
 
         starts = [sum(GROUPS[:g]) for g in range(len(GROUPS))]
         last_group = len(GROUPS) - 1
-        magnitude, larger, h_bf, h_codes, h_sc = {}, {}, {}, {}, {}
+        magnitude, larger, minus_d, h_bf, h_codes, h_sc = {}, {}, {}, {}, {}, {}
 
         def project_turned(role, b, j):
             half, c0 = divmod(j, HALF)
@@ -211,7 +204,7 @@ def tile_list_payment_fraud_decoder_kernel(
                 codes, scales = wm_codes[:, 2 * cols.start : 2 * cols.stop].bitcast(FP4X4), w_sc["m"][:, cols]
             else:
                 codes, scales = wd_codes[:, cols].bitcast(FP8X4), w_sc["d"][:, cols]
-            bank = psum.tile([P, PACK * CHUNK], F32, name="bank_pm", bufs=SCALAR_BANKS)
+            bank = next_bank()
             nc.tensor.matmul_mx(
                 out=bank[:],
                 lhsT=picked[role, half][:, c0 : c0 + CHUNK].bitcast(FP8X4),
@@ -224,7 +217,7 @@ def tile_list_payment_fraud_decoder_kernel(
             return bank[:].rearrange("p (n t) -> p n t", t=PACK)
 
         def turned(g, b, c0):
-            return (g, b) in TURNED and c0 == 0
+            return b in TURNED_PASSES[g] and c0 == 0
 
         def take_magnitudes(roles, g, b):
             for role in roles:
@@ -240,27 +233,32 @@ def tile_list_payment_fraud_decoder_kernel(
                 out=larger[g, b], in0=magnitude["p", g, b][:], in1=magnitude["m", g, b][:], op=ALU.max
             )
 
-        def copy_device(g, b, c0):
-            device = keep.tile([P, CHUNK, PACK], F32, name="device%d%d" % (g, b))
-            nc.scalar.activation(out=device[:], in_=project_turned("d", b, starts[g] + c0), func=ACT.Copy, scale=-1.0)
-            return device[:]
+        def negate_device(g, b):
+            tile = keep.tile([P, CHUNK, PACK], F32, name="minus_d%d%d" % (g, b))
+            nc.scalar.activation(out=tile[:], in_=project_turned("d", b, starts[g]), func=ACT.Copy, scale=-1.0)
+            minus_d[g, b] = tile[:]
 
-        def subtract_turned(g, b, c0, device):
-            bank = psum.tile([P, PACK * CHUNK], F32, name="bank_pm", bufs=SCALAR_BANKS)
-            terms = [term.rearrange("p n t -> p (n t)") for term in (larger[g, b][:, c0 : c0 + CHUNK, :], device)]
+        def subtract_turned(g, b):
+            bank = next_bank()
+            terms = [term.rearrange("p n t -> p (n t)") for term in (larger[g, b][:, 0:CHUNK, :], minus_d[g, b])]
             for t in range(PACK):
                 cols = slice(t * P, (t + 1) * P)
                 for n, term in enumerate(terms):
                     nc.tensor.matmul(
-                        out=bank[:, cols], lhsT=term[:, cols], rhs=identity[:], start=(n == 0), stop=(n == 1), is_transpose=True
+                        out=bank[:, cols],
+                        lhsT=term[:, cols],
+                        rhs=identity[:],
+                        start=(n == 0),
+                        stop=(n == 1),
+                        is_transpose=True,
                     )
-            nc.scalar.copy(out=h_bf[g][:, b, c0 : c0 + CHUNK, :], in_=bank[:].rearrange("p (t n) -> p n t", t=PACK))
+            nc.scalar.copy(out=h_bf[g][:, b, 0:CHUNK, :], in_=bank[:].rearrange("p (t n) -> p n t", t=PACK))
 
-        def subtract(engine, g, b, c0, device):
-            engine.tensor_tensor(
+        def subtract(g, b, c0):
+            nc.vector.tensor_tensor(
                 out=h_bf[g][:, b, c0 : c0 + CHUNK, :],
                 in0=larger[g, b][:, c0 : c0 + CHUNK, :],
-                in1=device,
+                in1=project("d", b, starts[g] + c0),
                 op=ALU.subtract,
             )
 
@@ -274,11 +272,11 @@ def tile_list_payment_fraud_decoder_kernel(
         def decode(g):
             width = GROUPS[g]
             if g == last_group:
-                sums = [psum.tile([P, PACK * CHUNK], F32, name="bank_pm", bufs=SCALAR_BANKS)[:, 0:width] for n in range(N_TILES)]
+                sums = [next_bank()[:, 0:width] for n in range(N_TILES)]
                 order = [(n, b) for b in range(PASSES) for n in range(N_TILES)]
             else:
                 shared = PACK * CHUNK // width
-                banks = [psum.tile([P, PACK * CHUNK], F32, name="bank_pm", bufs=SCALAR_BANKS) for n in range(0, N_TILES, shared)]
+                banks = [next_bank() for n in range(0, N_TILES, shared)]
                 sums = [banks[n // shared][:, n % shared * width : (n % shared + 1) * width] for n in range(N_TILES)]
                 order = [(n, b) for n in range(N_TILES) for b in range(PASSES)]
             result = keep.tile([P, N_TILES, width], F32, name="result%d" % g)
@@ -295,51 +293,48 @@ def tile_list_payment_fraud_decoder_kernel(
                 )
             rows = out.rearrange("(c p) j -> p c j", p=P)[:, :, starts[g] : starts[g] + width]
             for n in range(N_TILES):
-                if (g, n) in VECTOR_BIAS:
+                if g == last_group and n == 1:
                     nc.vector.tensor_scalar(
                         out=result[:, n, :], in0=sums[n], scalar1=bias[:, n : n + 1], scalar2=None, op0=ALU.add
                     )
                 else:
                     nc.scalar.activation(out=result[:, n, :], in_=sums[n], func=ACT.Identity, bias=bias[:, n : n + 1])
-                if g >= 4:
+                if g == last_group:
                     nc.sync.dma_start(out=rows[:, n, :], in_=result[:, n, :])
-            if not g >= 4:
+            if g < last_group:
                 nc.sync.dma_start(out=rows, in_=result[:])
 
         reorder(wm_codes[:].bitcast(I32), wm_raw[:].bitcast(I32))
         gather_scales("m")
         gather_scales("p")
-        gather_words([("m", 0)], "first")
         reorder(w_sc["m"][:].bitcast(I32), sc_raw["m"][:].bitcast(I32))
-        gather_words([("m", 1), ("p", 0), ("p", 1)], "sc_raw_m")
+        gather_words([("m", 0), ("m", 1), ("p", 0), ("p", 1)], "mp")
         gather_scales("d")
-        gather_words([("d", 0)], "third")
+        gather_words([("d", 0)], "d0")
         for b in range(PASSES):
-            round_wp_gpsimd(b)
+            round_wp(b)
         for b in range(PASSES):
             quantize_wp(b)
         reorder(wd_codes[:], wd_raw[:])
         reorder(w_sc["d"][:].bitcast(I32), sc_raw["d"][:].bitcast(I32))
         gather_words([("d", 1)], "sc_raw_d")
-
         round_wo(0, "wp_bf1")
-        early = [(g, b) for g in range(len(GROUPS)) for b in range(PASSES)][:EARLY_STEPS]
-        for g, b in early:
-            take_magnitudes("m", g, b)
-        device = {}
 
         def prepare(g):
             for b in range(PASSES):
-                take_magnitudes("p" if (g, b) in early else "pm", g, b)
-            device.update({(g, b): copy_device(g, b, 0) for b in range(PASSES) if turned(g, b, 0)})
+                take_magnitudes("p" if g < EARLY_GROUPS else "pm", g, b)
+            for b in TURNED_PASSES[g]:
+                negate_device(g, b)
 
+        for g in range(EARLY_GROUPS):
+            for b in range(PASSES):
+                take_magnitudes("m", g, b)
         for g in range(AHEAD):
             prepare(g)
         for g in range(len(GROUPS)):
             h_bf[g] = keep.tile([P, PASSES, GROUPS[g], PACK], BF16, align_bytes=64, name="h_bf%d" % g)
             h_codes[g] = keep.tile([P, PASSES, GROUPS[g]], U32, align_bytes=64, name="h_codes%d" % g)
             h_sc[g] = keep.tile([P, PASSES, GROUPS[g]], U8, align_bytes=64, name="h_sc%d" % g)
-            units = [(b, c0) for b in range(PASSES) for c0 in range(0, GROUPS[g], CHUNK) if not turned(g, b, c0)]
             if g + AHEAD <= last_group:
                 prepare(g + AHEAD)
             take_maximum(g, 0)
@@ -348,21 +343,17 @@ def tile_list_payment_fraud_decoder_kernel(
             if g > 0:
                 quantize_h(g - 1, slice(0, PASSES))
             take_maximum(g, 1)
-            for c in range(len(GROUPS)):
-                if DECODE_AT[c] == 2 * g:
-                    decode(c)
-            for b in range(PASSES):
-                if turned(g, b, 0):
-                    subtract_turned(g, b, 0, device[g, b])
+            if g >= DECODE_LAG:
+                decode(g - DECODE_LAG)
+            for b in TURNED_PASSES[g]:
+                subtract_turned(g, b)
             if g + 1 < WO_PARTS:
                 round_wo(g + 1, "magnitude_m%d1" % g)
-            for b, c0 in units:
-                subtract(nc.vector, g, b, c0, project("d", b, starts[g] + c0))
-            for c in range(len(GROUPS)):
-                if DECODE_AT[c] == 2 * g + 1:
-                    decode(c)
+            for b in range(PASSES):
+                for c0 in range(0, GROUPS[g], CHUNK):
+                    if not turned(g, b, c0):
+                        subtract(g, b, c0)
         for b in range(PASSES):
             quantize_h(last_group, slice(b, b + 1))
-        for g in range(len(GROUPS)):
-            if DECODE_AT[g] == 10:
-                decode(g)
+        for g in range(len(GROUPS) - DECODE_LAG, len(GROUPS)):
+            decode(g)

@@ -28,13 +28,16 @@ HALF = S // 2
 CHUNK = 128
 N_TILES = N // P
 GROUPS = (256, 256, 256, 128, 128)
-TURNED_PASSES = ((), (0,), (0, 1), (0,), ())
-EARLY_GROUPS = 4
-AHEAD = 2
-DECODE_LAG = 2
-RING_BANKS = 4
-WO_PARTS = 3
+TURNED = (1, 1, 2, 1, 0)
+EARLY_UNITS = 15
+LEAD = 3
+FEEDS = 6
+BANKS = 8
+VECTOR_BANKS = 4
+WO_TILES = (((0, 0), (0, 1)), ((1, 0), (1, 1)), ((0, 2), (1, 2)))
+WO_PARTS = len(WO_TILES)
 WO_PART = PASSES * N // WO_PARTS
+FIRST = 256
 
 
 def tile_list_payment_fraud_decoder_kernel(
@@ -43,7 +46,7 @@ def tile_list_payment_fraud_decoder_kernel(
     nc = tc.nc
     with ExitStack() as ctx:
         keep = ctx.enter_context(tc.tile_pool(name="keep", bufs=1))
-        psum = ctx.enter_context(tc.psum_pool(name="psum", bufs=RING_BANKS))
+        psum = ctx.enter_context(tc.psum_pool(name="psum", bufs=1))
 
         lists = {role: keep.tile([P, S // LIST_ROWS], U16, name="list_" + role) for role in "pmd"}
         tab_sc = keep.tile([P, T], U8, align_bytes=64, name="tab_sc")
@@ -55,13 +58,9 @@ def tile_list_payment_fraud_decoder_kernel(
         wo_raw = [keep.tile([P, PACK, N], F32, align_bytes=64, name="wo_raw%d" % b) for b in range(PASSES)]
         bias = keep.tile([P, N_TILES], F32, name="bias")
 
-        identity = keep.tile([P, P], F32, name="identity")
-
         nc.vector.memset(tab_sc[:].bitcast(I32), 0)
         for role in "md":
-            nc.gpsimd.memset(sc_raw[role][:].bitcast(I32), 0)
-
-        make_identity(nc, identity[:])
+            nc.vector.memset(sc_raw[role][:].bitcast(I32), 0)
 
         def load_scale_rows(dst, src):
             rows = src[0].rearrange("(q r) n -> r q n", r=4)
@@ -106,12 +105,14 @@ def tile_list_payment_fraud_decoder_kernel(
         def gather_words(halves, tag):
             dst = keep.tile([P, len(halves), HALF], U32, align_bytes=64, name="picked_" + tag, tag=tag)
             for n, (role, half) in enumerate(halves):
-                offsets = lists[role][:, half * HALF // LIST_ROWS : (half + 1) * HALF // LIST_ROWS]
-                nc.vector.tensor_copy(dst[:, n], tab[:].bitcast(U32).indirect(offsets))
+                cuts = (0, FIRST, HALF) if (role, half) == ("m", 0) else (0, HALF)
+                for c0, c1 in zip(cuts, cuts[1:]):
+                    offsets = lists[role][:, (half * HALF + c0) // LIST_ROWS : (half * HALF + c1) // LIST_ROWS]
+                    nc.vector.tensor_copy(dst[:, n, c0:c1], tab[:].bitcast(U32).indirect(offsets))
                 picked[role, half] = dst[:, n]
 
-        def reorder(dst, src):
-            nc.vector.tensor_copy(
+        def reorder(copy, dst, src):
+            copy(
                 out=dst.rearrange("p (b t q i) -> p b t q i", b=PASSES, t=PACK, q=P // RUN),
                 in_=src.rearrange("p (b q t i) -> p b t q i", b=PASSES, t=PACK, q=P // RUN),
             )
@@ -143,13 +144,13 @@ def tile_list_payment_fraud_decoder_kernel(
 
         def round_wo(part, tag):
             wo_bf[part] = keep.tile([P, WO_PART, PACK], BF16, align_bytes=64, name="wo_bf%d" % part, tag=tag)
-            first = part * WO_PART
             for b in range(PASSES):
-                c0, c1 = max(first, b * N), min(first + WO_PART, (b + 1) * N)
-                if c0 < c1:
+                places = [place for place, tile in enumerate(WO_TILES[part]) if tile[0] == b]
+                if places:
+                    first = WO_TILES[part][places[0]][1]
                     round_on_gpsimd(
-                        wo_bf[part][:, c0 - first : c1 - first, :],
-                        wo_raw[b][:, :, c0 - b * N : c1 - b * N].rearrange("p t c -> p c t"),
+                        wo_bf[part][:, places[0] * P : (places[-1] + 1) * P, :],
+                        wo_raw[b][:, :, first * P : (first + len(places)) * P].rearrange("p t c -> p c t"),
                     )
 
         def quantize_wo():
@@ -172,12 +173,17 @@ def tile_list_payment_fraud_decoder_kernel(
                 return wm_codes[:, 2 * cols.start : 2 * cols.stop].bitcast(FP4X4), w_sc["m"][:, cols]
             return wd_codes[:, cols].bitcast(FP8X4), w_sc["d"][:, cols]
 
-        def next_bank(ring="bank"):
-            return psum.tile([P, PACK * CHUNK], F32, name=ring)
+        banks = [psum.tile([P, PACK * CHUNK], F32, name="bank%d" % n) for n in range(BANKS)]
+        rings = {"vector": banks[:VECTOR_BANKS], "scalar": banks[VECTOR_BANKS:]}
+        turns = {"vector": [], "scalar": []}
+
+        def next_bank(reader="scalar"):
+            turns[reader].append(rings[reader][len(turns[reader]) % len(rings[reader])])
+            return turns[reader][-1]
 
         def project(role, b, j):
             half, c0 = divmod(j, HALF)
-            bank = next_bank("bank_d" if role == "d" else "bank")
+            bank = next_bank("vector" if role == "d" else "scalar")
             for t in range(PACK):
                 codes, scales = stationary(role, b, t)
                 nc.tensor.matmul_mx(
@@ -217,30 +223,40 @@ def tile_list_payment_fraud_decoder_kernel(
             return bank[:].rearrange("p (n t) -> p n t", t=PACK)
 
         def turned(g, b, c0):
-            return b in TURNED_PASSES[g] and c0 == 0
+            return b * GROUPS[g] + c0 < TURNED[g] * CHUNK
 
-        def take_magnitudes(roles, g, b):
-            for role in roles:
-                tile = keep.tile([P, GROUPS[g], PACK], F32, align_bytes=64, name="magnitude_%s%d%d" % (role, g, b))
-                magnitude[role, g, b] = tile
-                for c0 in range(0, GROUPS[g], CHUNK):
-                    product = (project_turned if turned(g, b, c0) else project)(role, b, starts[g] + c0)
-                    nc.scalar.activation(out=tile[:, c0 : c0 + CHUNK, :], in_=product, func=ACT.Abs)
+        def steps(g):
+            return [range(b, b + 1) for b in range(PASSES)] if g == 0 else [range(PASSES)]
 
-        def take_maximum(g, b):
-            larger[g, b] = magnitude["p", g, b][:]
-            nc.vector.tensor_tensor(
-                out=larger[g, b], in0=magnitude["p", g, b][:], in1=magnitude["m", g, b][:], op=ALU.max
-            )
+        whole = {}
+        for g, width in enumerate(GROUPS):
+            for n, step in enumerate(steps(g)):
+                for role in "pm":
+                    name = "magnitude_%s%d%d" % (role, g, n)
+                    whole[role, g, n] = keep.tile([P, len(step), width, PACK], F32, align_bytes=64, name=name)
+                    for b in step:
+                        magnitude[role, g, b] = whole[role, g, n][:, b - step.start]
+            for b in range(PASSES):
+                larger[g, b] = magnitude["p", g, b]
 
-        def negate_device(g, b):
-            tile = keep.tile([P, CHUNK, PACK], F32, name="minus_d%d%d" % (g, b))
-            nc.scalar.activation(out=tile[:], in_=project_turned("d", b, starts[g]), func=ACT.Copy, scale=-1.0)
-            minus_d[g, b] = tile[:]
+        def take_magnitude(role, g, b, c0):
+            product = (project_turned if turned(g, b, c0) else project)(role, b, starts[g] + c0)
+            nc.scalar.activation(out=magnitude[role, g, b][:, c0 : c0 + CHUNK, :], in_=product, func=ACT.Abs)
 
-        def subtract_turned(g, b):
+        def take_maxima(g):
+            for n in range(len(steps(g))):
+                nc.vector.tensor_tensor(
+                    out=whole["p", g, n][:], in0=whole["p", g, n][:], in1=whole["m", g, n][:], op=ALU.max
+                )
+
+        def negate_device(g, b, c0):
+            tile = keep.tile([P, CHUNK, PACK], F32, name="minus_d%d%d_%d" % (g, b, c0))
+            nc.scalar.activation(out=tile[:], in_=project_turned("d", b, starts[g] + c0), func=ACT.Copy, scale=-1.0)
+            minus_d[g, b, c0] = tile[:]
+
+        def subtract_turned(g, b, c0):
             bank = next_bank()
-            terms = [term.rearrange("p n t -> p (n t)") for term in (larger[g, b][:, 0:CHUNK, :], minus_d[g, b])]
+            terms = [term.rearrange("p n t -> p (n t)") for term in (larger[g, b][:, c0 : c0 + CHUNK, :], minus_d[g, b, c0])]
             for t in range(PACK):
                 cols = slice(t * P, (t + 1) * P)
                 for n, term in enumerate(terms):
@@ -252,13 +268,13 @@ def tile_list_payment_fraud_decoder_kernel(
                         stop=(n == 1),
                         is_transpose=True,
                     )
-            nc.scalar.copy(out=h_bf[g][:, b, 0:CHUNK, :], in_=bank[:].rearrange("p (t n) -> p n t", t=PACK))
+            nc.scalar.copy(out=h_bf[g][:, b, c0 : c0 + CHUNK, :], in_=bank[:].rearrange("p (t n) -> p n t", t=PACK))
 
-        def subtract(g, b, c0):
+        def subtract(g, b, c0, device):
             nc.vector.tensor_tensor(
                 out=h_bf[g][:, b, c0 : c0 + CHUNK, :],
                 in0=larger[g, b][:, c0 : c0 + CHUNK, :],
-                in1=project("d", b, starts[g] + c0),
+                in1=device,
                 op=ALU.subtract,
             )
 
@@ -276,12 +292,13 @@ def tile_list_payment_fraud_decoder_kernel(
                 order = [(n, b) for b in range(PASSES) for n in range(N_TILES)]
             else:
                 shared = PACK * CHUNK // width
-                banks = [next_bank() for n in range(0, N_TILES, shared)]
-                sums = [banks[n // shared][:, n % shared * width : (n % shared + 1) * width] for n in range(N_TILES)]
+                taken = [next_bank() for n in range(0, N_TILES, shared)]
+                sums = [taken[n // shared][:, n % shared * width : (n % shared + 1) * width] for n in range(N_TILES)]
                 order = [(n, b) for n in range(N_TILES) for b in range(PASSES)]
             result = keep.tile([P, N_TILES, width], F32, name="result%d" % g)
             for n, b in order:
-                cols = slice(b * N + n * P, b * N + (n + 1) * P)
+                place = sum(WO_TILES, ()).index((b, n))
+                cols = slice(place * P, (place + 1) * P)
                 nc.tensor.matmul_mx(
                     out=sums[n],
                     lhsT=wo_mx["codes"][:, cols].bitcast(FP8X4),
@@ -304,10 +321,12 @@ def tile_list_payment_fraud_decoder_kernel(
             if g < last_group:
                 nc.sync.dma_start(out=rows, in_=result[:])
 
-        reorder(wm_codes[:].bitcast(I32), wm_raw[:].bitcast(I32))
+        reorder(nc.scalar.copy, wm_codes[:].bitcast(U32), wm_raw[:].bitcast(U32))
+        reorder(nc.scalar.copy, w_sc["m"][:].bitcast(U32), sc_raw["m"][:].bitcast(U32))
+        identity = keep.tile([P, P], F32, align_bytes=64, name="identity", tag="wm_raw")
+        make_identity(nc, identity[:])
         gather_scales("m")
         gather_scales("p")
-        reorder(w_sc["m"][:].bitcast(I32), sc_raw["m"][:].bitcast(I32))
         gather_words([("m", 0), ("m", 1), ("p", 0), ("p", 1)], "mp")
         gather_scales("d")
         gather_words([("d", 0)], "d0")
@@ -315,45 +334,54 @@ def tile_list_payment_fraud_decoder_kernel(
             round_wp(b)
         for b in range(PASSES):
             quantize_wp(b)
-        reorder(wd_codes[:], wd_raw[:])
-        reorder(w_sc["d"][:].bitcast(I32), sc_raw["d"][:].bitcast(I32))
+        reorder(nc.vector.tensor_copy, wd_codes[:], wd_raw[:])
+        reorder(nc.vector.tensor_copy, w_sc["d"][:].bitcast(I32), sc_raw["d"][:].bitcast(I32))
         gather_words([("d", 1)], "sc_raw_d")
         round_wo(0, "wp_bf1")
 
-        def prepare(g):
-            for b in range(PASSES):
-                take_magnitudes("p" if g < EARLY_GROUPS else "pm", g, b)
-            for b in TURNED_PASSES[g]:
-                negate_device(g, b)
+        units = [(g, b, c0) for g, width in enumerate(GROUPS) for b in range(PASSES) for c0 in range(0, width, CHUNK)]
+        for unit in units[:EARLY_UNITS]:
+            take_magnitude("m", *unit)
+        feeds = []
+        for n, unit in enumerate(units):
+            feeds.extend((role, unit) for role in ("p" if n < EARLY_UNITS else "pm"))
+            if n + 1 == len(units) or units[n + 1][0] > unit[0]:
+                feeds.extend(("d", other) for other in units if other[0] == unit[0] and turned(*other))
 
-        for g in range(EARLY_GROUPS):
-            for b in range(PASSES):
-                take_magnitudes("m", g, b)
-        for g in range(AHEAD):
-            prepare(g)
+        def feed(count):
+            for role, (g, b, c0) in feeds[:count]:
+                if role == "d":
+                    negate_device(g, b, c0)
+                else:
+                    take_magnitude(role, g, b, c0)
+            return feeds[count:]
+
+        feeds = feed(sum(1 for role, unit in feeds if unit[0] == 0))
+        decoded = 0
         for g in range(len(GROUPS)):
             h_bf[g] = keep.tile([P, PASSES, GROUPS[g], PACK], BF16, align_bytes=64, name="h_bf%d" % g)
             h_codes[g] = keep.tile([P, PASSES, GROUPS[g]], U32, align_bytes=64, name="h_codes%d" % g)
             h_sc[g] = keep.tile([P, PASSES, GROUPS[g]], U8, align_bytes=64, name="h_sc%d" % g)
-            if g + AHEAD <= last_group:
-                prepare(g + AHEAD)
-            take_maximum(g, 0)
+            take_maxima(g)
             if g == WO_PARTS - 1:
                 quantize_wo()
             if g > 0:
                 quantize_h(g - 1, slice(0, PASSES))
-            take_maximum(g, 1)
-            if g >= DECODE_LAG:
-                decode(g - DECODE_LAG)
-            for b in TURNED_PASSES[g]:
-                subtract_turned(g, b)
             if g + 1 < WO_PARTS:
-                round_wo(g + 1, "magnitude_m%d1" % g)
-            for b in range(PASSES):
-                for c0 in range(0, GROUPS[g], CHUNK):
-                    if not turned(g, b, c0):
-                        subtract(g, b, c0)
+                round_wo(g + 1, "magnitude_m%d%d" % (g, len(steps(g)) - 1))
+            feeds = feed(LEAD)
+            plain = [unit for unit in units if unit[0] == g and not turned(*unit)]
+            devices = [project("d", b, starts[g] + c0) for g, b, c0 in plain]
+            feeds = feed(FEEDS - LEAD)
+            for unit, device in zip(plain, devices):
+                subtract(*unit, device)
+            for unit in units:
+                if unit[0] == g and turned(*unit):
+                    subtract_turned(*unit)
+            if g >= WO_PARTS - 1:
+                for earlier in range(decoded, g):
+                    decode(earlier)
+                decoded = g
         for b in range(PASSES):
             quantize_h(last_group, slice(b, b + 1))
-        for g in range(len(GROUPS) - DECODE_LAG, len(GROUPS)):
-            decode(g)
+        decode(last_group)

@@ -28,7 +28,7 @@ HALF = S // 2
 CHUNK = 128
 N_TILES = N // P
 GROUPS = (256, 256, 256, 128, 128)
-TURNED = (1, 1, 2, 1, 0)
+TURNED = (1, 1, 1, 1, 0)
 EARLY_UNITS = 15
 LEAD = 3
 FEEDS = 6

@@ -29,14 +29,14 @@ CHUNK = 128
 N_TILES = N // P
 GROUPS = (256, 256, 256, 128, 128)
 TURNED = (1, 1, 1, 1, 0)
-EARLY_UNITS = 15
+EARLY_UNITS = 14
 LEAD = 3
 FEEDS = 6
 BANKS = 8
 VECTOR_BANKS = 4
 WO_TILES = (((0, 0), (0, 1)), ((1, 0), (1, 1)), ((0, 2), (1, 2)))
 WO_PARTS = len(WO_TILES)
-WO_PART = PASSES * N // WO_PARTS
+WP_LOADS = 2
 FIRST = 256
 
 
@@ -51,28 +51,28 @@ def tile_list_payment_fraud_decoder_kernel(
         lists = {role: keep.tile([P, S // LIST_ROWS], U16, name="list_" + role) for role in "pmd"}
         tab_sc = keep.tile([P, T], U8, align_bytes=64, name="tab_sc")
         tab = keep.tile([P, T], I32, align_bytes=64, name="tab")
-        wp_raw = [keep.tile([P, PACK, PASS], F32, name="wp_raw%d" % b) for b in range(PASSES)]
+        wp_raw = [keep.tile([P, PACK, PASS // WP_LOADS], F32, name="wp_raw%d" % n) for n in range(PASSES * WP_LOADS)]
         wm_raw = keep.tile([P, 2 * H], U8, align_bytes=64, name="wm_raw")
         wd_raw = keep.tile([P, H], I32, align_bytes=64, name="wd_raw")
         sc_raw = {role: keep.tile([P, H], U8, align_bytes=64, name="sc_raw_" + role) for role in "md"}
         wo_raw = [keep.tile([P, PACK, N], F32, align_bytes=64, name="wo_raw%d" % b) for b in range(PASSES)]
         bias = keep.tile([P, N_TILES], F32, name="bias")
+        identity = keep.tile([P, P], F32, name="identity")
 
         nc.vector.memset(tab_sc[:].bitcast(I32), 0)
         for role in "md":
             nc.vector.memset(sc_raw[role][:].bitcast(I32), 0)
+        nc.vector.memset(identity[:], 0.0)
+        make_identity(nc, identity[:], nomemset=True)
 
         def load_scale_rows(dst, src):
             rows = src[0].rearrange("(q r) n -> r q n", r=4)
             for r in range(4):
                 nc.sync.dma_start(out=dst[r:P:QUADRANT, :].bitcast(I32), in_=rows[r].bitcast(I32))
 
-        def load_table(c0, c1):
-            nc.sync.dma_start(out=tab[:, c0:c1], in_=tab_words[0].rearrange("p n t -> p (n t)").bitcast(I32)[:, c0:c1])
-
-        def load_wp(b):
-            rows = wp.rearrange("(p j) c -> p j c", j=PACK)
-            nc.sync.dma_start(out=wp_raw[b][:], in_=rows[:, :, PASS * b : PASS * (b + 1)])
+        def load_wp(n):
+            rows = wp.rearrange("(p j) (n c) -> n p j c", j=PACK, n=len(wp_raw))
+            nc.sync.dma_start(out=wp_raw[n][:], in_=rows[n])
 
         def load_wo(b):
             rows = wo.rearrange("(b q t i) n -> b t q i n", b=PASSES, t=PACK, i=RUN)
@@ -85,14 +85,13 @@ def tile_list_payment_fraud_decoder_kernel(
         with nc.allow_non_contiguous_dma(reason="one bias value a partition"):
             nc.sync.dma_start(out=bias[:], in_=bo.rearrange("(c p) -> p c", p=P))
         load_scale_rows(tab_sc, tab_scales)
-        load_table(0, T // 2)
-        load_scale_rows(sc_raw["m"], wm_scales)
-        load_table(T // 2, T)
+        nc.sync.dma_start(out=tab[:], in_=tab_words[0].rearrange("p n t -> p (n t)").bitcast(I32))
         nc.sync.dma_start(lists["d"][:], offs3)
-        load_wp(0)
-        load_wp(1)
-        nc.sync.dma_start(out=wd_raw[:], in_=wd_words[0].rearrange("p n t -> p (n t)").bitcast(I32))
+        load_scale_rows(sc_raw["m"], wm_scales)
+        for n in range(len(wp_raw)):
+            load_wp(n)
         load_scale_rows(sc_raw["d"], wd_scales)
+        nc.sync.dma_start(out=wd_raw[:], in_=wd_words[0].rearrange("p n t -> p (n t)").bitcast(I32))
         load_wo(0)
         load_wo(1)
 
@@ -102,14 +101,15 @@ def tile_list_payment_fraud_decoder_kernel(
             picked_sc[role] = keep.tile([P, S], U8, align_bytes=64, name="picked_sc_" + role)
             nc.vector.tensor_copy(picked_sc[role][:], tab_sc[:].indirect(lists[role][:]))
 
-        def gather_words(halves, tag):
-            dst = keep.tile([P, len(halves), HALF], U32, align_bytes=64, name="picked_" + tag, tag=tag)
-            for n, (role, half) in enumerate(halves):
-                cuts = (0, FIRST, HALF) if (role, half) == ("m", 0) else (0, HALF)
-                for c0, c1 in zip(cuts, cuts[1:]):
-                    offsets = lists[role][:, (half * HALF + c0) // LIST_ROWS : (half * HALF + c1) // LIST_ROWS]
-                    nc.vector.tensor_copy(dst[:, n, c0:c1], tab[:].bitcast(U32).indirect(offsets))
-                picked[role, half] = dst[:, n]
+        def gather_words(pieces, tag):
+            dst = keep.tile([P, sum(j1 - j0 for role, j0, j1 in pieces)], U32, align_bytes=64, name="picked_" + tag, tag=tag)
+            c0 = 0
+            for role, j0, j1 in pieces:
+                offsets = lists[role][:, j0 // LIST_ROWS : j1 // LIST_ROWS]
+                nc.vector.tensor_copy(dst[:, c0 : c0 + j1 - j0], tab[:].bitcast(U32).indirect(offsets))
+                for j in range(j0, j1, CHUNK):
+                    picked[role, j] = dst[:, c0 + j - j0 : c0 + j - j0 + CHUNK]
+                c0 = c0 + j1 - j0
 
         def reorder(copy, dst, src):
             copy(
@@ -127,10 +127,12 @@ def tile_list_payment_fraud_decoder_kernel(
         def round_on_gpsimd(dst, src):
             nc.gpsimd.tensor_scalar(out=dst, in0=src, scalar1=1.0, scalar2=0.0, op0=ALU.mult, op1=ALU.add)
 
-        def round_wp(b):
+        def round_wp(n):
+            b, share = divmod(n, WP_LOADS)
+            width = P // WP_LOADS
             round_on_gpsimd(
-                wp_bf[b][:].rearrange("p t (q i) j -> p q t i j", i=RUN),
-                wp_raw[b][:].rearrange("p j (q t i) -> p q t i j", t=PACK, i=RUN),
+                wp_bf[b][:, :, share * width : (share + 1) * width].rearrange("p t (q i) j -> p q t i j", i=RUN),
+                wp_raw[n][:].rearrange("p j (q t i) -> p q t i j", t=PACK, i=RUN),
             )
 
         def quantize_wp(b):
@@ -143,7 +145,7 @@ def tile_list_payment_fraud_decoder_kernel(
         wo_bf, wo_mx = {}, {}
 
         def round_wo(part, tag):
-            wo_bf[part] = keep.tile([P, WO_PART, PACK], BF16, align_bytes=64, name="wo_bf%d" % part, tag=tag)
+            wo_bf[part] = keep.tile([P, len(WO_TILES[part]) * P, PACK], BF16, align_bytes=64, name="wo_bf%d" % part, tag=tag)
             for b in range(PASSES):
                 places = [place for place, tile in enumerate(WO_TILES[part]) if tile[0] == b]
                 if places:
@@ -154,10 +156,11 @@ def tile_list_payment_fraud_decoder_kernel(
                     )
 
         def quantize_wo():
-            wo_mx["codes"] = keep.tile([P, PASSES * N], U32, align_bytes=64, name="wo_codes", tag="wo_raw1")
+            wo_mx["codes"] = keep.tile([P, PASSES * N], U32, align_bytes=64, name="wo_codes", tag="wo_raw%d" % WO_TILES[-1][-1][0])
             wo_mx["scales"] = keep.tile([P, PASSES * N], U8, align_bytes=64, name="wo_sc")
             for part in range(WO_PARTS):
-                cols = slice(part * WO_PART, (part + 1) * WO_PART)
+                first = sum(len(tiles) for tiles in WO_TILES[:part])
+                cols = slice(first * P, (first + len(WO_TILES[part])) * P)
                 nc.vector.quantize_mx(
                     out=wo_mx["codes"][:, cols].bitcast(FP8X4),
                     scales=wo_mx["scales"][:, cols],
@@ -182,7 +185,6 @@ def tile_list_payment_fraud_decoder_kernel(
             return turns[reader][-1]
 
         def project(role, b, j):
-            half, c0 = divmod(j, HALF)
             bank = next_bank("vector" if role == "d" else "scalar")
             for t in range(PACK):
                 codes, scales = stationary(role, b, t)
@@ -190,7 +192,7 @@ def tile_list_payment_fraud_decoder_kernel(
                     out=bank[:, t * CHUNK : (t + 1) * CHUNK],
                     lhsT=codes,
                     lhsT_scale=scales,
-                    rhs=picked[role, half][:, c0 : c0 + CHUNK].bitcast(FP8X4),
+                    rhs=picked[role, j].bitcast(FP8X4),
                     rhs_scale=picked_sc[role][:, j : j + CHUNK],
                     start=True,
                     stop=True,
@@ -202,7 +204,6 @@ def tile_list_payment_fraud_decoder_kernel(
         magnitude, larger, minus_d, h_bf, h_codes, h_sc = {}, {}, {}, {}, {}, {}
 
         def project_turned(role, b, j):
-            half, c0 = divmod(j, HALF)
             cols = slice(b * PASS, (b + 1) * PASS)
             if role == "p":
                 codes, scales = wp_codes[b][:].bitcast(FP8X4), wp_sc[b][:]
@@ -213,7 +214,7 @@ def tile_list_payment_fraud_decoder_kernel(
             bank = next_bank()
             nc.tensor.matmul_mx(
                 out=bank[:],
-                lhsT=picked[role, half][:, c0 : c0 + CHUNK].bitcast(FP8X4),
+                lhsT=picked[role, j].bitcast(FP8X4),
                 lhsT_scale=picked_sc[role][:, j : j + CHUNK],
                 rhs=codes,
                 rhs_scale=scales,
@@ -323,21 +324,19 @@ def tile_list_payment_fraud_decoder_kernel(
 
         reorder(nc.scalar.copy, wm_codes[:].bitcast(U32), wm_raw[:].bitcast(U32))
         reorder(nc.scalar.copy, w_sc["m"][:].bitcast(U32), sc_raw["m"][:].bitcast(U32))
-        identity = keep.tile([P, P], F32, align_bytes=64, name="identity", tag="wm_raw")
-        make_identity(nc, identity[:])
         gather_scales("m")
         gather_scales("p")
-        gather_words([("m", 0), ("m", 1), ("p", 0), ("p", 1)], "mp")
+        gather_words([("m", 0, FIRST)], "first")
         gather_scales("d")
-        gather_words([("d", 0)], "d0")
-        for b in range(PASSES):
-            round_wp(b)
+        gather_words([("m", FIRST, HALF), ("m", HALF, S), ("p", 0, S), ("d", 0, HALF)], "sc_raw_m")
+        for n in range(len(wp_raw)):
+            round_wp(n)
         for b in range(PASSES):
             quantize_wp(b)
-        reorder(nc.vector.tensor_copy, wd_codes[:], wd_raw[:])
         reorder(nc.vector.tensor_copy, w_sc["d"][:].bitcast(I32), sc_raw["d"][:].bitcast(I32))
-        gather_words([("d", 1)], "sc_raw_d")
-        round_wo(0, "wp_bf1")
+        reorder(nc.vector.tensor_copy, wd_codes[:], wd_raw[:])
+        gather_words([("d", HALF, S)], "wd_raw")
+        round_wo(0, "sc_raw_d")
 
         units = [(g, b, c0) for g, width in enumerate(GROUPS) for b in range(PASSES) for c0 in range(0, width, CHUNK)]
         for unit in units[:EARLY_UNITS]:

@@ -25,19 +25,20 @@ RUN = 8
 QUADRANT = 32
 LIST_ROWS = 16
 HALF = S // 2
+FIRST = 256
 CHUNK = 128
 N_TILES = N // P
 GROUPS = (256, 256, 256, 128, 128)
-TURNED = (1, 1, 1, 1, 0)
-EARLY_UNITS = 14
-LEAD = 3
-FEEDS = 6
-BANKS = 8
-VECTOR_BANKS = 4
+WP_LOADS = 2
 WO_TILES = (((0, 0), (0, 1)), ((1, 0), (1, 1)), ((0, 2), (1, 2)))
 WO_PARTS = len(WO_TILES)
-WP_LOADS = 2
-FIRST = 256
+WO_PART = PASSES * N // WO_PARTS
+GPSIMD_UNIT = (WO_PARTS - 1, PASSES - 1, CHUNK)
+EARLY_UNITS = 14
+FEEDS = 6
+LEAD = 3
+BANKS = 8
+VECTOR_BANKS = 4
 
 
 def tile_list_payment_fraud_decoder_kernel(
@@ -55,7 +56,7 @@ def tile_list_payment_fraud_decoder_kernel(
         wm_raw = keep.tile([P, 2 * H], U8, align_bytes=64, name="wm_raw")
         wd_raw = keep.tile([P, H], I32, align_bytes=64, name="wd_raw")
         sc_raw = {role: keep.tile([P, H], U8, align_bytes=64, name="sc_raw_" + role) for role in "md"}
-        wo_raw = [keep.tile([P, PACK, N], F32, align_bytes=64, name="wo_raw%d" % b) for b in range(PASSES)]
+        wo_raw = keep.tile([P, PASSES, PACK, N], F32, align_bytes=64, name="wo_raw")
         bias = keep.tile([P, N_TILES], F32, name="bias")
         identity = keep.tile([P, P], F32, name="identity")
 
@@ -77,7 +78,7 @@ def tile_list_payment_fraud_decoder_kernel(
         def load_wo(b):
             rows = wo.rearrange("(b q t i) n -> b t q i n", b=PASSES, t=PACK, i=RUN)
             for t in range(PACK):
-                nc.sync.dma_start(out=wo_raw[b][:, t, :], in_=rows[b, t])
+                nc.sync.dma_start(out=wo_raw[:, b, t, :], in_=rows[b, t])
 
         nc.sync.dma_start(lists["m"][:], offs2)
         nc.sync.dma_start(lists["p"][:], offs)
@@ -102,7 +103,8 @@ def tile_list_payment_fraud_decoder_kernel(
             nc.vector.tensor_copy(picked_sc[role][:], tab_sc[:].indirect(lists[role][:]))
 
         def gather_words(pieces, tag):
-            dst = keep.tile([P, sum(j1 - j0 for role, j0, j1 in pieces)], U32, align_bytes=64, name="picked_" + tag, tag=tag)
+            width = sum(j1 - j0 for role, j0, j1 in pieces)
+            dst = keep.tile([P, width], U32, align_bytes=64, name="picked_" + tag, tag=tag)
             c0 = 0
             for role, j0, j1 in pieces:
                 offsets = lists[role][:, j0 // LIST_ROWS : j1 // LIST_ROWS]
@@ -145,22 +147,18 @@ def tile_list_payment_fraud_decoder_kernel(
         wo_bf, wo_mx = {}, {}
 
         def round_wo(part, tag):
-            wo_bf[part] = keep.tile([P, len(WO_TILES[part]) * P, PACK], BF16, align_bytes=64, name="wo_bf%d" % part, tag=tag)
-            for b in range(PASSES):
-                places = [place for place, tile in enumerate(WO_TILES[part]) if tile[0] == b]
-                if places:
-                    first = WO_TILES[part][places[0]][1]
-                    round_on_gpsimd(
-                        wo_bf[part][:, places[0] * P : (places[-1] + 1) * P, :],
-                        wo_raw[b][:, :, first * P : (first + len(places)) * P].rearrange("p t c -> p c t"),
-                    )
+            wo_bf[part] = keep.tile([P, WO_PART, PACK], BF16, align_bytes=64, name="wo_bf%d" % part, tag=tag)
+            (b0, n0), (b1, n1) = WO_TILES[part][0], WO_TILES[part][-1]
+            round_on_gpsimd(
+                wo_bf[part][:].rearrange("p (b c) t -> p b c t", b=b1 + 1 - b0),
+                wo_raw[:, b0 : b1 + 1, :, n0 * P : (n1 + 1) * P].rearrange("p b t c -> p b c t"),
+            )
 
         def quantize_wo():
-            wo_mx["codes"] = keep.tile([P, PASSES * N], U32, align_bytes=64, name="wo_codes", tag="wo_raw%d" % WO_TILES[-1][-1][0])
+            wo_mx["codes"] = keep.tile([P, PASSES * N], U32, align_bytes=64, name="wo_codes", tag="wo_raw")
             wo_mx["scales"] = keep.tile([P, PASSES * N], U8, align_bytes=64, name="wo_sc")
             for part in range(WO_PARTS):
-                first = sum(len(tiles) for tiles in WO_TILES[:part])
-                cols = slice(first * P, (first + len(WO_TILES[part])) * P)
+                cols = slice(part * WO_PART, (part + 1) * WO_PART)
                 nc.vector.quantize_mx(
                     out=wo_mx["codes"][:, cols].bitcast(FP8X4),
                     scales=wo_mx["scales"][:, cols],
@@ -178,14 +176,14 @@ def tile_list_payment_fraud_decoder_kernel(
 
         banks = [psum.tile([P, PACK * CHUNK], F32, name="bank%d" % n) for n in range(BANKS)]
         rings = {"vector": banks[:VECTOR_BANKS], "scalar": banks[VECTOR_BANKS:]}
-        turns = {"vector": [], "scalar": []}
+        taken = {"vector": [], "scalar": []}
 
-        def next_bank(reader="scalar"):
-            turns[reader].append(rings[reader][len(turns[reader]) % len(rings[reader])])
-            return turns[reader][-1]
+        def next_bank(ring):
+            taken[ring].append(rings[ring][len(taken[ring]) % len(rings[ring])])
+            return taken[ring][-1]
 
-        def project(role, b, j):
-            bank = next_bank("vector" if role == "d" else "scalar")
+        def project(role, b, j, ring):
+            bank = next_bank(ring)
             for t in range(PACK):
                 codes, scales = stationary(role, b, t)
                 nc.tensor.matmul_mx(
@@ -201,7 +199,7 @@ def tile_list_payment_fraud_decoder_kernel(
 
         starts = [sum(GROUPS[:g]) for g in range(len(GROUPS))]
         last_group = len(GROUPS) - 1
-        magnitude, larger, minus_d, h_bf, h_codes, h_sc = {}, {}, {}, {}, {}, {}
+        magnitude, device_copy, h_bf, h_codes, h_sc = {}, {}, {}, {}, {}
 
         def project_turned(role, b, j):
             cols = slice(b * PASS, (b + 1) * PASS)
@@ -211,7 +209,7 @@ def tile_list_payment_fraud_decoder_kernel(
                 codes, scales = wm_codes[:, 2 * cols.start : 2 * cols.stop].bitcast(FP4X4), w_sc["m"][:, cols]
             else:
                 codes, scales = wd_codes[:, cols].bitcast(FP8X4), w_sc["d"][:, cols]
-            bank = next_bank()
+            bank = next_bank("scalar")
             nc.tensor.matmul_mx(
                 out=bank[:],
                 lhsT=picked[role, j].bitcast(FP8X4),
@@ -224,7 +222,7 @@ def tile_list_payment_fraud_decoder_kernel(
             return bank[:].rearrange("p (n t) -> p n t", t=PACK)
 
         def turned(g, b, c0):
-            return b * GROUPS[g] + c0 < TURNED[g] * CHUNK
+            return g < last_group and b == 0 and c0 == 0
 
         def steps(g):
             return [range(b, b + 1) for b in range(PASSES)] if g == 0 else [range(PASSES)]
@@ -237,11 +235,10 @@ def tile_list_payment_fraud_decoder_kernel(
                     whole[role, g, n] = keep.tile([P, len(step), width, PACK], F32, align_bytes=64, name=name)
                     for b in step:
                         magnitude[role, g, b] = whole[role, g, n][:, b - step.start]
-            for b in range(PASSES):
-                larger[g, b] = magnitude["p", g, b]
 
         def take_magnitude(role, g, b, c0):
-            product = (project_turned if turned(g, b, c0) else project)(role, b, starts[g] + c0)
+            j = starts[g] + c0
+            product = project_turned(role, b, j) if turned(g, b, c0) else project(role, b, j, "scalar")
             nc.scalar.activation(out=magnitude[role, g, b][:, c0 : c0 + CHUNK, :], in_=product, func=ACT.Abs)
 
         def take_maxima(g):
@@ -250,14 +247,20 @@ def tile_list_payment_fraud_decoder_kernel(
                     out=whole["p", g, n][:], in0=whole["p", g, n][:], in1=whole["m", g, n][:], op=ALU.max
                 )
 
-        def negate_device(g, b, c0):
-            tile = keep.tile([P, CHUNK, PACK], F32, name="minus_d%d%d_%d" % (g, b, c0))
-            nc.scalar.activation(out=tile[:], in_=project_turned("d", b, starts[g] + c0), func=ACT.Copy, scale=-1.0)
-            minus_d[g, b, c0] = tile[:]
+        def larger(g, b, c0):
+            return magnitude["p", g, b][:, c0 : c0 + CHUNK, :]
+
+        def copy_device(g, b, c0):
+            tile = keep.tile([P, CHUNK, PACK], F32, name="device%d%d" % (g, b))
+            if turned(g, b, c0):
+                nc.scalar.activation(out=tile[:], in_=project_turned("d", b, starts[g] + c0), func=ACT.Copy, scale=-1.0)
+            else:
+                nc.scalar.copy(out=tile[:], in_=project("d", b, starts[g] + c0, "scalar"))
+            device_copy[g, b, c0] = tile[:]
 
         def subtract_turned(g, b, c0):
-            bank = next_bank()
-            terms = [term.rearrange("p n t -> p (n t)") for term in (larger[g, b][:, c0 : c0 + CHUNK, :], minus_d[g, b, c0])]
+            bank = next_bank("scalar")
+            terms = [term.rearrange("p n t -> p (n t)") for term in (larger(g, b, c0), device_copy[g, b, c0])]
             for t in range(PACK):
                 cols = slice(t * P, (t + 1) * P)
                 for n, term in enumerate(terms):
@@ -271,12 +274,9 @@ def tile_list_payment_fraud_decoder_kernel(
                     )
             nc.scalar.copy(out=h_bf[g][:, b, c0 : c0 + CHUNK, :], in_=bank[:].rearrange("p (t n) -> p n t", t=PACK))
 
-        def subtract(g, b, c0, device):
-            nc.vector.tensor_tensor(
-                out=h_bf[g][:, b, c0 : c0 + CHUNK, :],
-                in0=larger[g, b][:, c0 : c0 + CHUNK, :],
-                in1=device,
-                op=ALU.subtract,
+        def subtract(engine, g, b, c0, device):
+            engine.tensor_tensor(
+                out=h_bf[g][:, b, c0 : c0 + CHUNK, :], in0=larger(g, b, c0), in1=device, op=ALU.subtract
             )
 
         def quantize_h(g, which):
@@ -289,12 +289,12 @@ def tile_list_payment_fraud_decoder_kernel(
         def decode(g):
             width = GROUPS[g]
             if g == last_group:
-                sums = [next_bank()[:, 0:width] for n in range(N_TILES)]
+                sums = [next_bank("scalar")[:, 0:width] for n in range(N_TILES)]
                 order = [(n, b) for b in range(PASSES) for n in range(N_TILES)]
             else:
                 shared = PACK * CHUNK // width
-                taken = [next_bank() for n in range(0, N_TILES, shared)]
-                sums = [taken[n // shared][:, n % shared * width : (n % shared + 1) * width] for n in range(N_TILES)]
+                used = [next_bank("scalar") for n in range(0, N_TILES, shared)]
+                sums = [used[n // shared][:, n % shared * width : (n % shared + 1) * width] for n in range(N_TILES)]
                 order = [(n, b) for n in range(N_TILES) for b in range(PASSES)]
             result = keep.tile([P, N_TILES, width], F32, name="result%d" % g)
             for n, b in order:
@@ -342,45 +342,49 @@ def tile_list_payment_fraud_decoder_kernel(
         for unit in units[:EARLY_UNITS]:
             take_magnitude("m", *unit)
         feeds = []
-        for n, unit in enumerate(units):
-            feeds.extend((role, unit) for role in ("p" if n < EARLY_UNITS else "pm"))
-            if n + 1 == len(units) or units[n + 1][0] > unit[0]:
-                feeds.extend(("d", other) for other in units if other[0] == unit[0] and turned(*other))
+        for g in range(len(GROUPS)):
+            own = [unit for unit in units if unit[0] == g]
+            feeds.extend((role, unit) for unit in own for role in ("p" if unit in units[:EARLY_UNITS] else "pm"))
+            feeds.extend(("d", unit) for unit in own if turned(*unit) or unit == GPSIMD_UNIT)
 
         def feed(count):
-            for role, (g, b, c0) in feeds[:count]:
+            for role, unit in feeds[:count]:
                 if role == "d":
-                    negate_device(g, b, c0)
+                    copy_device(*unit)
                 else:
-                    take_magnitude(role, g, b, c0)
+                    take_magnitude(role, *unit)
             return feeds[count:]
 
         feeds = feed(sum(1 for role, unit in feeds if unit[0] == 0))
-        decoded = 0
+        first_decoding = WO_PARTS - 1
         for g in range(len(GROUPS)):
             h_bf[g] = keep.tile([P, PASSES, GROUPS[g], PACK], BF16, align_bytes=64, name="h_bf%d" % g)
             h_codes[g] = keep.tile([P, PASSES, GROUPS[g]], U32, align_bytes=64, name="h_codes%d" % g)
             h_sc[g] = keep.tile([P, PASSES, GROUPS[g]], U8, align_bytes=64, name="h_sc%d" % g)
-            take_maxima(g)
-            if g == WO_PARTS - 1:
+            if g == first_decoding:
                 quantize_wo()
+            take_maxima(g)
             if g > 0:
                 quantize_h(g - 1, slice(0, PASSES))
-            if g + 1 < WO_PARTS:
+            if g < first_decoding:
                 round_wo(g + 1, "magnitude_m%d%d" % (g, len(steps(g)) - 1))
+            own = [unit for unit in units if unit[0] == g]
+            plain = [unit for unit in own if not turned(*unit) and unit != GPSIMD_UNIT]
             feeds = feed(LEAD)
-            plain = [unit for unit in units if unit[0] == g and not turned(*unit)]
-            devices = [project("d", b, starts[g] + c0) for g, b, c0 in plain]
+            devices = [project("d", b, starts[g] + c0, "vector") for g, b, c0 in plain]
             feeds = feed(FEEDS - LEAD)
-            for unit, device in zip(plain, devices):
-                subtract(*unit, device)
-            for unit in units:
-                if unit[0] == g and turned(*unit):
-                    subtract_turned(*unit)
-            if g >= WO_PARTS - 1:
-                for earlier in range(decoded, g):
+            if g == first_decoding:
+                for earlier in range(g - 1):
                     decode(earlier)
-                decoded = g
+            for unit, device in zip(plain, devices):
+                subtract(nc.vector, *unit, device)
+            for unit in own:
+                if turned(*unit):
+                    subtract_turned(*unit)
+                if unit == GPSIMD_UNIT:
+                    subtract(nc.gpsimd, *unit, device_copy[unit])
+            if g >= first_decoding:
+                decode(g - 1)
         for b in range(PASSES):
             quantize_h(last_group, slice(b, b + 1))
         decode(last_group)

@@ -38,7 +38,7 @@ EARLY_UNITS = 14
 FEEDS = 6
 LEAD = 3
 BANKS = 8
-VECTOR_BANKS = 4
+VECTOR_BANKS = 3
 
 
 def tile_list_payment_fraud_decoder_kernel(
@@ -155,7 +155,7 @@ def tile_list_payment_fraud_decoder_kernel(
             )
 
         def quantize_wo():
-            wo_mx["codes"] = keep.tile([P, PASSES * N], U32, align_bytes=64, name="wo_codes", tag="wo_raw")
+            wo_mx["codes"] = keep.tile([P, PASSES * N], U32, align_bytes=64, name="wo_codes", tag="h_bf0")
             wo_mx["scales"] = keep.tile([P, PASSES * N], U8, align_bytes=64, name="wo_sc")
             for part in range(WO_PARTS):
                 cols = slice(part * WO_PART, (part + 1) * WO_PART)
@@ -367,7 +367,7 @@ def tile_list_payment_fraud_decoder_kernel(
             if g > 0:
                 quantize_h(g - 1, slice(0, PASSES))
             if g < first_decoding:
-                round_wo(g + 1, "magnitude_m%d%d" % (g, len(steps(g)) - 1))
+                round_wo(g + 1, "magnitude_m%d0" % g)
             own = [unit for unit in units if unit[0] == g]
             plain = [unit for unit in own if not turned(*unit) and unit != GPSIMD_UNIT]
             feeds = feed(LEAD)

@@ -25,18 +25,21 @@ RUN = 8
 QUADRANT = 32
 LIST_ROWS = 16
 HALF = S // 2
-FIRST = 256
+QUARTER = S // 4
 CHUNK = 128
 N_TILES = N // P
+SCALE_ROWS = 16
 GROUPS = (256, 256, 256, 128, 128)
-WP_LOADS = 2
-WO_TILES = (((0, 0), (0, 1)), ((1, 0), (1, 1)), ((0, 2), (1, 2)))
+WP_LOADS = 4
+WO_TILES = (((0, 2), (1, 2)), ((0, 0), (0, 1)), ((1, 0), (1, 1)))
 WO_PARTS = len(WO_TILES)
 WO_PART = PASSES * N // WO_PARTS
-GPSIMD_UNIT = (WO_PARTS - 1, PASSES - 1, CHUNK)
-EARLY_UNITS = 14
-FEEDS = 6
-LEAD = 3
+TURNED_UNITS = ((0, 0, 0), (1, 0, 0))
+GPSIMD_UNITS = ((2, 1, CHUNK),)
+EARLY_UNITS = 8
+MAXIMA = (((0, 0), (1, 0), (0, 1)), ((1, 1),), ((2, 0),), ((3, 0),), ((4, 0),))
+LEAD = (3, 3, 3, 0, 0)
+WO_TAGS = ("magnitude_m10", "magnitude_m11")
 BANKS = 8
 VECTOR_BANKS = 3
 
@@ -49,114 +52,118 @@ def tile_list_payment_fraud_decoder_kernel(
         keep = ctx.enter_context(tc.tile_pool(name="keep", bufs=1))
         psum = ctx.enter_context(tc.psum_pool(name="psum", bufs=1))
 
-        lists = {role: keep.tile([P, S // LIST_ROWS], U16, name="list_" + role) for role in "pmd"}
-        tab_sc = keep.tile([P, T], U8, align_bytes=64, name="tab_sc")
-        tab = keep.tile([P, T], I32, align_bytes=64, name="tab")
-        wp_raw = [keep.tile([P, PACK, PASS // WP_LOADS], F32, name="wp_raw%d" % n) for n in range(PASSES * WP_LOADS)]
-        wm_raw = keep.tile([P, 2 * H], U8, align_bytes=64, name="wm_raw")
-        wd_raw = keep.tile([P, H], I32, align_bytes=64, name="wd_raw")
-        sc_raw = {role: keep.tile([P, H], U8, align_bytes=64, name="sc_raw_" + role) for role in "md"}
-        wo_raw = keep.tile([P, PASSES, PACK, N], F32, align_bytes=64, name="wo_raw")
-        bias = keep.tile([P, N_TILES], F32, name="bias")
-        identity = keep.tile([P, P], F32, name="identity")
+        def sbuf(name, shape, dtype, tag=None):
+            return keep.tile(shape, dtype, align_bytes=64, name=name, tag=tag or name)
 
-        nc.vector.memset(tab_sc[:].bitcast(I32), 0)
+        lists = {role: keep.tile([P, S // LIST_ROWS], U16, name="list_" + role) for role in "pmd"}
+        tab_sc = sbuf("tab_sc", [P, T], U8)
+        tab = sbuf("tab", [P, T], I32)
+        wp_raw = [sbuf("wp_raw%d" % n, [P, PACK, H // WP_LOADS], F32) for n in range(WP_LOADS)]
+        wm_raw = sbuf("wm_raw", [P, 2 * H], U8)
+        wd_raw = sbuf("wd_raw", [P, H], I32)
+        sc_raw = {role: sbuf("sc_raw_" + role, [P, H], U8) for role in "md"}
+        wo_raw = sbuf("wo_raw", [P, PASSES, PACK, N], F32)
+        bias = sbuf("bias", [P, N_TILES], F32)
+        identity = sbuf("identity", [P, P], F32)
+
         for role in "md":
             nc.vector.memset(sc_raw[role][:].bitcast(I32), 0)
+        nc.vector.memset(tab_sc[0 : P - SCALE_ROWS, :].bitcast(I32), 0)
         nc.vector.memset(identity[:], 0.0)
-        make_identity(nc, identity[:], nomemset=True)
 
-        def load_scale_rows(dst, src):
+        def load_scale_rows(queues, dst, src):
             rows = src[0].rearrange("(q r) n -> r q n", r=4)
-            for r in range(4):
-                nc.sync.dma_start(out=dst[r:P:QUADRANT, :].bitcast(I32), in_=rows[r].bitcast(I32))
+            for r, queue in enumerate(queues):
+                queue.dma_start(out=dst[r:P:QUADRANT, :].bitcast(I32), in_=rows[r].bitcast(I32))
 
         def load_wp(n):
-            rows = wp.rearrange("(p j) (n c) -> n p j c", j=PACK, n=len(wp_raw))
+            rows = wp.rearrange("(p j) (n c) -> n p j c", j=PACK, n=WP_LOADS)
             nc.sync.dma_start(out=wp_raw[n][:], in_=rows[n])
 
-        def load_wo(b):
+        def load_wo(b, t):
             rows = wo.rearrange("(b q t i) n -> b t q i n", b=PASSES, t=PACK, i=RUN)
-            for t in range(PACK):
-                nc.sync.dma_start(out=wo_raw[:, b, t, :], in_=rows[b, t])
-
-        nc.sync.dma_start(lists["m"][:], offs2)
-        nc.sync.dma_start(lists["p"][:], offs)
-        nc.sync.dma_start(out=wm_raw[:].bitcast(I32), in_=wm_words[0].bitcast(I32))
-        with nc.allow_non_contiguous_dma(reason="one bias value a partition"):
-            nc.sync.dma_start(out=bias[:], in_=bo.rearrange("(c p) -> p c", p=P))
-        load_scale_rows(tab_sc, tab_scales)
-        nc.sync.dma_start(out=tab[:], in_=tab_words[0].rearrange("p n t -> p (n t)").bitcast(I32))
-        nc.sync.dma_start(lists["d"][:], offs3)
-        load_scale_rows(sc_raw["m"], wm_scales)
-        for n in range(len(wp_raw)):
-            load_wp(n)
-        load_scale_rows(sc_raw["d"], wd_scales)
-        nc.sync.dma_start(out=wd_raw[:], in_=wd_words[0].rearrange("p n t -> p (n t)").bitcast(I32))
-        load_wo(0)
-        load_wo(1)
+            nc.sync.dma_start(out=wo_raw[:, b, t, :], in_=rows[b, t])
 
         picked, picked_sc = {}, {}
 
-        def gather_scales(role):
-            picked_sc[role] = keep.tile([P, S], U8, align_bytes=64, name="picked_sc_" + role)
-            nc.vector.tensor_copy(picked_sc[role][:], tab_sc[:].indirect(lists[role][:]))
+        def offsets(role, j0, j1):
+            return lists[role][:, j0 // LIST_ROWS : j1 // LIST_ROWS]
 
-        def gather_words(pieces, tag):
+        early = sbuf("staged_early", [P, HALF], U8)
+        later = sbuf("staged_later", [P, 2 * S], U8)
+
+        def gather_scales(role, j0, j1, staged, c0):
+            nc.vector.tensor_copy(staged[:, c0 : c0 + j1 - j0], tab_sc[:].indirect(offsets(role, j0, j1)))
+
+        def carry_scales(pieces, staged, name):
             width = sum(j1 - j0 for role, j0, j1 in pieces)
-            dst = keep.tile([P, width], U32, align_bytes=64, name="picked_" + tag, tag=tag)
+            plane = sbuf("plane_" + name, [P, width], U8)
+            for r in range(4):
+                nc.sync.dma_start(
+                    out=plane[r:P:QUADRANT, :].bitcast(I32),
+                    in_=staged[P - SCALE_ROWS + r : P : 4, :].bitcast(I32),
+                )
             c0 = 0
             for role, j0, j1 in pieces:
-                offsets = lists[role][:, j0 // LIST_ROWS : j1 // LIST_ROWS]
-                nc.vector.tensor_copy(dst[:, c0 : c0 + j1 - j0], tab[:].bitcast(U32).indirect(offsets))
+                for j in range(j0, j1, CHUNK):
+                    picked_sc[role, j] = plane[:, c0 + j - j0 : c0 + j - j0 + CHUNK]
+                c0 = c0 + j1 - j0
+
+        def gather_words(pieces, name, tag=None):
+            width = sum(j1 - j0 for role, j0, j1 in pieces)
+            dst = sbuf("picked_" + name, [P, width], U32, tag)
+            c0 = 0
+            for role, j0, j1 in pieces:
+                nc.vector.tensor_copy(dst[:, c0 : c0 + j1 - j0], tab[:].bitcast(U32).indirect(offsets(role, j0, j1)))
                 for j in range(j0, j1, CHUNK):
                     picked[role, j] = dst[:, c0 + j - j0 : c0 + j - j0 + CHUNK]
                 c0 = c0 + j1 - j0
 
         def reorder(copy, dst, src):
             copy(
-                out=dst.rearrange("p (b t q i) -> p b t q i", b=PASSES, t=PACK, q=P // RUN),
-                in_=src.rearrange("p (b q t i) -> p b t q i", b=PASSES, t=PACK, q=P // RUN),
+                out=dst.bitcast(U32).rearrange("p (b t q i) -> p b t q i", b=PASSES, t=PACK, q=P // RUN),
+                in_=src.bitcast(U32).rearrange("p (b q t i) -> p b t q i", b=PASSES, t=PACK, q=P // RUN),
             )
 
-        wm_codes = keep.tile([P, 2 * H], U8, align_bytes=64, name="wm_codes")
-        w_sc = {role: keep.tile([P, H], U8, align_bytes=64, name="w_sc_" + role) for role in "md"}
-        wd_codes = keep.tile([P, H], I32, align_bytes=64, name="wd_codes")
-        wp_bf = [keep.tile([P, PACK, P, PACK], BF16, align_bytes=64, name="wp_bf%d" % b) for b in range(PASSES)]
-        wp_codes = [keep.tile([P, PASS], U32, align_bytes=64, name="wp_codes%d" % b) for b in range(PASSES)]
-        wp_sc = [keep.tile([P, PASS], U8, align_bytes=64, name="wp_sc%d" % b) for b in range(PASSES)]
+        wm_codes = sbuf("wm_codes", [P, 2 * H], U8)
+        wd_codes = sbuf("wd_codes", [P, H], U32)
+        w_sc = {}
+        wp_bf = {}
+        wp_codes = sbuf("wp_codes", [P, H], U32)
+        w_sc["p"] = sbuf("w_sc_p", [P, H], U8)
 
-        def round_on_gpsimd(dst, src):
-            nc.gpsimd.tensor_scalar(out=dst, in0=src, scalar1=1.0, scalar2=0.0, op0=ALU.mult, op1=ALU.add)
+        def round_on_gpsimd(out, in_):
+            nc.gpsimd.tensor_scalar(out=out, in0=in_, scalar1=1.0, scalar2=0.0, op0=ALU.mult, op1=ALU.add)
 
         def round_wp(n):
-            b, share = divmod(n, WP_LOADS)
-            width = P // WP_LOADS
+            b, share = divmod(n, WP_LOADS // PASSES)
+            width = P * PASSES // WP_LOADS
             round_on_gpsimd(
-                wp_bf[b][:, :, share * width : (share + 1) * width].rearrange("p t (q i) j -> p q t i j", i=RUN),
-                wp_raw[n][:].rearrange("p j (q t i) -> p q t i j", t=PACK, i=RUN),
+                out=wp_bf[b][:, :, share * width : (share + 1) * width].rearrange("p t (q i) j -> p q t i j", i=RUN),
+                in_=wp_raw[n][:].rearrange("p j (q t i) -> p q t i j", t=PACK, i=RUN),
             )
 
         def quantize_wp(b):
+            cols = slice(b * PASS, (b + 1) * PASS)
             nc.vector.quantize_mx(
-                out=wp_codes[b][:].bitcast(FP8X4),
-                scales=wp_sc[b][:],
+                out=wp_codes[:, cols].bitcast(FP8X4),
+                scales=w_sc["p"][:, cols],
                 in_=wp_bf[b][:].rearrange("p t c j -> p (t c j)"),
             )
 
         wo_bf, wo_mx = {}, {}
 
-        def round_wo(part, tag):
-            wo_bf[part] = keep.tile([P, WO_PART, PACK], BF16, align_bytes=64, name="wo_bf%d" % part, tag=tag)
+        def round_wo(rounding, part, tag):
+            wo_bf[part] = sbuf("wo_bf%d" % part, [P, WO_PART, PACK], BF16, tag)
             (b0, n0), (b1, n1) = WO_TILES[part][0], WO_TILES[part][-1]
-            round_on_gpsimd(
-                wo_bf[part][:].rearrange("p (b c) t -> p b c t", b=b1 + 1 - b0),
-                wo_raw[:, b0 : b1 + 1, :, n0 * P : (n1 + 1) * P].rearrange("p b t c -> p b c t"),
+            rounding(
+                out=wo_bf[part][:].rearrange("p (b c) t -> p b c t", b=b1 + 1 - b0),
+                in_=wo_raw[:, b0 : b1 + 1, :, n0 * P : (n1 + 1) * P].rearrange("p b t c -> p b c t"),
             )
 
         def quantize_wo():
-            wo_mx["codes"] = keep.tile([P, PASSES * N], U32, align_bytes=64, name="wo_codes", tag="h_bf0")
-            wo_mx["scales"] = keep.tile([P, PASSES * N], U8, align_bytes=64, name="wo_sc")
+            wo_mx["codes"] = sbuf("wo_codes", [P, PASSES * N], U32, "h_bf0")
+            wo_mx["scales"] = sbuf("wo_sc", [P, PASSES * N], U8)
             for part in range(WO_PARTS):
                 cols = slice(part * WO_PART, (part + 1) * WO_PART)
                 nc.vector.quantize_mx(
@@ -165,14 +172,10 @@ def tile_list_payment_fraud_decoder_kernel(
                     in_=wo_bf[part][:].rearrange("p c j -> p (c j)"),
                 )
 
-        def stationary(role, b, t):
-            cols = slice((b * PACK + t) * P, (b * PACK + t + 1) * P)
-            if role == "p":
-                local = slice(t * P, (t + 1) * P)
-                return wp_codes[b][:, local].bitcast(FP8X4), wp_sc[b][:, local]
+        def weights(role, cols):
             if role == "m":
                 return wm_codes[:, 2 * cols.start : 2 * cols.stop].bitcast(FP4X4), w_sc["m"][:, cols]
-            return wd_codes[:, cols].bitcast(FP8X4), w_sc["d"][:, cols]
+            return {"p": wp_codes, "d": wd_codes}[role][:, cols].bitcast(FP8X4), w_sc[role][:, cols]
 
         banks = [psum.tile([P, PACK * CHUNK], F32, name="bank%d" % n) for n in range(BANKS)]
         rings = {"vector": banks[:VECTOR_BANKS], "scalar": banks[VECTOR_BANKS:]}
@@ -182,85 +185,81 @@ def tile_list_payment_fraud_decoder_kernel(
             taken[ring].append(rings[ring][len(taken[ring]) % len(rings[ring])])
             return taken[ring][-1]
 
-        def project(role, b, j, ring):
+        starts = [sum(GROUPS[:g]) for g in range(len(GROUPS))]
+        last_group = len(GROUPS) - 1
+        magnitude, device_copy, h_bf, h_codes, h_sc = {}, {}, {}, {}, {}
+
+        def project(role, unit, ring):
+            g, b, c0 = unit
+            j = starts[g] + c0
             bank = next_bank(ring)
+            if unit in TURNED_UNITS:
+                codes, scales = weights(role, slice(b * PASS, (b + 1) * PASS))
+                nc.tensor.matmul_mx(
+                    out=bank[:],
+                    lhsT=picked[role, j].bitcast(FP8X4),
+                    lhsT_scale=picked_sc[role, j],
+                    rhs=codes,
+                    rhs_scale=scales,
+                    start=True,
+                    stop=True,
+                )
+                return bank[:].rearrange("p (n t) -> p n t", t=PACK)
             for t in range(PACK):
-                codes, scales = stationary(role, b, t)
+                codes, scales = weights(role, slice((b * PACK + t) * P, (b * PACK + t + 1) * P))
                 nc.tensor.matmul_mx(
                     out=bank[:, t * CHUNK : (t + 1) * CHUNK],
                     lhsT=codes,
                     lhsT_scale=scales,
                     rhs=picked[role, j].bitcast(FP8X4),
-                    rhs_scale=picked_sc[role][:, j : j + CHUNK],
+                    rhs_scale=picked_sc[role, j],
                     start=True,
                     stop=True,
                 )
             return bank[:].rearrange("p (t n) -> p n t", t=PACK)
 
-        starts = [sum(GROUPS[:g]) for g in range(len(GROUPS))]
-        last_group = len(GROUPS) - 1
-        magnitude, device_copy, h_bf, h_codes, h_sc = {}, {}, {}, {}, {}
-
-        def project_turned(role, b, j):
-            cols = slice(b * PASS, (b + 1) * PASS)
-            if role == "p":
-                codes, scales = wp_codes[b][:].bitcast(FP8X4), wp_sc[b][:]
-            elif role == "m":
-                codes, scales = wm_codes[:, 2 * cols.start : 2 * cols.stop].bitcast(FP4X4), w_sc["m"][:, cols]
-            else:
-                codes, scales = wd_codes[:, cols].bitcast(FP8X4), w_sc["d"][:, cols]
-            bank = next_bank("scalar")
-            nc.tensor.matmul_mx(
-                out=bank[:],
-                lhsT=picked[role, j].bitcast(FP8X4),
-                lhsT_scale=picked_sc[role][:, j : j + CHUNK],
-                rhs=codes,
-                rhs_scale=scales,
-                start=True,
-                stop=True,
-            )
-            return bank[:].rearrange("p (n t) -> p n t", t=PACK)
-
-        def turned(g, b, c0):
-            return g < last_group and b == 0 and c0 == 0
-
         def steps(g):
-            return [range(b, b + 1) for b in range(PASSES)] if g == 0 else [range(PASSES)]
+            return [range(b, b + 1) for b in range(PASSES)] if g < 2 else [range(PASSES)]
 
         whole = {}
         for g, width in enumerate(GROUPS):
             for n, step in enumerate(steps(g)):
                 for role in "pm":
-                    name = "magnitude_%s%d%d" % (role, g, n)
-                    whole[role, g, n] = keep.tile([P, len(step), width, PACK], F32, align_bytes=64, name=name)
+                    whole[role, g, n] = sbuf("magnitude_%s%d%d" % (role, g, n), [P, len(step), width, PACK], F32)
                     for b in step:
                         magnitude[role, g, b] = whole[role, g, n][:, b - step.start]
 
-        def take_magnitude(role, g, b, c0):
-            j = starts[g] + c0
-            product = project_turned(role, b, j) if turned(g, b, c0) else project(role, b, j, "scalar")
-            nc.scalar.activation(out=magnitude[role, g, b][:, c0 : c0 + CHUNK, :], in_=product, func=ACT.Abs)
+        def take_magnitude(role, unit):
+            g, b, c0 = unit
+            nc.scalar.activation(
+                out=magnitude[role, g, b][:, c0 : c0 + CHUNK, :], in_=project(role, unit, "scalar"), func=ACT.Abs
+            )
 
-        def take_maxima(g):
-            for n in range(len(steps(g))):
+        def take_maxima(turn):
+            for g, n in MAXIMA[turn]:
                 nc.vector.tensor_tensor(
                     out=whole["p", g, n][:], in0=whole["p", g, n][:], in1=whole["m", g, n][:], op=ALU.max
                 )
 
-        def larger(g, b, c0):
+        def larger(unit):
+            g, b, c0 = unit
             return magnitude["p", g, b][:, c0 : c0 + CHUNK, :]
 
-        def copy_device(g, b, c0):
-            tile = keep.tile([P, CHUNK, PACK], F32, name="device%d%d" % (g, b))
-            if turned(g, b, c0):
-                nc.scalar.activation(out=tile[:], in_=project_turned("d", b, starts[g] + c0), func=ACT.Copy, scale=-1.0)
+        def copy_device(unit):
+            tile = sbuf("device%d%d%d" % unit, [P, CHUNK, PACK], F32)
+            if unit in TURNED_UNITS:
+                nc.scalar.activation(out=tile[:], in_=project("d", unit, "scalar"), func=ACT.Copy, scale=-1.0)
             else:
-                nc.scalar.copy(out=tile[:], in_=project("d", b, starts[g] + c0, "scalar"))
-            device_copy[g, b, c0] = tile[:]
+                nc.scalar.copy(out=tile[:], in_=project("d", unit, "scalar"))
+            device_copy[unit] = tile[:]
 
-        def subtract_turned(g, b, c0):
+        def h_of(unit):
+            g, b, c0 = unit
+            return h_bf[g][:, b, c0 : c0 + CHUNK, :]
+
+        def subtract_turned(unit):
             bank = next_bank("scalar")
-            terms = [term.rearrange("p n t -> p (n t)") for term in (larger(g, b, c0), device_copy[g, b, c0])]
+            terms = [term.rearrange("p n t -> p (n t)") for term in (larger(unit), device_copy[unit])]
             for t in range(PACK):
                 cols = slice(t * P, (t + 1) * P)
                 for n, term in enumerate(terms):
@@ -272,12 +271,10 @@ def tile_list_payment_fraud_decoder_kernel(
                         stop=(n == 1),
                         is_transpose=True,
                     )
-            nc.scalar.copy(out=h_bf[g][:, b, c0 : c0 + CHUNK, :], in_=bank[:].rearrange("p (t n) -> p n t", t=PACK))
+            nc.scalar.copy(out=h_of(unit), in_=bank[:].rearrange("p (t n) -> p n t", t=PACK))
 
-        def subtract(engine, g, b, c0, device):
-            engine.tensor_tensor(
-                out=h_bf[g][:, b, c0 : c0 + CHUNK, :], in0=larger(g, b, c0), in1=device, op=ALU.subtract
-            )
+        def subtract(engine, unit, device):
+            engine.tensor_tensor(out=h_of(unit), in0=larger(unit), in1=device, op=ALU.subtract)
 
         def quantize_h(g, which):
             nc.vector.quantize_mx(
@@ -322,69 +319,101 @@ def tile_list_payment_fraud_decoder_kernel(
             if g < last_group:
                 nc.sync.dma_start(out=rows, in_=result[:])
 
-        reorder(nc.scalar.copy, wm_codes[:].bitcast(U32), wm_raw[:].bitcast(U32))
-        reorder(nc.scalar.copy, w_sc["m"][:].bitcast(U32), sc_raw["m"][:].bitcast(U32))
-        gather_scales("m")
-        gather_scales("p")
-        gather_words([("m", 0, FIRST)], "first")
-        gather_scales("d")
-        gather_words([("m", FIRST, HALF), ("m", HALF, S), ("p", 0, S), ("d", 0, HALF)], "sc_raw_m")
-        for n in range(len(wp_raw)):
-            round_wp(n)
-        for b in range(PASSES):
-            quantize_wp(b)
-        reorder(nc.vector.tensor_copy, w_sc["d"][:].bitcast(I32), sc_raw["d"][:].bitcast(I32))
-        reorder(nc.vector.tensor_copy, wd_codes[:], wd_raw[:])
-        gather_words([("d", HALF, S)], "wd_raw")
-        round_wo(0, "sc_raw_d")
-
+        nc.sync.dma_start(lists["m"][:], offs2)
+        nc.sync.dma_start(out=tab_sc[P - SCALE_ROWS : P, :].bitcast(I32), in_=tab_scales[0].bitcast(I32))
+        nc.sync.dma_start(out=wm_raw[:].bitcast(I32), in_=wm_words[0].bitcast(I32))
+        nc.sync.dma_start(lists["p"][:], offs)
+        load_scale_rows([nc.sync, nc.sync, nc.gpsimd, nc.gpsimd], sc_raw["m"], wm_scales)
+        nc.sync.dma_start(lists["d"][:], offs3)
+        nc.sync.dma_start(out=tab[:], in_=tab_words[0].rearrange("p n t -> p (n t)").bitcast(I32))
+        load_scale_rows([nc.gpsimd] * 4, sc_raw["d"], wd_scales)
+        make_identity(nc, identity[:], nomemset=True)
+        reorder(nc.scalar.copy, wm_codes[:], wm_raw[:])
+        w_sc["m"] = sbuf("w_sc_m", [P, H], U8)
+        reorder(nc.scalar.copy, w_sc["m"][:], sc_raw["m"][:])
+        gather_scales("m", 0, HALF, early, 0)
+        carry_scales([("m", 0, HALF)], early, "first")
+        for n in range(WP_LOADS):
+            load_wp(n)
+        gather_scales("m", HALF, S, later, 0)
+        gather_scales("p", 0, S, later, HALF)
+        gather_scales("d", 0, HALF, later, S + HALF)
+        carry_scales([("m", HALF, S), ("p", 0, S), ("d", 0, HALF)], later, "second")
+        nc.sync.dma_start(out=wd_raw[:], in_=wd_words[0].rearrange("p n t -> p (n t)").bitcast(I32))
+        gather_words([("m", 0, QUARTER), ("m", QUARTER, HALF), ("p", 0, HALF), ("m", HALF, S)], "first")
+        last = sbuf("staged_last", [P, HALF], U8, "staged_early")
+        gather_scales("d", HALF, S, last, 0)
+        carry_scales([("d", HALF, S)], last, "third")
+        for n in range(PASSES * PACK):
+            load_wo(*divmod(n, PACK))
+        with nc.allow_non_contiguous_dma(reason="one bias value a partition"):
+            nc.sync.dma_start(out=bias[:], in_=bo.rearrange("(c p) -> p c", p=P))
         units = [(g, b, c0) for g, width in enumerate(GROUPS) for b in range(PASSES) for c0 in range(0, width, CHUNK)]
-        for unit in units[:EARLY_UNITS]:
-            take_magnitude("m", *unit)
-        feeds = []
-        for g in range(len(GROUPS)):
-            own = [unit for unit in units if unit[0] == g]
-            feeds.extend((role, unit) for unit in own for role in ("p" if unit in units[:EARLY_UNITS] else "pm"))
-            feeds.extend(("d", unit) for unit in own if turned(*unit) or unit == GPSIMD_UNIT)
+        for unit in units[:4]:
+            take_magnitude("m", unit)
+        for b in range(PASSES):
+            wp_bf[b] = sbuf("wp_bf%d" % b, [P, PACK, P, PACK], BF16, "wp_bf")
+            for n in range(2 * b, 2 * b + 2):
+                round_wp(n)
+            quantize_wp(b)
+            if b == 0:
+                gather_words([("d", 0, HALF), ("p", HALF, S), ("d", HALF, S)], "second", "wp_raw1")
+        reorder(nc.vector.tensor_copy, wd_codes[:], wd_raw[:])
+        w_sc["d"] = sbuf("w_sc_d", [P, H], U8, "wp_raw0")
+        reorder(nc.scalar.copy, w_sc["d"][:], sc_raw["d"][:])
+        for unit in units[4:EARLY_UNITS]:
+            take_magnitude("m", unit)
+        def own(g, among=None):
+            return [unit for unit in units if unit[0] == g and (among is None or unit in among)]
 
-        def feed(count):
-            for role, unit in feeds[:count]:
-                if role == "d":
-                    copy_device(*unit)
+        def magnitudes(roles, some):
+            return [(role, unit) for unit in some for role in roles]
+
+        def feed(items):
+            for what, unit in items:
+                if what == "d":
+                    copy_device(unit)
+                elif what == "turned":
+                    subtract_turned(unit)
+                elif what == "wo":
+                    round_wo(nc.scalar.copy, 0, "wo_bf0")
+                elif what == "decode":
+                    decode(unit)
                 else:
-                    take_magnitude(role, *unit)
-            return feeds[count:]
+                    take_magnitude(what, unit)
 
-        feeds = feed(sum(1 for role, unit in feeds if unit[0] == 0))
-        first_decoding = WO_PARTS - 1
         for g in range(len(GROUPS)):
-            h_bf[g] = keep.tile([P, PASSES, GROUPS[g], PACK], BF16, align_bytes=64, name="h_bf%d" % g)
-            h_codes[g] = keep.tile([P, PASSES, GROUPS[g]], U32, align_bytes=64, name="h_codes%d" % g)
-            h_sc[g] = keep.tile([P, PASSES, GROUPS[g]], U8, align_bytes=64, name="h_sc%d" % g)
-            if g == first_decoding:
+            h_bf[g] = sbuf("h_bf%d" % g, [P, PASSES, GROUPS[g], PACK], BF16)
+            h_codes[g] = sbuf("h_codes%d" % g, [P, PASSES, GROUPS[g]], U32)
+            h_sc[g] = sbuf("h_sc%d" % g, [P, PASSES, GROUPS[g]], U8)
+        feed(magnitudes("p", own(0)[:2] + own(1)[:2]) + magnitudes("m", own(2)[:3]) + magnitudes("p", own(0)[2:]))
+        turned = [[("d", unit), ("turned", unit)] for unit in TURNED_UNITS]
+        turns = [
+            turned[0][:1] + magnitudes("p", own(1)[2:]) + turned[1][:1] + turned[0][1:] + [("wo", None)],
+            magnitudes("p", own(2)[:3]) + magnitudes("mp", own(2)[3:]) + turned[1][1:] + [("d", GPSIMD_UNITS[0])],
+            magnitudes("mp", own(3)) + [("decode", 0)] + magnitudes("mp", own(4)) + [("decode", 1)],
+            [("decode", 2)],
+            [("decode", 3)],
+        ]
+        devices = {}
+        for g in range(len(GROUPS)):
+            if g == 2:
                 quantize_wo()
             take_maxima(g)
             if g > 0:
                 quantize_h(g - 1, slice(0, PASSES))
-            if g < first_decoding:
-                round_wo(g + 1, "magnitude_m%d0" % g)
-            own = [unit for unit in units if unit[0] == g]
-            plain = [unit for unit in own if not turned(*unit) and unit != GPSIMD_UNIT]
-            feeds = feed(LEAD)
-            devices = [project("d", b, starts[g] + c0, "vector") for g, b, c0 in plain]
-            feeds = feed(FEEDS - LEAD)
-            if g == first_decoding:
-                for earlier in range(g - 1):
-                    decode(earlier)
-            for unit, device in zip(plain, devices):
-                subtract(nc.vector, *unit, device)
-            for unit in own:
-                if turned(*unit):
-                    subtract_turned(*unit)
-                if unit == GPSIMD_UNIT:
-                    subtract(nc.gpsimd, *unit, device_copy[unit])
-            if g >= first_decoding:
-                decode(g - 1)
+            if g < 2:
+                round_wo(round_on_gpsimd, g + 1, WO_TAGS[g])
+            plain = [unit for unit in own(g) if unit not in TURNED_UNITS + GPSIMD_UNITS]
+            feed(turns[g][: LEAD[g]])
+            for unit in plain + (own(last_group)[:1] if g == last_group - 1 else []):
+                if unit not in devices:
+                    devices[unit] = project("d", unit, "vector")
+            feed(turns[g][LEAD[g] :])
+            for unit in plain:
+                subtract(nc.vector, unit, devices[unit])
+            for unit in own(g, GPSIMD_UNITS):
+                subtract(nc.gpsimd, unit, device_copy[unit])
         for b in range(PASSES):
             quantize_h(last_group, slice(b, b + 1))
         decode(last_group)

@@ -237,9 +237,11 @@ def tile_list_payment_fraud_decoder_kernel(
 
         def take_maxima(turn):
             for g, n in MAXIMA[turn]:
-                nc.vector.tensor_tensor(
-                    out=whole["p", g, n][:], in0=whole["p", g, n][:], in1=whole["m", g, n][:], op=ALU.max
-                )
+                dst = whole["p", g, n]
+                if (g, n) == (0, 0):
+                    dst = sbuf("larger00", [P, 1, GROUPS[0], PACK], F32, "staged_early")
+                    magnitude["p", 0, 0] = dst[:, 0]
+                nc.vector.tensor_tensor(out=dst[:], in0=whole["p", g, n][:], in1=whole["m", g, n][:], op=ALU.max)
 
         def larger(unit):
             g, b, c0 = unit
@@ -343,8 +345,9 @@ def tile_list_payment_fraud_decoder_kernel(
         gather_words([("m", 0, QUARTER), ("m", QUARTER, HALF), ("p", 0, HALF), ("m", HALF, S)], "first")
         last = sbuf("staged_last", [P, HALF], U8, "staged_early")
         gather_scales("d", HALF, S, last, 0)
-        carry_scales([("d", HALF, S)], last, "third")
         for n in range(PASSES * PACK):
+            if n == 2:
+                carry_scales([("d", HALF, S)], last, "third")
             load_wo(*divmod(n, PACK))
         with nc.allow_non_contiguous_dma(reason="one bias value a partition"):
             nc.sync.dma_start(out=bias[:], in_=bo.rearrange("(c p) -> p c", p=P))

@@ -39,7 +39,7 @@ GPSIMD_UNITS = ((2, 1, CHUNK),)
 EARLY_UNITS = 8
 MAXIMA = (((0, 0), (1, 0), (0, 1)), ((1, 1),), ((2, 0),), ((3, 0),), ((4, 0),))
 LEAD = (3, 3, 3, 0, 0)
-WO_TAGS = ("magnitude_m10", "magnitude_m11")
+WO_TAGS = ("magnitude_m01", "magnitude_m11")
 BANKS = 8
 VECTOR_BANKS = 3
 

@@ -37,7 +37,7 @@ WO_PART = PASSES * N // WO_PARTS
 TURNED_UNITS = ((0, 0, 0), (1, 0, 0))
 GPSIMD_UNITS = ((2, 1, CHUNK),)
 EARLY_UNITS = 8
-MAXIMA = (((0, 0), (1, 0), (0, 1)), ((1, 1),), ((2, 0),), ((3, 0),), ((4, 0),))
+MAXIMA = (((0, 0), (1, 0), (0, 1)), ((1, 1),), ((2, 0), (2, 1)), ((3, 0),), ((4, 0),))
 LEAD = (3, 3, 3, 0, 0)
 WO_TAGS = ("magnitude_m01", "magnitude_m11")
 BANKS = 8
@@ -162,7 +162,7 @@ def tile_list_payment_fraud_decoder_kernel(
             )
 
         def quantize_wo():
-            wo_mx["codes"] = sbuf("wo_codes", [P, PASSES * N], U32, "h_bf0")
+            wo_mx["codes"] = sbuf("wo_codes", [P, PASSES * N], U32)
             wo_mx["scales"] = sbuf("wo_sc", [P, PASSES * N], U8)
             for part in range(WO_PARTS):
                 cols = slice(part * WO_PART, (part + 1) * WO_PART)
@@ -219,7 +219,7 @@ def tile_list_payment_fraud_decoder_kernel(
             return bank[:].rearrange("p (t n) -> p n t", t=PACK)
 
         def steps(g):
-            return [range(b, b + 1) for b in range(PASSES)] if g < 2 else [range(PASSES)]
+            return [range(b, b + 1) for b in range(PASSES)] if g < 3 else [range(PASSES)]
 
         whole = {}
         for g, width in enumerate(GROUPS):
@@ -394,16 +394,14 @@ def tile_list_payment_fraud_decoder_kernel(
         turns = [
             turned[0][:1] + magnitudes("p", own(1)[2:]) + turned[1][:1] + turned[0][1:] + [("wo", None)],
             magnitudes("p", own(2)[:3]) + magnitudes("mp", own(2)[3:]) + turned[1][1:] + [("d", GPSIMD_UNITS[0])],
-            magnitudes("mp", own(3)) + [("decode", 0)] + magnitudes("mp", own(4)) + [("decode", 1)],
-            [("decode", 2)],
+            magnitudes("mp", own(3)) + [("decode", 0)] + magnitudes("mp", own(4)),
+            [("decode", 1), ("decode", 2)],
             [("decode", 3)],
         ]
         devices = {}
         for g in range(len(GROUPS)):
-            if g == 2:
-                quantize_wo()
             take_maxima(g)
-            if g > 0:
+            if g > 2:
                 quantize_h(g - 1, slice(0, PASSES))
             if g < 2:
                 round_wo(round_on_gpsimd, g + 1, WO_TAGS[g])
@@ -417,6 +415,10 @@ def tile_list_payment_fraud_decoder_kernel(
                 subtract(nc.vector, unit, devices[unit])
             for unit in own(g, GPSIMD_UNITS):
                 subtract(nc.gpsimd, unit, device_copy[unit])
+            if g in (1, 2):
+                quantize_h(g - 1, slice(0, PASSES))
+            if g == 1:
+                quantize_wo()
         for b in range(PASSES):
             quantize_h(last_group, slice(b, b + 1))
         decode(last_group)

@@ -37,11 +37,12 @@ WO_PART = PASSES * N // WO_PARTS
 TURNED_UNITS = ((0, 0, 0), (1, 0, 0))
 GPSIMD_UNITS = ((2, 1, CHUNK),)
 EARLY_UNITS = 8
-MAXIMA = (((0, 0), (1, 0), (0, 1)), ((1, 1),), ((2, 0), (2, 1)), ((3, 0),), ((4, 0),))
+MAXIMA = (((0, 0), (1, 0), (0, 1)), ((1, 1),), ((2, 0),), ((3, 0),), ((4, 0),))
 LEAD = (3, 3, 3, 0, 0)
 WO_TAGS = ("magnitude_m01", "magnitude_m11")
 BANKS = 8
 VECTOR_BANKS = 3
+EARLY_BANKS = 4
 
 
 def tile_list_payment_fraud_decoder_kernel(
@@ -162,7 +163,7 @@ def tile_list_payment_fraud_decoder_kernel(
             )
 
         def quantize_wo():
-            wo_mx["codes"] = sbuf("wo_codes", [P, PASSES * N], U32)
+            wo_mx["codes"] = sbuf("wo_codes", [P, PASSES * N], U32, "h_bf0")
             wo_mx["scales"] = sbuf("wo_sc", [P, PASSES * N], U8)
             for part in range(WO_PARTS):
                 cols = slice(part * WO_PART, (part + 1) * WO_PART)
@@ -178,8 +179,8 @@ def tile_list_payment_fraud_decoder_kernel(
             return {"p": wp_codes, "d": wd_codes}[role][:, cols].bitcast(FP8X4), w_sc[role][:, cols]
 
         banks = [psum.tile([P, PACK * CHUNK], F32, name="bank%d" % n) for n in range(BANKS)]
-        rings = {"vector": banks[:VECTOR_BANKS], "scalar": banks[VECTOR_BANKS:]}
-        taken = {"vector": [], "scalar": []}
+        rings = {"vector": banks[:VECTOR_BANKS], "scalar": banks[VECTOR_BANKS:], "early": banks[BANKS - EARLY_BANKS :]}
+        taken = {ring: [] for ring in rings}
 
         def next_bank(ring):
             taken[ring].append(rings[ring][len(taken[ring]) % len(rings[ring])])
@@ -219,7 +220,7 @@ def tile_list_payment_fraud_decoder_kernel(
             return bank[:].rearrange("p (t n) -> p n t", t=PACK)
 
         def steps(g):
-            return [range(b, b + 1) for b in range(PASSES)] if g < 3 else [range(PASSES)]
+            return [range(b, b + 1) for b in range(PASSES)] if g < 2 else [range(PASSES)]
 
         whole = {}
         for g, width in enumerate(GROUPS):
@@ -229,10 +230,10 @@ def tile_list_payment_fraud_decoder_kernel(
                     for b in step:
                         magnitude[role, g, b] = whole[role, g, n][:, b - step.start]
 
-        def take_magnitude(role, unit):
+        def take_magnitude(role, unit, ring):
             g, b, c0 = unit
             nc.scalar.activation(
-                out=magnitude[role, g, b][:, c0 : c0 + CHUNK, :], in_=project(role, unit, "scalar"), func=ACT.Abs
+                out=magnitude[role, g, b][:, c0 : c0 + CHUNK, :], in_=project(role, unit, ring), func=ACT.Abs
             )
 
         def take_maxima(turn):
@@ -247,12 +248,12 @@ def tile_list_payment_fraud_decoder_kernel(
             g, b, c0 = unit
             return magnitude["p", g, b][:, c0 : c0 + CHUNK, :]
 
-        def copy_device(unit):
+        def copy_device(unit, ring):
             tile = sbuf("device%d%d%d" % unit, [P, CHUNK, PACK], F32)
             if unit in TURNED_UNITS:
-                nc.scalar.activation(out=tile[:], in_=project("d", unit, "scalar"), func=ACT.Copy, scale=-1.0)
+                nc.scalar.activation(out=tile[:], in_=project("d", unit, ring), func=ACT.Copy, scale=-1.0)
             else:
-                nc.scalar.copy(out=tile[:], in_=project("d", unit, "scalar"))
+                nc.scalar.copy(out=tile[:], in_=project("d", unit, ring))
             device_copy[unit] = tile[:]
 
         def h_of(unit):
@@ -335,13 +336,15 @@ def tile_list_payment_fraud_decoder_kernel(
         reorder(nc.scalar.copy, w_sc["m"][:], sc_raw["m"][:])
         gather_scales("m", 0, HALF, early, 0)
         carry_scales([("m", 0, HALF)], early, "first")
-        for n in range(WP_LOADS):
-            load_wp(n)
+        load_wp(0)
+        load_wp(1)
+        nc.sync.dma_start(out=wd_raw[:], in_=wd_words[0].rearrange("p n t -> p (n t)").bitcast(I32))
+        load_wp(2)
         gather_scales("m", HALF, S, later, 0)
         gather_scales("p", 0, S, later, HALF)
         gather_scales("d", 0, HALF, later, S + HALF)
         carry_scales([("m", HALF, S), ("p", 0, S), ("d", 0, HALF)], later, "second")
-        nc.sync.dma_start(out=wd_raw[:], in_=wd_words[0].rearrange("p n t -> p (n t)").bitcast(I32))
+        load_wp(3)
         gather_words([("m", 0, QUARTER), ("m", QUARTER, HALF), ("p", 0, HALF), ("m", HALF, S)], "first")
         last = sbuf("staged_last", [P, HALF], U8, "staged_early")
         gather_scales("d", HALF, S, last, 0)
@@ -353,29 +356,29 @@ def tile_list_payment_fraud_decoder_kernel(
             nc.sync.dma_start(out=bias[:], in_=bo.rearrange("(c p) -> p c", p=P))
         units = [(g, b, c0) for g, width in enumerate(GROUPS) for b in range(PASSES) for c0 in range(0, width, CHUNK)]
         for unit in units[:4]:
-            take_magnitude("m", unit)
+            take_magnitude("m", unit, "early")
         for b in range(PASSES):
             wp_bf[b] = sbuf("wp_bf%d" % b, [P, PACK, P, PACK], BF16, "wp_bf")
             for n in range(2 * b, 2 * b + 2):
                 round_wp(n)
             quantize_wp(b)
             if b == 0:
+                reorder(nc.vector.tensor_copy, wd_codes[:], wd_raw[:])
                 gather_words([("d", 0, HALF), ("p", HALF, S), ("d", HALF, S)], "second", "wp_raw1")
-        reorder(nc.vector.tensor_copy, wd_codes[:], wd_raw[:])
         w_sc["d"] = sbuf("w_sc_d", [P, H], U8, "wp_raw0")
         reorder(nc.scalar.copy, w_sc["d"][:], sc_raw["d"][:])
         for unit in units[4:EARLY_UNITS]:
-            take_magnitude("m", unit)
+            take_magnitude("m", unit, "early")
         def own(g, among=None):
             return [unit for unit in units if unit[0] == g and (among is None or unit in among)]
 
         def magnitudes(roles, some):
             return [(role, unit) for unit in some for role in roles]
 
-        def feed(items):
+        def feed(items, ring="scalar"):
             for what, unit in items:
                 if what == "d":
-                    copy_device(unit)
+                    copy_device(unit, ring)
                 elif what == "turned":
                     subtract_turned(unit)
                 elif what == "wo":
@@ -383,25 +386,29 @@ def tile_list_payment_fraud_decoder_kernel(
                 elif what == "decode":
                     decode(unit)
                 else:
-                    take_magnitude(what, unit)
+                    take_magnitude(what, unit, ring)
 
         for g in range(len(GROUPS)):
             h_bf[g] = sbuf("h_bf%d" % g, [P, PASSES, GROUPS[g], PACK], BF16)
             h_codes[g] = sbuf("h_codes%d" % g, [P, PASSES, GROUPS[g]], U32)
             h_sc[g] = sbuf("h_sc%d" % g, [P, PASSES, GROUPS[g]], U8)
-        feed(magnitudes("p", own(0)[:2] + own(1)[:2]) + magnitudes("m", own(2)[:3]) + magnitudes("p", own(0)[2:]))
         turned = [[("d", unit), ("turned", unit)] for unit in TURNED_UNITS]
+        devices = {}
+        feed(magnitudes("p", own(0)[:2] + own(1)[:2]), "early")
+        for unit in own(0)[1:]:
+            devices[unit] = project("d", unit, "vector")
+        feed(turned[0][:1] + turned[1][:1] + magnitudes("m", own(2)[:1]), "early")
+        feed(magnitudes("p", own(0)[2:]))
         turns = [
-            turned[0][:1] + magnitudes("p", own(1)[2:]) + turned[1][:1] + turned[0][1:] + [("wo", None)],
+            magnitudes("p", own(1)[2:]) + turned[0][1:] + magnitudes("m", own(2)[1:3]) + [("wo", None)],
             magnitudes("p", own(2)[:3]) + magnitudes("mp", own(2)[3:]) + turned[1][1:] + [("d", GPSIMD_UNITS[0])],
-            magnitudes("mp", own(3)) + [("decode", 0)] + magnitudes("mp", own(4)),
-            [("decode", 1), ("decode", 2)],
+            magnitudes("mp", own(3)) + [("decode", 0)] + magnitudes("mp", own(4)) + [("decode", 1)],
+            [("decode", 2)],
             [("decode", 3)],
         ]
-        devices = {}
         for g in range(len(GROUPS)):
             take_maxima(g)
-            if g > 2:
+            if g > 0:
                 quantize_h(g - 1, slice(0, PASSES))
             if g < 2:
                 round_wo(round_on_gpsimd, g + 1, WO_TAGS[g])
@@ -415,8 +422,6 @@ def tile_list_payment_fraud_decoder_kernel(
                 subtract(nc.vector, unit, devices[unit])
             for unit in own(g, GPSIMD_UNITS):
                 subtract(nc.gpsimd, unit, device_copy[unit])
-            if g in (1, 2):
-                quantize_h(g - 1, slice(0, PASSES))
             if g == 1:
                 quantize_wo()
         for b in range(PASSES):

@@ -31,15 +31,15 @@ N_TILES = N // P
 SCALE_ROWS = 16
 GROUPS = (256, 256, 256, 128, 128)
 WP_LOADS = 4
-WO_TILES = (((0, 2), (1, 2)), ((0, 0), (0, 1)), ((1, 0), (1, 1)))
+WO_TILES = (((0, 0), (0, 1)), ((1, 0), (1, 1)), ((0, 2), (1, 2)))
 WO_PARTS = len(WO_TILES)
 WO_PART = PASSES * N // WO_PARTS
-TURNED_UNITS = ((0, 0, 0), (1, 0, 0))
-GPSIMD_UNITS = ((2, 1, CHUNK),)
+TURNED_UNITS = ((0, 0, 0), (1, 0, 0), (2, 0, 0), (3, 0, 0))
+GPSIMD_UNITS = ()
 EARLY_UNITS = 8
-MAXIMA = (((0, 0), (1, 0), (0, 1)), ((1, 1),), ((2, 0),), ((3, 0),), ((4, 0),))
+MAXIMA = (((0, 0), (1, 0), (0, 1)), ((1, 1),), ((2, 0), (2, 1)), ((3, 0),), ((4, 0),))
 LEAD = (3, 3, 3, 0, 0)
-WO_TAGS = ("magnitude_m01", "magnitude_m11")
+WO_TAGS = ("magnitude_m01", "magnitude_m11", "magnitude_m21")
 BANKS = 8
 VECTOR_BANKS = 3
 EARLY_BANKS = 4
@@ -162,10 +162,8 @@ def tile_list_payment_fraud_decoder_kernel(
                 in_=wo_raw[:, b0 : b1 + 1, :, n0 * P : (n1 + 1) * P].rearrange("p b t c -> p b c t"),
             )
 
-        def quantize_wo():
-            wo_mx["codes"] = sbuf("wo_codes", [P, PASSES * N], U32, "h_bf0")
-            wo_mx["scales"] = sbuf("wo_sc", [P, PASSES * N], U8)
-            for part in range(WO_PARTS):
+        def quantize_wo(parts):
+            for part in parts:
                 cols = slice(part * WO_PART, (part + 1) * WO_PART)
                 nc.vector.quantize_mx(
                     out=wo_mx["codes"][:, cols].bitcast(FP8X4),
@@ -220,7 +218,7 @@ def tile_list_payment_fraud_decoder_kernel(
             return bank[:].rearrange("p (t n) -> p n t", t=PACK)
 
         def steps(g):
-            return [range(b, b + 1) for b in range(PASSES)] if g < 2 else [range(PASSES)]
+            return [range(b, b + 1) for b in range(PASSES)] if g < 3 else [range(PASSES)]
 
         whole = {}
         for g, width in enumerate(GROUPS):
@@ -286,17 +284,16 @@ def tile_list_payment_fraud_decoder_kernel(
                 in_=h_bf[g][:, which].rearrange("p b c j -> p (b c j)"),
             )
 
-        def decode(g):
+        def decode(g, tiles):
             width = GROUPS[g]
             if g == last_group:
-                sums = [next_bank("scalar")[:, 0:width] for n in range(N_TILES)]
-                order = [(n, b) for b in range(PASSES) for n in range(N_TILES)]
+                sums = {n: next_bank("scalar")[:, 0:width] for n in tiles}
+                order = [(n, b) for b in range(PASSES) for n in tiles]
             else:
-                shared = PACK * CHUNK // width
-                used = [next_bank("scalar") for n in range(0, N_TILES, shared)]
-                sums = [used[n // shared][:, n % shared * width : (n % shared + 1) * width] for n in range(N_TILES)]
-                order = [(n, b) for n in range(N_TILES) for b in range(PASSES)]
-            result = keep.tile([P, N_TILES, width], F32, name="result%d" % g)
+                bank = next_bank("scalar")
+                sums = {n: bank[:, i * width : (i + 1) * width] for i, n in enumerate(tiles)}
+                order = [(n, b) for n in tiles for b in range(PASSES)]
+            result = sbuf("result%d%d" % (g, tiles[0]), [P, len(tiles), width], F32)
             for n, b in order:
                 place = sum(WO_TILES, ()).index((b, n))
                 cols = slice(place * P, (place + 1) * P)
@@ -309,21 +306,21 @@ def tile_list_payment_fraud_decoder_kernel(
                     start=(b == 0),
                     stop=(b == PASSES - 1),
                 )
-            rows = out.rearrange("(c p) j -> p c j", p=P)[:, :, starts[g] : starts[g] + width]
-            for n in range(N_TILES):
+            rows = out.rearrange("(c p) j -> p c j", p=P)[:, tiles[0] : tiles[-1] + 1, starts[g] : starts[g] + width]
+            for i, n in enumerate(tiles):
                 if g == last_group and n == 1:
                     nc.vector.tensor_scalar(
-                        out=result[:, n, :], in0=sums[n], scalar1=bias[:, n : n + 1], scalar2=None, op0=ALU.add
+                        out=result[:, i, :], in0=sums[n], scalar1=bias[:, n : n + 1], scalar2=None, op0=ALU.add
                     )
                 else:
-                    nc.scalar.activation(out=result[:, n, :], in_=sums[n], func=ACT.Identity, bias=bias[:, n : n + 1])
+                    nc.scalar.activation(out=result[:, i, :], in_=sums[n], func=ACT.Identity, bias=bias[:, n : n + 1])
                 if g == last_group:
-                    nc.sync.dma_start(out=rows[:, n, :], in_=result[:, n, :])
+                    nc.sync.dma_start(out=rows[:, i, :], in_=result[:, i, :])
             if g < last_group:
                 nc.sync.dma_start(out=rows, in_=result[:])
 
-        nc.sync.dma_start(lists["m"][:], offs2)
         nc.sync.dma_start(out=tab_sc[P - SCALE_ROWS : P, :].bitcast(I32), in_=tab_scales[0].bitcast(I32))
+        nc.sync.dma_start(lists["m"][:], offs2)
         nc.sync.dma_start(out=wm_raw[:].bitcast(I32), in_=wm_words[0].bitcast(I32))
         nc.sync.dma_start(lists["p"][:], offs)
         load_scale_rows([nc.sync, nc.sync, nc.gpsimd, nc.gpsimd], sc_raw["m"], wm_scales)
@@ -384,7 +381,7 @@ def tile_list_payment_fraud_decoder_kernel(
                 elif what == "wo":
                     round_wo(nc.scalar.copy, 0, "wo_bf0")
                 elif what == "decode":
-                    decode(unit)
+                    decode(*unit)
                 else:
                     take_magnitude(what, unit, ring)
 
@@ -400,21 +397,23 @@ def tile_list_payment_fraud_decoder_kernel(
         feed(turned[0][:1] + turned[1][:1] + magnitudes("m", own(2)[:1]), "early")
         feed(magnitudes("p", own(0)[2:]))
         turns = [
-            magnitudes("p", own(1)[2:]) + turned[0][1:] + magnitudes("m", own(2)[1:3]) + [("wo", None)],
-            magnitudes("p", own(2)[:3]) + magnitudes("mp", own(2)[3:]) + turned[1][1:] + [("d", GPSIMD_UNITS[0])],
-            magnitudes("mp", own(3)) + [("decode", 0)] + magnitudes("mp", own(4)) + [("decode", 1)],
-            [("decode", 2)],
-            [("decode", 3)],
+            magnitudes("p", own(1)[2:]) + turned[0][1:] + magnitudes("m", own(2)[1:3]),
+            magnitudes("p", own(2)[:3]) + magnitudes("mp", own(2)[3:]) + turned[1][1:] + turned[2][:1],
+            magnitudes("mp", own(3)) + [("decode", (0, [0, 1]))] + turned[2][1:] + turned[3][:1] + magnitudes("mp", own(4)),
+            [("decode", (1, [0, 1]))] + turned[3][1:] + [("decode", (0, [2])), ("decode", (1, [2])), ("decode", (2, [0, 1])), ("decode", (2, [2]))],
+            [("decode", (3, range(N_TILES)))],
         ]
         for g in range(len(GROUPS)):
             take_maxima(g)
+            if g == 3:
+                quantize_wo([2])
             if g > 0:
                 quantize_h(g - 1, slice(0, PASSES))
-            if g < 2:
-                round_wo(round_on_gpsimd, g + 1, WO_TAGS[g])
+            if g < 3:
+                round_wo(round_on_gpsimd, g, WO_TAGS[g])
             plain = [unit for unit in own(g) if unit not in TURNED_UNITS + GPSIMD_UNITS]
             feed(turns[g][: LEAD[g]])
-            for unit in plain + (own(last_group)[:1] if g == last_group - 1 else []):
+            for unit in plain + (own(last_group) if g == last_group - 1 else []):
                 if unit not in devices:
                     devices[unit] = project("d", unit, "vector")
             feed(turns[g][LEAD[g] :])
@@ -423,7 +422,9 @@ def tile_list_payment_fraud_decoder_kernel(
             for unit in own(g, GPSIMD_UNITS):
                 subtract(nc.gpsimd, unit, device_copy[unit])
             if g == 1:
-                quantize_wo()
+                wo_mx["codes"] = sbuf("wo_codes", [P, PASSES * N], U32, "h_bf0")
+                wo_mx["scales"] = sbuf("wo_sc", [P, PASSES * N], U8)
+                quantize_wo(range(2))
         for b in range(PASSES):
             quantize_h(last_group, slice(b, b + 1))
-        decode(last_group)
+        decode(last_group, range(N_TILES))

@@ -37,9 +37,9 @@ WO_PART = PASSES * N // WO_PARTS
 TURNED_UNITS = ((0, 0, 0), (1, 0, 0), (2, 0, 0), (3, 0, 0))
 GPSIMD_UNITS = ()
 EARLY_UNITS = 8
-MAXIMA = (((0, 0), (1, 0), (0, 1)), ((1, 1),), ((2, 0), (2, 1)), ((3, 0),), ((4, 0),))
+MAXIMA = (((0, 2), (4, 6), (2, 3), (3, 4)), ((6, 8),), ((8, 10), (10, 12)), ((12, 14),), ((14, 16),))
 LEAD = (3, 3, 3, 0, 0)
-WO_TAGS = ("magnitude_m01", "magnitude_m11", "magnitude_m21")
+WO_TAGS = ("magnitude_m01128", "magnitude_m110", "magnitude_m210")
 BANKS = 8
 VECTOR_BANKS = 3
 EARLY_BANKS = 4
@@ -186,7 +186,7 @@ def tile_list_payment_fraud_decoder_kernel(
 
         starts = [sum(GROUPS[:g]) for g in range(len(GROUPS))]
         last_group = len(GROUPS) - 1
-        magnitude, device_copy, h_bf, h_codes, h_sc = {}, {}, {}, {}, {}
+        magnitude, larger, device_copy, h_bf, h_codes, h_sc = {}, {}, {}, {}, {}, {}
 
         def project(role, unit, ring):
             g, b, c0 = unit
@@ -217,34 +217,27 @@ def tile_list_payment_fraud_decoder_kernel(
                 )
             return bank[:].rearrange("p (t n) -> p n t", t=PACK)
 
-        def steps(g):
-            return [range(b, b + 1) for b in range(PASSES)] if g < 3 else [range(PASSES)]
-
+        units = [(g, b, c0) for g, width in enumerate(GROUPS) for b in range(PASSES) for c0 in range(0, width, CHUNK)]
+        steps = [[tuple(units[first:end]) for first, end in turn] for turn in MAXIMA]
         whole = {}
-        for g, width in enumerate(GROUPS):
-            for n, step in enumerate(steps(g)):
-                for role in "pm":
-                    whole[role, g, n] = sbuf("magnitude_%s%d%d" % (role, g, n), [P, len(step), width, PACK], F32)
-                    for b in step:
-                        magnitude[role, g, b] = whole[role, g, n][:, b - step.start]
+        for step in sum(steps, []):
+            for role in "pm":
+                whole[role, step] = sbuf("magnitude_%s%d%d%d" % (role, *step[0]), [P, len(step), CHUNK, PACK], F32)
+                for n, unit in enumerate(step):
+                    magnitude[role, unit] = whole[role, step][:, n]
 
         def take_magnitude(role, unit, ring):
-            g, b, c0 = unit
-            nc.scalar.activation(
-                out=magnitude[role, g, b][:, c0 : c0 + CHUNK, :], in_=project(role, unit, ring), func=ACT.Abs
-            )
+            nc.scalar.activation(out=magnitude[role, unit], in_=project(role, unit, ring), func=ACT.Abs)
 
         def take_maxima(turn):
-            for g, n in MAXIMA[turn]:
-                dst = whole["p", g, n]
-                if (g, n) == (0, 0):
-                    dst = sbuf("larger00", [P, 1, GROUPS[0], PACK], F32, "staged_early")
-                    magnitude["p", 0, 0] = dst[:, 0]
-                nc.vector.tensor_tensor(out=dst[:], in0=whole["p", g, n][:], in1=whole["m", g, n][:], op=ALU.max)
-
-        def larger(unit):
-            g, b, c0 = unit
-            return magnitude["p", g, b][:, c0 : c0 + CHUNK, :]
+            for step in steps[turn]:
+                dst = whole["p", step][:]
+                if turn == 0:
+                    first = sum(steps[0], ()).index(step[0])
+                    dst = first_larger[:, first : first + len(step)]
+                nc.vector.tensor_tensor(out=dst, in0=whole["p", step][:], in1=whole["m", step][:], op=ALU.max)
+                for n, unit in enumerate(step):
+                    larger[unit] = dst[:, n]
 
         def copy_device(unit, ring):
             tile = sbuf("device%d%d%d" % unit, [P, CHUNK, PACK], F32)
@@ -260,7 +253,7 @@ def tile_list_payment_fraud_decoder_kernel(
 
         def subtract_turned(unit):
             bank = next_bank("scalar")
-            terms = [term.rearrange("p n t -> p (n t)") for term in (larger(unit), device_copy[unit])]
+            terms = [term.rearrange("p n t -> p (n t)") for term in (larger[unit], device_copy[unit])]
             for t in range(PACK):
                 cols = slice(t * P, (t + 1) * P)
                 for n, term in enumerate(terms):
@@ -275,7 +268,7 @@ def tile_list_payment_fraud_decoder_kernel(
             nc.scalar.copy(out=h_of(unit), in_=bank[:].rearrange("p (t n) -> p n t", t=PACK))
 
         def subtract(engine, unit, device):
-            engine.tensor_tensor(out=h_of(unit), in0=larger(unit), in1=device, op=ALU.subtract)
+            engine.tensor_tensor(out=h_of(unit), in0=larger[unit], in1=device, op=ALU.subtract)
 
         def quantize_h(g, which):
             nc.vector.quantize_mx(
@@ -351,7 +344,6 @@ def tile_list_payment_fraud_decoder_kernel(
             load_wo(*divmod(n, PACK))
         with nc.allow_non_contiguous_dma(reason="one bias value a partition"):
             nc.sync.dma_start(out=bias[:], in_=bo.rearrange("(c p) -> p c", p=P))
-        units = [(g, b, c0) for g, width in enumerate(GROUPS) for b in range(PASSES) for c0 in range(0, width, CHUNK)]
         for unit in units[:4]:
             take_magnitude("m", unit, "early")
         for b in range(PASSES):
@@ -391,6 +383,7 @@ def tile_list_payment_fraud_decoder_kernel(
             h_sc[g] = sbuf("h_sc%d" % g, [P, PASSES, GROUPS[g]], U8)
         turned = [[("d", unit), ("turned", unit)] for unit in TURNED_UNITS]
         devices = {}
+        first_larger = sbuf("first_larger", [P, len(sum(steps[0], ())), CHUNK, PACK], F32, "staged_early")
         feed(magnitudes("p", own(0)[:2] + own(1)[:2]), "early")
         for unit in own(0)[1:]:
             devices[unit] = project("d", unit, "vector")

@@ -36,6 +36,7 @@ WO_PARTS = len(WO_TILES)
 WO_PART = PASSES * N // WO_PARTS
 TURNED_UNITS = ((0, 0, 0), (1, 0, 0), (2, 0, 0), (3, 0, 0))
 GPSIMD_UNITS = ()
+SHARED = 64
 EARLY_UNITS = 8
 MAXIMA = (((0, 2), (4, 6), (2, 3), (3, 4)), ((6, 8),), ((8, 10), (10, 12)), ((12, 14),), ((14, 16),))
 LEAD = (3, 3, 3, 0, 0)
@@ -267,8 +268,8 @@ def tile_list_payment_fraud_decoder_kernel(
                     )
             nc.scalar.copy(out=h_of(unit), in_=bank[:].rearrange("p (t n) -> p n t", t=PACK))
 
-        def subtract(engine, unit, device):
-            engine.tensor_tensor(out=h_of(unit), in0=larger[unit], in1=device, op=ALU.subtract)
+        def subtract(engine, unit, cols, device):
+            engine.tensor_tensor(out=h_of(unit)[:, cols], in0=larger[unit][:, cols], in1=device, op=ALU.subtract)
 
         def quantize_h(g, which):
             nc.vector.quantize_mx(
@@ -370,8 +371,8 @@ def tile_list_payment_fraud_decoder_kernel(
                     copy_device(unit, ring)
                 elif what == "turned":
                     subtract_turned(unit)
-                elif what == "wo":
-                    round_wo(nc.scalar.copy, 0, "wo_bf0")
+                elif what == "rest":
+                    nc.scalar.copy(out=device_rest[:], in_=devices[unit][:, SHARED:CHUNK])
                 elif what == "decode":
                     decode(*unit)
                 else:
@@ -383,6 +384,7 @@ def tile_list_payment_fraud_decoder_kernel(
             h_sc[g] = sbuf("h_sc%d" % g, [P, PASSES, GROUPS[g]], U8)
         turned = [[("d", unit), ("turned", unit)] for unit in TURNED_UNITS]
         devices = {}
+        device_rest = sbuf("device_rest", [P, CHUNK - SHARED, PACK], F32)
         first_larger = sbuf("first_larger", [P, len(sum(steps[0], ())), CHUNK, PACK], F32, "staged_early")
         feed(magnitudes("p", own(0)[:2] + own(1)[:2]), "early")
         for unit in own(0)[1:]:
@@ -393,7 +395,7 @@ def tile_list_payment_fraud_decoder_kernel(
             magnitudes("p", own(1)[2:]) + turned[0][1:] + magnitudes("m", own(2)[1:3]),
             magnitudes("p", own(2)[:3]) + magnitudes("mp", own(2)[3:]) + turned[1][1:] + turned[2][:1],
             magnitudes("mp", own(3)) + [("decode", (0, [0, 1]))] + turned[2][1:] + turned[3][:1] + magnitudes("mp", own(4)),
-            [("decode", (1, [0, 1]))] + turned[3][1:] + [("decode", (0, [2])), ("decode", (1, [2])), ("decode", (2, [0, 1])), ("decode", (2, [2]))],
+            [("decode", (1, [0, 1]))] + turned[3][1:] + [("rest", units[-1]), ("decode", (0, [2])), ("decode", (1, [2])), ("decode", (2, [0, 1])), ("decode", (2, [2]))],
             [("decode", (3, range(N_TILES)))],
         ]
         for g in range(len(GROUPS)):
@@ -411,9 +413,10 @@ def tile_list_payment_fraud_decoder_kernel(
                     devices[unit] = project("d", unit, "vector")
             feed(turns[g][LEAD[g] :])
             for unit in plain:
-                subtract(nc.vector, unit, devices[unit])
-            for unit in own(g, GPSIMD_UNITS):
-                subtract(nc.gpsimd, unit, device_copy[unit])
+                cols = slice(0, SHARED if unit == units[-1] else CHUNK)
+                subtract(nc.vector, unit, cols, devices[unit][:, cols])
+            if g == last_group:
+                subtract(nc.gpsimd, units[-1], slice(SHARED, CHUNK), device_rest[:])
             if g == 1:
                 wo_mx["codes"] = sbuf("wo_codes", [P, PASSES * N], U32, "h_bf0")
                 wo_mx["scales"] = sbuf("wo_sc", [P, PASSES * N], U8)

@@ -38,7 +38,7 @@ TURNED_UNITS = ((0, 0, 0), (1, 0, 0), (2, 0, 0), (3, 0, 0))
 GPSIMD_UNITS = ()
 SHARED = 64
 EARLY_UNITS = 8
-MAXIMA = (((0, 2), (4, 6), (2, 3), (3, 4)), ((6, 8),), ((8, 10), (10, 12)), ((12, 14),), ((14, 16),))
+MAXIMA = (((0, 2), (4, 6), (2, 3), (3, 4)), ((6, 8),), ((8, 10), (10, 12)), ((12, 13), (13, 14)), ((14, 16),))
 LEAD = (3, 3, 3, 0, 0)
 WO_TAGS = ("magnitude_m01128", "magnitude_m110", "magnitude_m210")
 BANKS = 8
@@ -320,7 +320,6 @@ def tile_list_payment_fraud_decoder_kernel(
         load_scale_rows([nc.sync, nc.sync, nc.gpsimd, nc.gpsimd], sc_raw["m"], wm_scales)
         nc.sync.dma_start(lists["d"][:], offs3)
         nc.sync.dma_start(out=tab[:], in_=tab_words[0].rearrange("p n t -> p (n t)").bitcast(I32))
-        load_scale_rows([nc.gpsimd] * 4, sc_raw["d"], wd_scales)
         make_identity(nc, identity[:], nomemset=True)
         reorder(nc.scalar.copy, wm_codes[:], wm_raw[:])
         w_sc["m"] = sbuf("w_sc_m", [P, H], U8)
@@ -330,6 +329,7 @@ def tile_list_payment_fraud_decoder_kernel(
         load_wp(0)
         load_wp(1)
         nc.sync.dma_start(out=wd_raw[:], in_=wd_words[0].rearrange("p n t -> p (n t)").bitcast(I32))
+        load_scale_rows([nc.sync] * 4, sc_raw["d"], wd_scales)
         load_wp(2)
         gather_scales("m", HALF, S, later, 0)
         gather_scales("p", 0, S, later, HALF)
@@ -355,10 +355,10 @@ def tile_list_payment_fraud_decoder_kernel(
             if b == 0:
                 reorder(nc.vector.tensor_copy, wd_codes[:], wd_raw[:])
                 gather_words([("d", 0, HALF), ("p", HALF, S), ("d", HALF, S)], "second", "wp_raw1")
-        w_sc["d"] = sbuf("w_sc_d", [P, H], U8, "wp_raw0")
-        reorder(nc.scalar.copy, w_sc["d"][:], sc_raw["d"][:])
         for unit in units[4:EARLY_UNITS]:
             take_magnitude("m", unit, "early")
+        w_sc["d"] = sbuf("w_sc_d", [P, H], U8)
+        reorder(nc.scalar.copy, w_sc["d"][:], sc_raw["d"][:])
         def own(g, among=None):
             return [unit for unit in units if unit[0] == g and (among is None or unit in among)]
 

@@ -35,11 +35,10 @@ WO_TILES = (((0, 0), (0, 1)), ((1, 0), (1, 1)), ((0, 2), (1, 2)))
 WO_PARTS = len(WO_TILES)
 WO_PART = PASSES * N // WO_PARTS
 TURNED_UNITS = ((0, 0, 0), (1, 0, 0), (2, 0, 0), (3, 0, 0))
-GPSIMD_UNITS = ()
 SHARED = 64
-EARLY_UNITS = 8
+EARLY_UNITS = 9
 MAXIMA = (((0, 2), (4, 6), (2, 3), (3, 4)), ((6, 8),), ((8, 10), (10, 12)), ((12, 13), (13, 14)), ((14, 16),))
-LEAD = (3, 3, 3, 0, 0)
+LEAD = (1, 3, 3, 0, 0)
 WO_TAGS = ("magnitude_m01128", "magnitude_m110", "magnitude_m210")
 BANKS = 8
 VECTOR_BANKS = 3
@@ -91,8 +90,8 @@ def tile_list_payment_fraud_decoder_kernel(
         def offsets(role, j0, j1):
             return lists[role][:, j0 // LIST_ROWS : j1 // LIST_ROWS]
 
-        early = sbuf("staged_early", [P, HALF], U8)
-        later = sbuf("staged_later", [P, 2 * S], U8)
+        early = sbuf("staged_early", [P, S], U8)
+        later = sbuf("staged_later", [P, S], U8)
 
         def gather_scales(role, j0, j1, staged, c0):
             nc.vector.tensor_copy(staged[:, c0 : c0 + j1 - j0], tab_sc[:].indirect(offsets(role, j0, j1)))
@@ -194,7 +193,13 @@ def tile_list_payment_fraud_decoder_kernel(
             j = starts[g] + c0
             bank = next_bank(ring)
             if unit in TURNED_UNITS:
-                codes, scales = weights(role, slice(b * PASS, (b + 1) * PASS))
+                cols = slice(b * PASS, (b + 1) * PASS)
+                if role == "m":
+                    codes, scales = wm_raw[:, 2 * cols.start : 2 * cols.stop].bitcast(FP4X4), sc_raw["m"][:, cols]
+                elif role == "d":
+                    codes, scales = wd_raw[:, cols].bitcast(FP8X4), sc_raw["d"][:, cols]
+                else:
+                    codes, scales = weights(role, cols)
                 nc.tensor.matmul_mx(
                     out=bank[:],
                     lhsT=picked[role, j].bitcast(FP8X4),
@@ -204,7 +209,9 @@ def tile_list_payment_fraud_decoder_kernel(
                     start=True,
                     stop=True,
                 )
-                return bank[:].rearrange("p (n t) -> p n t", t=PACK)
+                if role == "p":
+                    return bank[:].rearrange("p (t q i) -> p t q i", t=PACK, i=RUN)
+                return bank[:].rearrange("p (q t i) -> p t q i", t=PACK, i=RUN)
             for t in range(PACK):
                 codes, scales = weights(role, slice((b * PACK + t) * P, (b * PACK + t + 1) * P))
                 nc.tensor.matmul_mx(
@@ -227,8 +234,12 @@ def tile_list_payment_fraud_decoder_kernel(
                 for n, unit in enumerate(step):
                     magnitude[role, unit] = whole[role, step][:, n]
 
+        def by_slot(tile):
+            return tile.rearrange("p n t -> p (n t)").rearrange("p (t q i) -> p t q i", t=PACK, i=RUN)
+
         def take_magnitude(role, unit, ring):
-            nc.scalar.activation(out=magnitude[role, unit], in_=project(role, unit, ring), func=ACT.Abs)
+            dst = by_slot(magnitude[role, unit]) if unit in TURNED_UNITS else magnitude[role, unit]
+            nc.scalar.activation(out=dst, in_=project(role, unit, ring), func=ACT.Abs)
 
         def take_maxima(turn):
             for step in steps[turn]:
@@ -242,10 +253,7 @@ def tile_list_payment_fraud_decoder_kernel(
 
         def copy_device(unit, ring):
             tile = sbuf("device%d%d%d" % unit, [P, CHUNK, PACK], F32)
-            if unit in TURNED_UNITS:
-                nc.scalar.activation(out=tile[:], in_=project("d", unit, ring), func=ACT.Copy, scale=-1.0)
-            else:
-                nc.scalar.copy(out=tile[:], in_=project("d", unit, ring))
+            nc.scalar.activation(out=by_slot(tile[:]), in_=project("d", unit, ring), func=ACT.Copy, scale=-1.0)
             device_copy[unit] = tile[:]
 
         def h_of(unit):
@@ -315,37 +323,37 @@ def tile_list_payment_fraud_decoder_kernel(
 
         nc.sync.dma_start(out=tab_sc[P - SCALE_ROWS : P, :].bitcast(I32), in_=tab_scales[0].bitcast(I32))
         nc.sync.dma_start(lists["m"][:], offs2)
-        nc.sync.dma_start(out=wm_raw[:].bitcast(I32), in_=wm_words[0].bitcast(I32))
         nc.sync.dma_start(lists["p"][:], offs)
-        load_scale_rows([nc.sync, nc.sync, nc.gpsimd, nc.gpsimd], sc_raw["m"], wm_scales)
         nc.sync.dma_start(lists["d"][:], offs3)
+        load_scale_rows([nc.sync, nc.sync, nc.gpsimd, nc.gpsimd], sc_raw["m"], wm_scales)
         nc.sync.dma_start(out=tab[:], in_=tab_words[0].rearrange("p n t -> p (n t)").bitcast(I32))
         make_identity(nc, identity[:], nomemset=True)
-        reorder(nc.scalar.copy, wm_codes[:], wm_raw[:])
+        gather_scales("m", 0, S, early, 0)
+        carry_scales([("m", 0, S)], early, "first")
+        nc.sync.dma_start(out=wm_raw[:].bitcast(I32), in_=wm_words[0].bitcast(I32))
         w_sc["m"] = sbuf("w_sc_m", [P, H], U8)
         reorder(nc.scalar.copy, w_sc["m"][:], sc_raw["m"][:])
-        gather_scales("m", 0, HALF, early, 0)
-        carry_scales([("m", 0, HALF)], early, "first")
+        reorder(nc.scalar.copy, wm_codes[:], wm_raw[:])
         load_wp(0)
         load_wp(1)
-        nc.sync.dma_start(out=wd_raw[:], in_=wd_words[0].rearrange("p n t -> p (n t)").bitcast(I32))
         load_scale_rows([nc.sync] * 4, sc_raw["d"], wd_scales)
         load_wp(2)
-        gather_scales("m", HALF, S, later, 0)
-        gather_scales("p", 0, S, later, HALF)
-        gather_scales("d", 0, HALF, later, S + HALF)
-        carry_scales([("m", HALF, S), ("p", 0, S), ("d", 0, HALF)], later, "second")
+        gather_scales("p", 0, HALF, later, 0)
+        gather_scales("d", 0, HALF, later, HALF)
+        carry_scales([("p", 0, HALF), ("d", 0, HALF)], later, "second")
         load_wp(3)
+        nc.sync.dma_start(out=wd_raw[:], in_=wd_words[0].rearrange("p n t -> p (n t)").bitcast(I32))
         gather_words([("m", 0, QUARTER), ("m", QUARTER, HALF), ("p", 0, HALF), ("m", HALF, S)], "first")
-        last = sbuf("staged_last", [P, HALF], U8, "staged_early")
-        gather_scales("d", HALF, S, last, 0)
+        last = sbuf("staged_last", [P, S], U8, "staged_early")
+        gather_scales("p", HALF, S, last, 0)
+        gather_scales("d", HALF, S, last, HALF)
+        carry_scales([("p", HALF, S), ("d", HALF, S)], last, "third")
         for n in range(PASSES * PACK):
-            if n == 2:
-                carry_scales([("d", HALF, S)], last, "third")
             load_wo(*divmod(n, PACK))
         with nc.allow_non_contiguous_dma(reason="one bias value a partition"):
             nc.sync.dma_start(out=bias[:], in_=bo.rearrange("(c p) -> p c", p=P))
-        for unit in units[:4]:
+        early_units = sorted(units[:EARLY_UNITS], key=lambda unit: unit not in TURNED_UNITS[:2])
+        for unit in early_units[:4]:
             take_magnitude("m", unit, "early")
         for b in range(PASSES):
             wp_bf[b] = sbuf("wp_bf%d" % b, [P, PACK, P, PACK], BF16, "wp_bf")
@@ -353,12 +361,11 @@ def tile_list_payment_fraud_decoder_kernel(
                 round_wp(n)
             quantize_wp(b)
             if b == 0:
-                reorder(nc.vector.tensor_copy, wd_codes[:], wd_raw[:])
                 gather_words([("d", 0, HALF), ("p", HALF, S), ("d", HALF, S)], "second", "wp_raw1")
-        for unit in units[4:EARLY_UNITS]:
+        reorder(nc.vector.tensor_copy, wd_codes[:], wd_raw[:])
+        for unit in early_units[4:]:
             take_magnitude("m", unit, "early")
-        w_sc["d"] = sbuf("w_sc_d", [P, H], U8)
-        reorder(nc.scalar.copy, w_sc["d"][:], sc_raw["d"][:])
+
         def own(g, among=None):
             return [unit for unit in units if unit[0] == g and (among is None or unit in among)]
 
@@ -387,9 +394,9 @@ def tile_list_payment_fraud_decoder_kernel(
         device_rest = sbuf("device_rest", [P, CHUNK - SHARED, PACK], F32)
         first_larger = sbuf("first_larger", [P, len(sum(steps[0], ())), CHUNK, PACK], F32, "staged_early")
         feed(magnitudes("p", own(0)[:2] + own(1)[:2]), "early")
-        for unit in own(0)[1:]:
-            devices[unit] = project("d", unit, "vector")
-        feed(turned[0][:1] + turned[1][:1] + magnitudes("m", own(2)[:1]), "early")
+        w_sc["d"] = sbuf("w_sc_d", [P, H], U8)
+        reorder(nc.scalar.copy, w_sc["d"][:], sc_raw["d"][:])
+        feed(turned[0][:1] + turned[1][:1], "early")
         feed(magnitudes("p", own(0)[2:]))
         turns = [
             magnitudes("p", own(1)[2:]) + turned[0][1:] + magnitudes("m", own(2)[1:3]),
@@ -406,7 +413,7 @@ def tile_list_payment_fraud_decoder_kernel(
                 quantize_h(g - 1, slice(0, PASSES))
             if g < 3:
                 round_wo(round_on_gpsimd, g, WO_TAGS[g])
-            plain = [unit for unit in own(g) if unit not in TURNED_UNITS + GPSIMD_UNITS]
+            plain = [unit for unit in own(g) if unit not in TURNED_UNITS]
             feed(turns[g][: LEAD[g]])
             for unit in plain + (own(last_group) if g == last_group - 1 else []):
                 if unit not in devices:

@@ -36,7 +36,7 @@ WO_PARTS = len(WO_TILES)
 WO_PART = PASSES * N // WO_PARTS
 TURNED_UNITS = ((0, 0, 0), (1, 0, 0), (2, 0, 0), (3, 0, 0))
 SHARED = 64
-EARLY_UNITS = 9
+EARLY_UNITS = 8
 MAXIMA = (((0, 2), (4, 6), (2, 3), (3, 4)), ((6, 8),), ((8, 10), (10, 12)), ((12, 13), (13, 14)), ((14, 16),))
 LEAD = (1, 3, 3, 0, 0)
 WO_TAGS = ("magnitude_m01128", "magnitude_m110", "magnitude_m210")
@@ -91,7 +91,7 @@ def tile_list_payment_fraud_decoder_kernel(
             return lists[role][:, j0 // LIST_ROWS : j1 // LIST_ROWS]
 
         early = sbuf("staged_early", [P, S], U8)
-        later = sbuf("staged_later", [P, S], U8)
+        later = sbuf("staged_later", [P, S + HALF], U8)
 
         def gather_scales(role, j0, j1, staged, c0):
             nc.vector.tensor_copy(staged[:, c0 : c0 + j1 - j0], tab_sc[:].indirect(offsets(role, j0, j1)))
@@ -338,16 +338,15 @@ def tile_list_payment_fraud_decoder_kernel(
         load_wp(1)
         load_scale_rows([nc.sync] * 4, sc_raw["d"], wd_scales)
         load_wp(2)
-        gather_scales("p", 0, HALF, later, 0)
-        gather_scales("d", 0, HALF, later, HALF)
-        carry_scales([("p", 0, HALF), ("d", 0, HALF)], later, "second")
+        gather_scales("p", 0, S, later, 0)
+        gather_scales("d", 0, HALF, later, S)
+        carry_scales([("p", 0, S), ("d", 0, HALF)], later, "second")
         load_wp(3)
         nc.sync.dma_start(out=wd_raw[:], in_=wd_words[0].rearrange("p n t -> p (n t)").bitcast(I32))
         gather_words([("m", 0, QUARTER), ("m", QUARTER, HALF), ("p", 0, HALF), ("m", HALF, S)], "first")
-        last = sbuf("staged_last", [P, S], U8, "staged_early")
-        gather_scales("p", HALF, S, last, 0)
-        gather_scales("d", HALF, S, last, HALF)
-        carry_scales([("p", HALF, S), ("d", HALF, S)], last, "third")
+        last = sbuf("staged_last", [P, HALF], U8, "staged_early")
+        gather_scales("d", HALF, S, last, 0)
+        carry_scales([("d", HALF, S)], last, "third")
         for n in range(PASSES * PACK):
             load_wo(*divmod(n, PACK))
         with nc.allow_non_contiguous_dma(reason="one bias value a partition"):
@@ -396,10 +395,10 @@ def tile_list_payment_fraud_decoder_kernel(
         feed(magnitudes("p", own(0)[:2] + own(1)[:2]), "early")
         w_sc["d"] = sbuf("w_sc_d", [P, H], U8)
         reorder(nc.scalar.copy, w_sc["d"][:], sc_raw["d"][:])
-        feed(turned[0][:1] + turned[1][:1], "early")
+        feed(magnitudes("m", own(2)[:1]) + turned[0][:1] + turned[1][:1] + magnitudes("m", own(2)[1:2]), "early")
         feed(magnitudes("p", own(0)[2:]))
         turns = [
-            magnitudes("p", own(1)[2:]) + turned[0][1:] + magnitudes("m", own(2)[1:3]),
+            magnitudes("p", own(1)[2:]) + turned[0][1:] + magnitudes("m", own(2)[2:3]),
             magnitudes("p", own(2)[:3]) + magnitudes("mp", own(2)[3:]) + turned[1][1:] + turned[2][:1],
             magnitudes("mp", own(3)) + [("decode", (0, [0, 1]))] + turned[2][1:] + turned[3][:1] + magnitudes("mp", own(4)),
             [("decode", (1, [0, 1]))] + turned[3][1:] + [("rest", units[-1]), ("decode", (0, [2])), ("decode", (1, [2])), ("decode", (2, [0, 1])), ("decode", (2, [2]))],

@@ -34,12 +34,12 @@ WP_LOADS = 4
 WO_TILES = (((0, 0), (0, 1)), ((1, 0), (1, 1)), ((0, 2), (1, 2)))
 WO_PARTS = len(WO_TILES)
 WO_PART = PASSES * N // WO_PARTS
-TURNED_UNITS = ((0, 0, 0), (1, 0, 0), (2, 0, 0), (3, 0, 0))
+TURNED_UNITS = ((2, 0, 0),)
+GPSIMD_UNITS = ((1, 0, 0), (1, 0, 128))
+RETURNED_UNITS = ((0, 1, 0), (0, 1, 128), (1, 1, 0), (1, 1, 128), (4, 0, 0), (4, 1, 0))
 SHARED = 64
 EARLY_UNITS = 8
-MAXIMA = (((0, 2), (4, 6), (2, 3), (3, 4)), ((6, 8),), ((8, 10), (10, 12)), ((12, 13), (13, 14)), ((14, 16),))
-LEAD = (1, 3, 3, 0, 0)
-WO_TAGS = ("magnitude_m01128", "magnitude_m110", "magnitude_m210")
+MAXIMA = (((0, 2), (4, 6)), (), ((8, 10), (10, 12)), ((12, 14),))
 BANKS = 8
 VECTOR_BANKS = 3
 EARLY_BANKS = 4
@@ -154,11 +154,11 @@ def tile_list_payment_fraud_decoder_kernel(
 
         wo_bf, wo_mx = {}, {}
 
-        def round_wo(rounding, part, tag):
-            wo_bf[part] = sbuf("wo_bf%d" % part, [P, WO_PART, PACK], BF16, tag)
+        def round_wo(rounding, part, dst):
+            wo_bf[part] = dst
             (b0, n0), (b1, n1) = WO_TILES[part][0], WO_TILES[part][-1]
             rounding(
-                out=wo_bf[part][:].rearrange("p (b c) t -> p b c t", b=b1 + 1 - b0),
+                out=dst.rearrange("p (b c) t -> p b c t", b=b1 + 1 - b0),
                 in_=wo_raw[:, b0 : b1 + 1, :, n0 * P : (n1 + 1) * P].rearrange("p b t c -> p b c t"),
             )
 
@@ -168,7 +168,7 @@ def tile_list_payment_fraud_decoder_kernel(
                 nc.vector.quantize_mx(
                     out=wo_mx["codes"][:, cols].bitcast(FP8X4),
                     scales=wo_mx["scales"][:, cols],
-                    in_=wo_bf[part][:].rearrange("p c j -> p (c j)"),
+                    in_=wo_bf[part].rearrange("p c j -> p (c j)"),
                 )
 
         def weights(role, cols):
@@ -177,22 +177,27 @@ def tile_list_payment_fraud_decoder_kernel(
             return {"p": wp_codes, "d": wd_codes}[role][:, cols].bitcast(FP8X4), w_sc[role][:, cols]
 
         banks = [psum.tile([P, PACK * CHUNK], F32, name="bank%d" % n) for n in range(BANKS)]
-        rings = {"vector": banks[:VECTOR_BANKS], "scalar": banks[VECTOR_BANKS:], "early": banks[BANKS - EARLY_BANKS :]}
-        taken = {ring: [] for ring in rings}
+        rings = {"vector": range(VECTOR_BANKS), "scalar": range(VECTOR_BANKS, BANKS), "early": range(BANKS - EARLY_BANKS, BANKS)}
+        by_age = list(range(BANKS))
 
         def next_bank(ring):
-            taken[ring].append(rings[ring][len(taken[ring]) % len(rings[ring])])
-            return taken[ring][-1]
+            oldest = [n for n in by_age if n in rings[ring]][0]
+            by_age.remove(oldest)
+            by_age.append(oldest)
+            return banks[oldest]
 
         starts = [sum(GROUPS[:g]) for g in range(len(GROUPS))]
         last_group = len(GROUPS) - 1
         magnitude, larger, device_copy, h_bf, h_codes, h_sc = {}, {}, {}, {}, {}, {}
 
+        def turned_product(role, unit):
+            return unit in TURNED_UNITS or (role == "m" and unit in RETURNED_UNITS)
+
         def project(role, unit, ring):
             g, b, c0 = unit
             j = starts[g] + c0
             bank = next_bank(ring)
-            if unit in TURNED_UNITS:
+            if turned_product(role, unit):
                 cols = slice(b * PASS, (b + 1) * PASS)
                 if role == "m":
                     codes, scales = wm_raw[:, 2 * cols.start : 2 * cols.stop].bitcast(FP4X4), sc_raw["m"][:, cols]
@@ -234,11 +239,15 @@ def tile_list_payment_fraud_decoder_kernel(
                 for n, unit in enumerate(step):
                     magnitude[role, unit] = whole[role, step][:, n]
 
+        for unit in RETURNED_UNITS:
+            for role in "pm":
+                magnitude[role, unit] = sbuf("magnitude_%s%d%d%d" % (role, *unit), [P, CHUNK, PACK], F32)[:]
+
         def by_slot(tile):
             return tile.rearrange("p n t -> p (n t)").rearrange("p (t q i) -> p t q i", t=PACK, i=RUN)
 
         def take_magnitude(role, unit, ring):
-            dst = by_slot(magnitude[role, unit]) if unit in TURNED_UNITS else magnitude[role, unit]
+            dst = by_slot(magnitude[role, unit]) if turned_product(role, unit) else magnitude[role, unit]
             nc.scalar.activation(out=dst, in_=project(role, unit, ring), func=ACT.Abs)
 
         def take_maxima(turn):
@@ -253,8 +262,25 @@ def tile_list_payment_fraud_decoder_kernel(
 
         def copy_device(unit, ring):
             tile = sbuf("device%d%d%d" % unit, [P, CHUNK, PACK], F32)
-            nc.scalar.activation(out=by_slot(tile[:]), in_=project("d", unit, ring), func=ACT.Copy, scale=-1.0)
+            if unit in TURNED_UNITS:
+                nc.scalar.activation(out=by_slot(tile[:]), in_=project("d", unit, ring), func=ACT.Copy, scale=-1.0)
+            else:
+                nc.scalar.copy(out=tile[:], in_=project("d", unit, ring))
             device_copy[unit] = tile[:]
+
+        def turn_back(unit):
+            bank = next_bank("vector")
+            term = magnitude["m", unit].rearrange("p n t -> p (n t)")
+            for t in range(PACK):
+                cols = slice(t * P, (t + 1) * P)
+                nc.tensor.matmul(
+                    out=bank[:, cols], lhsT=term[:, cols], rhs=identity[:], start=True, stop=True, is_transpose=True
+                )
+            return bank[:].rearrange("p (t n) -> p n t", t=PACK)
+
+        def take_maximum_from(bank, unit, tag=None):
+            larger[unit] = sbuf("larger%d%d%d" % unit, [P, CHUNK, PACK], F32, tag)[:] if tag else magnitude["p", unit]
+            nc.vector.tensor_tensor(out=larger[unit], in0=magnitude["p", unit], in1=bank, op=ALU.max)
 
         def h_of(unit):
             g, b, c0 = unit
@@ -287,6 +313,9 @@ def tile_list_payment_fraud_decoder_kernel(
             )
 
         def decode(g, tiles):
+            add_bias(g, tiles, multiply(g, tiles))
+
+        def multiply(g, tiles):
             width = GROUPS[g]
             if g == last_group:
                 sums = {n: next_bank("scalar")[:, 0:width] for n in tiles}
@@ -295,7 +324,6 @@ def tile_list_payment_fraud_decoder_kernel(
                 bank = next_bank("scalar")
                 sums = {n: bank[:, i * width : (i + 1) * width] for i, n in enumerate(tiles)}
                 order = [(n, b) for n in tiles for b in range(PASSES)]
-            result = sbuf("result%d%d" % (g, tiles[0]), [P, len(tiles), width], F32)
             for n, b in order:
                 place = sum(WO_TILES, ()).index((b, n))
                 cols = slice(place * P, (place + 1) * P)
@@ -308,6 +336,11 @@ def tile_list_payment_fraud_decoder_kernel(
                     start=(b == 0),
                     stop=(b == PASSES - 1),
                 )
+            return sums
+
+        def add_bias(g, tiles, sums):
+            width = GROUPS[g]
+            result = sbuf("result%d%d" % (g, tiles[0]), [P, len(tiles), width], F32)
             rows = out.rearrange("(c p) j -> p c j", p=P)[:, tiles[0] : tiles[-1] + 1, starts[g] : starts[g] + width]
             for i, n in enumerate(tiles):
                 if g == last_group and n == 1:
@@ -346,12 +379,12 @@ def tile_list_payment_fraud_decoder_kernel(
         gather_words([("m", 0, QUARTER), ("m", QUARTER, HALF), ("p", 0, HALF), ("m", HALF, S)], "first")
         last = sbuf("staged_last", [P, HALF], U8, "staged_early")
         gather_scales("d", HALF, S, last, 0)
-        carry_scales([("d", HALF, S)], last, "third")
         for n in range(PASSES * PACK):
             load_wo(*divmod(n, PACK))
+        carry_scales([("d", HALF, S)], last, "third")
         with nc.allow_non_contiguous_dma(reason="one bias value a partition"):
             nc.sync.dma_start(out=bias[:], in_=bo.rearrange("(c p) -> p c", p=P))
-        early_units = sorted(units[:EARLY_UNITS], key=lambda unit: unit not in TURNED_UNITS[:2])
+        early_units = sorted(units[:EARLY_UNITS], key=lambda unit: (unit[0], -unit[1]))
         for unit in early_units[:4]:
             take_magnitude("m", unit, "early")
         for b in range(PASSES):
@@ -361,7 +394,6 @@ def tile_list_payment_fraud_decoder_kernel(
             quantize_wp(b)
             if b == 0:
                 gather_words([("d", 0, HALF), ("p", HALF, S), ("d", HALF, S)], "second", "wp_raw1")
-        reorder(nc.vector.tensor_copy, wd_codes[:], wd_raw[:])
         for unit in early_units[4:]:
             take_magnitude("m", unit, "early")
 
@@ -385,48 +417,89 @@ def tile_list_payment_fraud_decoder_kernel(
                     take_magnitude(what, unit, ring)
 
         for g in range(len(GROUPS)):
-            h_bf[g] = sbuf("h_bf%d" % g, [P, PASSES, GROUPS[g], PACK], BF16)
+            if g != 1:
+                h_bf[g] = sbuf("h_bf%d" % g, [P, PASSES, GROUPS[g], PACK], BF16)
             h_codes[g] = sbuf("h_codes%d" % g, [P, PASSES, GROUPS[g]], U32)
             h_sc[g] = sbuf("h_sc%d" % g, [P, PASSES, GROUPS[g]], U8)
         turned = [[("d", unit), ("turned", unit)] for unit in TURNED_UNITS]
         devices = {}
         device_rest = sbuf("device_rest", [P, CHUNK - SHARED, PACK], F32)
-        first_larger = sbuf("first_larger", [P, len(sum(steps[0], ())), CHUNK, PACK], F32, "staged_early")
-        feed(magnitudes("p", own(0)[:2] + own(1)[:2]), "early")
+        first_larger = sbuf("first_larger", [P, len(sum(steps[0], ())), CHUNK, PACK], F32, "wp_raw3")
         w_sc["d"] = sbuf("w_sc_d", [P, H], U8)
         reorder(nc.scalar.copy, w_sc["d"][:], sc_raw["d"][:])
-        feed(magnitudes("m", own(2)[:1]) + turned[0][:1] + turned[1][:1] + magnitudes("m", own(2)[1:2]), "early")
+        feed(magnitudes("p", own(0)[:2] + own(1)[:2]) + magnitudes("m", own(2)[:1]), "early")
+        ahead = project("m", own(2)[1], "early")
+        backs = [turn_back(unit) for unit in own(0)[2:]]
+        reorder(nc.scalar.copy, wd_codes[:], wd_raw[:])
         feed(magnitudes("p", own(0)[2:]))
-        turns = [
-            magnitudes("p", own(1)[2:]) + turned[0][1:] + magnitudes("m", own(2)[2:3]),
-            magnitudes("p", own(2)[:3]) + magnitudes("mp", own(2)[3:]) + turned[1][1:] + turned[2][:1],
-            magnitudes("mp", own(3)) + [("decode", (0, [0, 1]))] + turned[2][1:] + turned[3][:1] + magnitudes("mp", own(4)),
-            [("decode", (1, [0, 1]))] + turned[3][1:] + [("rest", units[-1]), ("decode", (0, [2])), ("decode", (1, [2])), ("decode", (2, [0, 1])), ("decode", (2, [2]))],
-            [("decode", (3, range(N_TILES)))],
-        ]
-        for g in range(len(GROUPS)):
-            take_maxima(g)
-            if g == 3:
-                quantize_wo([2])
-            if g > 0:
-                quantize_h(g - 1, slice(0, PASSES))
-            if g < 3:
-                round_wo(round_on_gpsimd, g, WO_TAGS[g])
-            plain = [unit for unit in own(g) if unit not in TURNED_UNITS]
-            feed(turns[g][: LEAD[g]])
-            for unit in plain + (own(last_group) if g == last_group - 1 else []):
-                if unit not in devices:
-                    devices[unit] = project("d", unit, "vector")
-            feed(turns[g][LEAD[g] :])
-            for unit in plain:
-                cols = slice(0, SHARED if unit == units[-1] else CHUNK)
-                subtract(nc.vector, unit, cols, devices[unit][:, cols])
-            if g == last_group:
-                subtract(nc.gpsimd, units[-1], slice(SHARED, CHUNK), device_rest[:])
-            if g == 1:
-                wo_mx["codes"] = sbuf("wo_codes", [P, PASSES * N], U32, "h_bf0")
-                wo_mx["scales"] = sbuf("wo_sc", [P, PASSES * N], U8)
-                quantize_wo(range(2))
+        devices[units[0]] = project("d", units[0], "vector")
+        nc.scalar.activation(out=magnitude["m", own(2)[1]], in_=ahead, func=ACT.Abs)
+        feed(magnitudes("p", own(1)[2:]))
+        wo_mx["scales"] = sbuf("wo_sc", [P, PASSES * N], U8)
+
+        take_maxima(0)
+        for part, tag in enumerate(("magnitude_m000", "magnitude_m100")):
+            round_wo(round_on_gpsimd, part, sbuf("wo_bf%d" % part, [P, WO_PART, PACK], BF16, tag)[:])
+        for bank, unit, tag, copied in zip(backs, own(0)[2:], ("magnitude_p000", "magnitude_p100"), GPSIMD_UNITS):
+            take_maximum_from(bank, unit, tag)
+            devices[units[len(devices)]] = project("d", units[len(devices)], "vector")
+            feed([("d", copied)])
+        subtract(nc.vector, units[0], slice(0, CHUNK), devices[units[0]])
+        devices[units[3]] = project("d", units[3], "vector")
+        feed(magnitudes("m", own(2)[2:3]) + magnitudes("p", own(2)[:2]))
+        for unit in own(0)[1:]:
+            subtract(nc.vector, unit, slice(0, CHUNK), devices[unit])
+
+        backs = [turn_back(unit) for unit in own(1)[2:]]
+        wo_mx["codes"] = sbuf("wo_codes", [P, PASSES * N], U32, "magnitude_p000")
+        quantize_wo([0])
+        quantize_h(0, slice(0, PASSES))
+        h_bf[1] = sbuf("h_bf1", [P, PASSES, GROUPS[1], PACK], BF16, "h_bf0")
+        quantize_wo([1])
+        for unit in GPSIMD_UNITS:
+            subtract(nc.gpsimd, unit, slice(0, CHUNK), device_copy[unit])
+        feed(magnitudes("p", own(2)[2:3]))
+        devices[units[6]] = project("d", units[6], "vector")
+        feed(magnitudes("mp", own(2)[3:]))
+        for bank, unit in zip(backs, own(1)[2:]):
+            take_maximum_from(bank, unit)
+        devices[units[7]] = project("d", units[7], "vector")
+        feed(turned[0][:1] + [("decode", (0, [0, 1]))])
+        for unit in own(1)[2:]:
+            subtract(nc.vector, unit, slice(0, CHUNK), devices[unit])
+
+        take_maxima(2)
+        quantize_h(1, slice(0, PASSES))
+        round_wo(round_on_gpsimd, 2, sbuf("wo_last", [P, WO_PART, PACK], BF16, "magnitude_m210")[:])
+        feed(magnitudes("mp", own(3)[:1]) + magnitudes("m", own(3)[1:]))
+        for unit in own(2)[1:]:
+            devices[unit] = project("d", unit, "vector")
+        feed(magnitudes("p", own(3)[1:]) + turned[0][1:] + [("d", units[12])] + magnitudes("m", own(4)) + [("decode", (1, [0, 1]))])
+        for unit in own(2)[1:]:
+            subtract(nc.vector, unit, slice(0, CHUNK), devices[unit])
+
+        quantize_wo([2])
+        take_maxima(3)
+        quantize_h(2, slice(0, PASSES))
+        subtract(nc.gpsimd, units[12], slice(0, CHUNK), device_copy[units[12]])
+        devices[units[13]] = project("d", units[13], "vector")
+        feed(magnitudes("p", own(4)[:1]))
+        backs = [turn_back(unit) for unit in own(4)]
+        feed(magnitudes("p", own(4)[1:]) + [("decode", (0, [2])), ("decode", (1, [2]))])
+        sums = multiply(2, [0, 1])
+        subtract(nc.vector, units[13], slice(0, CHUNK), devices[units[13]])
+        devices[units[15]] = project("d", units[15], "vector")
+        feed([("rest", units[15])])
+        add_bias(2, [0, 1], sums)
+        take_maximum_from(backs[0], units[14])
+        devices[units[14]] = project("d", units[14], "vector")
+        feed([("decode", (2, [2]))])
+        take_maximum_from(backs[1], units[15])
+        quantize_h(3, slice(0, PASSES))
+        feed([("decode", (3, range(N_TILES)))])
+        subtract(nc.vector, units[14], slice(0, CHUNK), devices[units[14]])
+        subtract(nc.vector, units[15], slice(0, SHARED), devices[units[15]][:, 0:SHARED])
+        subtract(nc.gpsimd, units[15], slice(SHARED, CHUNK), device_rest[:])
         for b in range(PASSES):
             quantize_h(last_group, slice(b, b + 1))
         decode(last_group, range(N_TILES))

@@ -23,25 +23,20 @@ PASS = P * PACK
 PASSES = H // PASS
 RUN = 8
 QUADRANT = 32
+SCALE_ROWS = 16
 LIST_ROWS = 16
 HALF = S // 2
 QUARTER = S // 4
 CHUNK = 128
 N_TILES = N // P
-SCALE_ROWS = 16
 GROUPS = (256, 256, 256, 128, 128)
 WP_LOADS = 4
 WO_TILES = (((0, 0), (0, 1)), ((1, 0), (1, 1)), ((0, 2), (1, 2)))
-WO_PARTS = len(WO_TILES)
-WO_PART = PASSES * N // WO_PARTS
-TURNED_UNITS = ((2, 0, 0),)
-GPSIMD_UNITS = ((1, 0, 0), (1, 0, 128))
-RETURNED_UNITS = ((0, 1, 0), (0, 1, 128), (1, 1, 0), (1, 1, 128), (4, 0, 0), (4, 1, 0))
-SHARED = 64
-EARLY_UNITS = 8
-MAXIMA = (((0, 2), (4, 6)), (), ((8, 10), (10, 12)), ((12, 14),))
+WO_PART = PASSES * N // len(WO_TILES)
+TURNED = (0, 8)
+RETURNED = (2, 3, 5, 14, 15)
+VECTOR_SHARE = 64
 BANKS = 8
-VECTOR_BANKS = 3
 EARLY_BANKS = 4
 
 
@@ -90,269 +85,254 @@ def tile_list_payment_fraud_decoder_kernel(
         def offsets(role, j0, j1):
             return lists[role][:, j0 // LIST_ROWS : j1 // LIST_ROWS]
 
-        early = sbuf("staged_early", [P, S], U8)
-        later = sbuf("staged_later", [P, S + HALF], U8)
+        def by_chunk(into, tile, pieces):
+            c0 = 0
+            for role, j0, j1 in pieces:
+                for j in range(j0, j1, CHUNK):
+                    into[role, j] = tile[:, c0 + j - j0 : c0 + j - j0 + CHUNK]
+                c0 = c0 + j1 - j0
 
-        def gather_scales(role, j0, j1, staged, c0):
-            nc.vector.tensor_copy(staged[:, c0 : c0 + j1 - j0], tab_sc[:].indirect(offsets(role, j0, j1)))
+        def gather(dst, window, pieces):
+            c0 = 0
+            for role, j0, j1 in pieces:
+                nc.vector.tensor_copy(dst[:, c0 : c0 + j1 - j0], window.indirect(offsets(role, j0, j1)))
+                c0 = c0 + j1 - j0
 
-        def carry_scales(pieces, staged, name):
-            width = sum(j1 - j0 for role, j0, j1 in pieces)
-            plane = sbuf("plane_" + name, [P, width], U8)
+        def width_of(pieces):
+            return sum(j1 - j0 for role, j0, j1 in pieces)
+
+        def gather_scales(pieces, name, tag=None):
+            staged = sbuf("staged_" + name, [P, width_of(pieces)], U8, tag)
+            gather(staged, tab_sc[:], pieces)
+            return staged
+
+        def carry_scales(pieces, name, staged):
+            plane = sbuf("plane_" + name, [P, width_of(pieces)], U8)
             for r in range(4):
                 nc.sync.dma_start(
                     out=plane[r:P:QUADRANT, :].bitcast(I32),
                     in_=staged[P - SCALE_ROWS + r : P : 4, :].bitcast(I32),
                 )
-            c0 = 0
-            for role, j0, j1 in pieces:
-                for j in range(j0, j1, CHUNK):
-                    picked_sc[role, j] = plane[:, c0 + j - j0 : c0 + j - j0 + CHUNK]
-                c0 = c0 + j1 - j0
+            by_chunk(picked_sc, plane, pieces)
 
         def gather_words(pieces, name, tag=None):
-            width = sum(j1 - j0 for role, j0, j1 in pieces)
-            dst = sbuf("picked_" + name, [P, width], U32, tag)
-            c0 = 0
-            for role, j0, j1 in pieces:
-                nc.vector.tensor_copy(dst[:, c0 : c0 + j1 - j0], tab[:].bitcast(U32).indirect(offsets(role, j0, j1)))
-                for j in range(j0, j1, CHUNK):
-                    picked[role, j] = dst[:, c0 + j - j0 : c0 + j - j0 + CHUNK]
-                c0 = c0 + j1 - j0
+            words = sbuf("picked_" + name, [P, width_of(pieces)], U32, tag)
+            gather(words, tab[:].bitcast(U32), pieces)
+            by_chunk(picked, words, pieces)
 
-        def reorder(copy, dst, src):
-            copy(
+        def reorder(dst, src):
+            nc.scalar.copy(
                 out=dst.bitcast(U32).rearrange("p (b t q i) -> p b t q i", b=PASSES, t=PACK, q=P // RUN),
                 in_=src.bitcast(U32).rearrange("p (b q t i) -> p b t q i", b=PASSES, t=PACK, q=P // RUN),
             )
 
-        wm_codes = sbuf("wm_codes", [P, 2 * H], U8)
-        wd_codes = sbuf("wd_codes", [P, H], U32)
-        w_sc = {}
-        wp_bf = {}
-        wp_codes = sbuf("wp_codes", [P, H], U32)
-        w_sc["p"] = sbuf("w_sc_p", [P, H], U8)
+        codes = {"p": sbuf("wp_codes", [P, H], U32), "m": sbuf("wm_codes", [P, 2 * H], U8), "d": sbuf("wd_codes", [P, H], U32)}
+        scales = {role: sbuf("w_sc_" + role, [P, H], U8) for role in "pmd"}
+        raw_codes = {"m": wm_raw, "d": wd_raw}
 
-        def round_on_gpsimd(out, in_):
-            nc.gpsimd.tensor_scalar(out=out, in0=in_, scalar1=1.0, scalar2=0.0, op0=ALU.mult, op1=ALU.add)
+        def round_to_bf16(dst, src):
+            nc.gpsimd.tensor_scalar(out=dst, in0=src, scalar1=1.0, scalar2=0.0, op0=ALU.mult, op1=ALU.add)
 
-        def round_wp(n):
-            b, share = divmod(n, WP_LOADS // PASSES)
-            width = P * PASSES // WP_LOADS
-            round_on_gpsimd(
-                out=wp_bf[b][:, :, share * width : (share + 1) * width].rearrange("p t (q i) j -> p q t i j", i=RUN),
-                in_=wp_raw[n][:].rearrange("p j (q t i) -> p q t i j", t=PACK, i=RUN),
-            )
+        def quantize(dst_codes, dst_scales, src):
+            nc.vector.quantize_mx(out=dst_codes.bitcast(FP8X4), scales=dst_scales, in_=src)
 
         def quantize_wp(b):
-            cols = slice(b * PASS, (b + 1) * PASS)
-            nc.vector.quantize_mx(
-                out=wp_codes[:, cols].bitcast(FP8X4),
-                scales=w_sc["p"][:, cols],
-                in_=wp_bf[b][:].rearrange("p t c j -> p (t c j)"),
-            )
-
-        wo_bf, wo_mx = {}, {}
-
-        def round_wo(rounding, part, dst):
-            wo_bf[part] = dst
-            (b0, n0), (b1, n1) = WO_TILES[part][0], WO_TILES[part][-1]
-            rounding(
-                out=dst.rearrange("p (b c) t -> p b c t", b=b1 + 1 - b0),
-                in_=wo_raw[:, b0 : b1 + 1, :, n0 * P : (n1 + 1) * P].rearrange("p b t c -> p b c t"),
-            )
-
-        def quantize_wo(parts):
-            for part in parts:
-                cols = slice(part * WO_PART, (part + 1) * WO_PART)
-                nc.vector.quantize_mx(
-                    out=wo_mx["codes"][:, cols].bitcast(FP8X4),
-                    scales=wo_mx["scales"][:, cols],
-                    in_=wo_bf[part].rearrange("p c j -> p (c j)"),
+            rounded = sbuf("wp_bf%d" % b, [P, PACK, P, PACK], BF16, "wp_bf")
+            width = P * PASSES // WP_LOADS
+            for share in range(WP_LOADS // PASSES):
+                round_to_bf16(
+                    rounded[:, :, share * width : (share + 1) * width].rearrange("p t (q i) j -> p q t i j", i=RUN),
+                    wp_raw[b * WP_LOADS // PASSES + share][:].rearrange("p j (q t i) -> p q t i j", t=PACK, i=RUN),
                 )
+            cols = slice(b * PASS, (b + 1) * PASS)
+            quantize(codes["p"][:, cols], scales["p"][:, cols], rounded[:].rearrange("p t c j -> p (t c j)"))
 
-        def weights(role, cols):
+        def round_wo(part, dst):
+            (b0, n0), (b1, n1) = WO_TILES[part][0], WO_TILES[part][-1]
+            round_to_bf16(
+                dst.rearrange("p (b c) t -> p b c t", b=b1 + 1 - b0),
+                wo_raw[:, b0 : b1 + 1, :, n0 * P : (n1 + 1) * P].rearrange("p b t c -> p b c t"),
+            )
+
+        def weights(role, cols, raw=False):
+            words, plane = (raw_codes[role], sc_raw[role]) if raw else (codes[role], scales[role])
             if role == "m":
-                return wm_codes[:, 2 * cols.start : 2 * cols.stop].bitcast(FP4X4), w_sc["m"][:, cols]
-            return {"p": wp_codes, "d": wd_codes}[role][:, cols].bitcast(FP8X4), w_sc[role][:, cols]
+                return words[:, 2 * cols.start : 2 * cols.stop].bitcast(FP4X4), plane[:, cols]
+            return words[:, cols].bitcast(FP8X4), plane[:, cols]
 
         banks = [psum.tile([P, PACK * CHUNK], F32, name="bank%d" % n) for n in range(BANKS)]
-        rings = {"vector": range(VECTOR_BANKS), "scalar": range(VECTOR_BANKS, BANKS), "early": range(BANKS - EARLY_BANKS, BANKS)}
-        by_age = list(range(BANKS))
+        free = list(range(EARLY_BANKS))
+        held = {}
 
-        def next_bank(ring):
-            oldest = [n for n in by_age if n in rings[ring]][0]
-            by_age.remove(oldest)
-            by_age.append(oldest)
-            return banks[oldest]
+        def take_bank(what):
+            held[what] = free.pop(0)
+            return banks[held[what]]
+
+        def give_back(what):
+            free.append(held.pop(what))
 
         starts = [sum(GROUPS[:g]) for g in range(len(GROUPS))]
-        last_group = len(GROUPS) - 1
-        magnitude, larger, device_copy, h_bf, h_codes, h_sc = {}, {}, {}, {}, {}, {}
+        units = [(g, b, c0) for g, width in enumerate(GROUPS) for b in range(PASSES) for c0 in range(0, width, CHUNK)]
+        filled = {}
 
-        def turned_product(role, unit):
-            return unit in TURNED_UNITS or (role == "m" and unit in RETURNED_UNITS)
+        def is_turned(role, u):
+            return u in TURNED or (role == "m" and u in RETURNED)
 
-        def project(role, unit, ring):
-            g, b, c0 = unit
+        def by_slot(tile):
+            return tile.rearrange("p n t -> p (n t)").rearrange("p (t q i) -> p t q i", t=PACK, i=RUN)
+
+        def project(role, u):
+            g, b, c0 = units[u]
             j = starts[g] + c0
-            bank = next_bank(ring)
-            if turned_product(role, unit):
-                cols = slice(b * PASS, (b + 1) * PASS)
-                if role == "m":
-                    codes, scales = wm_raw[:, 2 * cols.start : 2 * cols.stop].bitcast(FP4X4), sc_raw["m"][:, cols]
-                elif role == "d":
-                    codes, scales = wd_raw[:, cols].bitcast(FP8X4), sc_raw["d"][:, cols]
-                else:
-                    codes, scales = weights(role, cols)
+            bank = take_bank((role, u))
+            if is_turned(role, u):
+                words, plane = weights(role, slice(b * PASS, (b + 1) * PASS), raw=role != "p")
                 nc.tensor.matmul_mx(
                     out=bank[:],
                     lhsT=picked[role, j].bitcast(FP8X4),
                     lhsT_scale=picked_sc[role, j],
-                    rhs=codes,
-                    rhs_scale=scales,
+                    rhs=words,
+                    rhs_scale=plane,
                     start=True,
                     stop=True,
                 )
-                if role == "p":
-                    return bank[:].rearrange("p (t q i) -> p t q i", t=PACK, i=RUN)
-                return bank[:].rearrange("p (q t i) -> p t q i", t=PACK, i=RUN)
+                order = "p (t q i) -> p t q i" if role == "p" else "p (q t i) -> p t q i"
+                filled[role, u] = bank[:].rearrange(order, t=PACK, i=RUN)
+                return
             for t in range(PACK):
-                codes, scales = weights(role, slice((b * PACK + t) * P, (b * PACK + t + 1) * P))
+                words, plane = weights(role, slice((b * PACK + t) * P, (b * PACK + t + 1) * P))
                 nc.tensor.matmul_mx(
                     out=bank[:, t * CHUNK : (t + 1) * CHUNK],
-                    lhsT=codes,
-                    lhsT_scale=scales,
+                    lhsT=words,
+                    lhsT_scale=plane,
                     rhs=picked[role, j].bitcast(FP8X4),
                     rhs_scale=picked_sc[role, j],
                     start=True,
                     stop=True,
                 )
-            return bank[:].rearrange("p (t n) -> p n t", t=PACK)
+            filled[role, u] = bank[:].rearrange("p (t n) -> p n t", t=PACK)
 
-        units = [(g, b, c0) for g, width in enumerate(GROUPS) for b in range(PASSES) for c0 in range(0, width, CHUNK)]
-        steps = [[tuple(units[first:end]) for first, end in turn] for turn in MAXIMA]
-        whole = {}
-        for step in sum(steps, []):
+        steps = ((0, 2), (2, 3), (3, 4), (4, 5), (5, 6), (6, 8), (8, 10), (10, 12), (12, 14), (14, 15), (15, 16))
+        whole, value, larger = {}, {}, {}
+        for first, end in steps:
             for role in "pm":
-                whole[role, step] = sbuf("magnitude_%s%d%d%d" % (role, *step[0]), [P, len(step), CHUNK, PACK], F32)
-                for n, unit in enumerate(step):
-                    magnitude[role, unit] = whole[role, step][:, n]
+                if (role, first) == ("m", 8):
+                    continue
+                whole[role, first] = sbuf("magnitude_%s%d" % (role, first), [P, end - first, CHUNK, PACK], F32)
+                for u in range(first, end):
+                    value[role, u] = whole[role, first][:, u - first]
 
-        for unit in RETURNED_UNITS:
-            for role in "pm":
-                magnitude[role, unit] = sbuf("magnitude_%s%d%d%d" % (role, *unit), [P, CHUNK, PACK], F32)[:]
-
-        def by_slot(tile):
-            return tile.rearrange("p n t -> p (n t)").rearrange("p (t q i) -> p t q i", t=PACK, i=RUN)
-
-        def take_magnitude(role, unit, ring):
-            dst = by_slot(magnitude[role, unit]) if turned_product(role, unit) else magnitude[role, unit]
-            nc.scalar.activation(out=dst, in_=project(role, unit, ring), func=ACT.Abs)
-
-        def take_maxima(turn):
-            for step in steps[turn]:
-                dst = whole["p", step][:]
-                if turn == 0:
-                    first = sum(steps[0], ()).index(step[0])
-                    dst = first_larger[:, first : first + len(step)]
-                nc.vector.tensor_tensor(out=dst, in0=whole["p", step][:], in1=whole["m", step][:], op=ALU.max)
-                for n, unit in enumerate(step):
-                    larger[unit] = dst[:, n]
-
-        def copy_device(unit, ring):
-            tile = sbuf("device%d%d%d" % unit, [P, CHUNK, PACK], F32)
-            if unit in TURNED_UNITS:
-                nc.scalar.activation(out=by_slot(tile[:]), in_=project("d", unit, ring), func=ACT.Copy, scale=-1.0)
+        def empty(role, u):
+            if role == "d":
+                value[role, u] = sbuf("device%d" % u, [P, CHUNK, PACK], F32)[:]
+            dst = by_slot(value[role, u]) if is_turned(role, u) else value[role, u]
+            if role != "d":
+                nc.scalar.activation(out=dst, in_=filled[role, u], func=ACT.Abs)
+            elif u in TURNED:
+                nc.scalar.activation(out=dst, in_=filled[role, u], func=ACT.Copy, scale=-1.0)
             else:
-                nc.scalar.copy(out=tile[:], in_=project("d", unit, ring))
-            device_copy[unit] = tile[:]
+                nc.scalar.copy(out=dst, in_=filled[role, u])
+            give_back((role, u))
 
-        def turn_back(unit):
-            bank = next_bank("vector")
-            term = magnitude["m", unit].rearrange("p n t -> p (n t)")
+        def feed(roles, *some):
+            for u in some:
+                for role in roles:
+                    project(role, u)
+                    empty(role, u)
+
+        def transpose_sum(what, terms):
+            bank = take_bank(what)
+            flat = [term.rearrange("p n t -> p (n t)") for term in terms]
             for t in range(PACK):
                 cols = slice(t * P, (t + 1) * P)
-                nc.tensor.matmul(
-                    out=bank[:, cols], lhsT=term[:, cols], rhs=identity[:], start=True, stop=True, is_transpose=True
-                )
-            return bank[:].rearrange("p (t n) -> p n t", t=PACK)
-
-        def take_maximum_from(bank, unit, tag=None):
-            larger[unit] = sbuf("larger%d%d%d" % unit, [P, CHUNK, PACK], F32, tag)[:] if tag else magnitude["p", unit]
-            nc.vector.tensor_tensor(out=larger[unit], in0=magnitude["p", unit], in1=bank, op=ALU.max)
-
-        def h_of(unit):
-            g, b, c0 = unit
-            return h_bf[g][:, b, c0 : c0 + CHUNK, :]
-
-        def subtract_turned(unit):
-            bank = next_bank("scalar")
-            terms = [term.rearrange("p n t -> p (n t)") for term in (larger[unit], device_copy[unit])]
-            for t in range(PACK):
-                cols = slice(t * P, (t + 1) * P)
-                for n, term in enumerate(terms):
+                for n, term in enumerate(flat):
                     nc.tensor.matmul(
                         out=bank[:, cols],
                         lhsT=term[:, cols],
                         rhs=identity[:],
                         start=(n == 0),
-                        stop=(n == 1),
+                        stop=(n == len(flat) - 1),
                         is_transpose=True,
                     )
-            nc.scalar.copy(out=h_of(unit), in_=bank[:].rearrange("p (t n) -> p n t", t=PACK))
+            filled[what] = bank[:].rearrange("p (t n) -> p n t", t=PACK)
 
-        def subtract(engine, unit, cols, device):
-            engine.tensor_tensor(out=h_of(unit)[:, cols], in0=larger[unit][:, cols], in1=device, op=ALU.subtract)
+        def turn_back(*some):
+            for u in some:
+                transpose_sum(("back", u), [value["m", u]])
 
-        def quantize_h(g, which):
-            nc.vector.quantize_mx(
-                out=h_codes[g][:, which].rearrange("p b c -> p (b c)").bitcast(FP8X4),
-                scales=h_sc[g][:, which].rearrange("p b c -> p (b c)"),
-                in_=h_bf[g][:, which].rearrange("p b c j -> p (b c j)"),
+        def maximum(first, dst=None):
+            payer = whole["p", first][:]
+            dst = payer if dst is None else dst
+            if first in RETURNED:
+                nc.vector.tensor_tensor(out=dst[:, 0], in0=payer[:, 0], in1=filled["back", first], op=ALU.max)
+                give_back(("back", first))
+            else:
+                nc.vector.tensor_tensor(out=dst, in0=payer, in1=whole["m", first][:], op=ALU.max)
+            for n in range(payer.shape[1]):
+                larger[first + n] = dst[:, n]
+
+        h_bf, h_codes, h_sc = {}, {}, {}
+
+        def h_of(u):
+            g, b, c0 = units[u]
+            return h_bf[g][:, b, c0 : c0 + CHUNK, :]
+
+        def round_sum(u):
+            nc.scalar.copy(out=h_of(u), in_=filled["h", u])
+            give_back(("h", u))
+
+        def subtract(u, cols=slice(0, CHUNK)):
+            nc.vector.tensor_tensor(out=h_of(u)[:, cols], in0=larger[u][:, cols], in1=filled["d", u][:, cols], op=ALU.subtract)
+            give_back(("d", u))
+
+        def subtract_on_gpsimd(u, device, cols=slice(0, CHUNK)):
+            nc.gpsimd.tensor_tensor(out=h_of(u)[:, cols], in0=larger[u][:, cols], in1=device, op=ALU.subtract)
+
+        def quantize_h(g, which=slice(0, PASSES)):
+            quantize(
+                h_codes[g][:, which].rearrange("p b c -> p (b c)"),
+                h_sc[g][:, which].rearrange("p b c -> p (b c)"),
+                h_bf[g][:, which].rearrange("p b c j -> p (b c j)"),
+            )
+
+        wo_mx = {}
+
+        def multiply(g, b, n, dst):
+            place = sum(WO_TILES, ()).index((b, n))
+            cols = slice(place * P, (place + 1) * P)
+            nc.tensor.matmul_mx(
+                out=dst,
+                lhsT=wo_mx["codes"][:, cols].bitcast(FP8X4),
+                lhsT_scale=wo_mx["scales"][:, cols],
+                rhs=h_codes[g][:, b].bitcast(FP8X4),
+                rhs_scale=h_sc[g][:, b],
+                start=(b == 0),
+                stop=(b == PASSES - 1),
             )
 
         def decode(g, tiles):
-            add_bias(g, tiles, multiply(g, tiles))
-
-        def multiply(g, tiles):
-            width = GROUPS[g]
-            if g == last_group:
-                sums = {n: next_bank("scalar")[:, 0:width] for n in tiles}
-                order = [(n, b) for b in range(PASSES) for n in tiles]
-            else:
-                bank = next_bank("scalar")
-                sums = {n: bank[:, i * width : (i + 1) * width] for i, n in enumerate(tiles)}
-                order = [(n, b) for n in tiles for b in range(PASSES)]
-            for n, b in order:
-                place = sum(WO_TILES, ()).index((b, n))
-                cols = slice(place * P, (place + 1) * P)
-                nc.tensor.matmul_mx(
-                    out=sums[n],
-                    lhsT=wo_mx["codes"][:, cols].bitcast(FP8X4),
-                    lhsT_scale=wo_mx["scales"][:, cols],
-                    rhs=h_codes[g][:, b].bitcast(FP8X4),
-                    rhs_scale=h_sc[g][:, b],
-                    start=(b == 0),
-                    stop=(b == PASSES - 1),
-                )
-            return sums
-
-        def add_bias(g, tiles, sums):
-            width = GROUPS[g]
-            result = sbuf("result%d%d" % (g, tiles[0]), [P, len(tiles), width], F32)
-            rows = out.rearrange("(c p) j -> p c j", p=P)[:, tiles[0] : tiles[-1] + 1, starts[g] : starts[g] + width]
+            bank = take_bank(("y", g, tiles[0]))
             for i, n in enumerate(tiles):
-                if g == last_group and n == 1:
-                    nc.vector.tensor_scalar(
-                        out=result[:, i, :], in0=sums[n], scalar1=bias[:, n : n + 1], scalar2=None, op0=ALU.add
-                    )
-                else:
-                    nc.scalar.activation(out=result[:, i, :], in_=sums[n], func=ACT.Identity, bias=bias[:, n : n + 1])
-                if g == last_group:
-                    nc.sync.dma_start(out=rows[:, i, :], in_=result[:, i, :])
-            if g < last_group:
-                nc.sync.dma_start(out=rows, in_=result[:])
+                for b in range(PASSES):
+                    multiply(g, b, n, bank[:, i * GROUPS[g] : (i + 1) * GROUPS[g]])
+
+        def rows_of(g, tiles):
+            return out.rearrange("(c p) j -> p c j", p=P)[:, tiles[0] : tiles[-1] + 1, starts[g] : starts[g] + GROUPS[g]]
+
+        def add_bias(g, tiles):
+            width = GROUPS[g]
+            bank = banks[held["y", g, tiles[0]]]
+            result = sbuf("result%d%d" % (g, tiles[0]), [P, len(tiles), width], F32)
+            for i, n in enumerate(tiles):
+                nc.scalar.activation(
+                    out=result[:, i, :], in_=bank[:, i * width : (i + 1) * width], func=ACT.Identity, bias=bias[:, n : n + 1]
+                )
+            nc.sync.dma_start(out=rows_of(g, tiles), in_=result[:])
+            give_back(("y", g, tiles[0]))
+
+        def decode_and_store(g, tiles):
+            decode(g, tiles)
+            add_bias(g, tiles)
 
         nc.sync.dma_start(out=tab_sc[P - SCALE_ROWS : P, :].bitcast(I32), in_=tab_scales[0].bitcast(I32))
         nc.sync.dma_start(lists["m"][:], offs2)
@@ -361,145 +341,154 @@ def tile_list_payment_fraud_decoder_kernel(
         load_scale_rows([nc.sync, nc.sync, nc.gpsimd, nc.gpsimd], sc_raw["m"], wm_scales)
         nc.sync.dma_start(out=tab[:], in_=tab_words[0].rearrange("p n t -> p (n t)").bitcast(I32))
         make_identity(nc, identity[:], nomemset=True)
-        gather_scales("m", 0, S, early, 0)
-        carry_scales([("m", 0, S)], early, "first")
+        first = [("m", 0, S)]
+        carry_scales(first, "first", gather_scales(first, "first"))
         nc.sync.dma_start(out=wm_raw[:].bitcast(I32), in_=wm_words[0].bitcast(I32))
-        w_sc["m"] = sbuf("w_sc_m", [P, H], U8)
-        reorder(nc.scalar.copy, w_sc["m"][:], sc_raw["m"][:])
-        reorder(nc.scalar.copy, wm_codes[:], wm_raw[:])
+        reorder(scales["m"][:], sc_raw["m"][:])
+        reorder(codes["m"][:], wm_raw[:])
         load_wp(0)
         load_wp(1)
         load_scale_rows([nc.sync] * 4, sc_raw["d"], wd_scales)
         load_wp(2)
-        gather_scales("p", 0, S, later, 0)
-        gather_scales("d", 0, HALF, later, S)
-        carry_scales([("p", 0, S), ("d", 0, HALF)], later, "second")
+        second = [("p", 0, S), ("d", 0, HALF)]
+        carry_scales(second, "second", gather_scales(second, "second"))
         load_wp(3)
         nc.sync.dma_start(out=wd_raw[:], in_=wd_words[0].rearrange("p n t -> p (n t)").bitcast(I32))
         gather_words([("m", 0, QUARTER), ("m", QUARTER, HALF), ("p", 0, HALF), ("m", HALF, S)], "first")
-        last = sbuf("staged_last", [P, HALF], U8, "staged_early")
-        gather_scales("d", HALF, S, last, 0)
+        third = [("d", HALF, S)]
+        staged = gather_scales(third, "third", "staged_first")
         for n in range(PASSES * PACK):
             load_wo(*divmod(n, PACK))
-        carry_scales([("d", HALF, S)], last, "third")
+        carry_scales(third, "third", staged)
         with nc.allow_non_contiguous_dma(reason="one bias value a partition"):
             nc.sync.dma_start(out=bias[:], in_=bo.rearrange("(c p) -> p c", p=P))
-        early_units = sorted(units[:EARLY_UNITS], key=lambda unit: (unit[0], -unit[1]))
-        for unit in early_units[:4]:
-            take_magnitude("m", unit, "early")
-        for b in range(PASSES):
-            wp_bf[b] = sbuf("wp_bf%d" % b, [P, PACK, P, PACK], BF16, "wp_bf")
-            for n in range(2 * b, 2 * b + 2):
-                round_wp(n)
-            quantize_wp(b)
-            if b == 0:
-                gather_words([("d", 0, HALF), ("p", HALF, S), ("d", HALF, S)], "second", "wp_raw1")
-        for unit in early_units[4:]:
-            take_magnitude("m", unit, "early")
 
-        def own(g, among=None):
-            return [unit for unit in units if unit[0] == g and (among is None or unit in among)]
-
-        def magnitudes(roles, some):
-            return [(role, unit) for unit in some for role in roles]
-
-        def feed(items, ring="scalar"):
-            for what, unit in items:
-                if what == "d":
-                    copy_device(unit, ring)
-                elif what == "turned":
-                    subtract_turned(unit)
-                elif what == "rest":
-                    nc.scalar.copy(out=device_rest[:], in_=devices[unit][:, SHARED:CHUNK])
-                elif what == "decode":
-                    decode(*unit)
-                else:
-                    take_magnitude(what, unit, ring)
-
-        for g in range(len(GROUPS)):
+        for g, width in enumerate(GROUPS):
             if g != 1:
-                h_bf[g] = sbuf("h_bf%d" % g, [P, PASSES, GROUPS[g], PACK], BF16)
-            h_codes[g] = sbuf("h_codes%d" % g, [P, PASSES, GROUPS[g]], U32)
-            h_sc[g] = sbuf("h_sc%d" % g, [P, PASSES, GROUPS[g]], U8)
-        turned = [[("d", unit), ("turned", unit)] for unit in TURNED_UNITS]
-        devices = {}
-        device_rest = sbuf("device_rest", [P, CHUNK - SHARED, PACK], F32)
-        first_larger = sbuf("first_larger", [P, len(sum(steps[0], ())), CHUNK, PACK], F32, "wp_raw3")
-        w_sc["d"] = sbuf("w_sc_d", [P, H], U8)
-        reorder(nc.scalar.copy, w_sc["d"][:], sc_raw["d"][:])
-        feed(magnitudes("p", own(0)[:2] + own(1)[:2]) + magnitudes("m", own(2)[:1]), "early")
-        ahead = project("m", own(2)[1], "early")
-        backs = [turn_back(unit) for unit in own(0)[2:]]
-        reorder(nc.scalar.copy, wd_codes[:], wd_raw[:])
-        feed(magnitudes("p", own(0)[2:]))
-        devices[units[0]] = project("d", units[0], "vector")
-        nc.scalar.activation(out=magnitude["m", own(2)[1]], in_=ahead, func=ACT.Abs)
-        feed(magnitudes("p", own(1)[2:]))
+                h_bf[g] = sbuf("h_bf%d" % g, [P, PASSES, width, PACK], BF16)
+            h_codes[g] = sbuf("h_codes%d" % g, [P, PASSES, width], U32)
+            h_sc[g] = sbuf("h_sc%d" % g, [P, PASSES, width], U8)
+
+        feed("m", 0, 2, 3, 1)
+        quantize_wp(0)
+        gather_words([("d", 0, HALF), ("p", HALF, S), ("d", HALF, S)], "second", "wp_raw1")
+        quantize_wp(1)
+        feed("m", 5, 4, 6, 7)
+        reorder(scales["d"][:], sc_raw["d"][:])
+        spare = list(range(EARLY_BANKS, BANKS))
+        ring = list(free)
+        free[:] = spare[:3]
+        turn_back(5, 2, 3)
+        free[:] = ring
+        feed("p", 0, 1, 4, 5)
+        feed("d", 0)
+        project("m", 8)
+        project("m", 9)
+        free.insert(0, spare[3])
+        reorder(codes["d"][:], wd_raw[:])
+
+        first_larger = sbuf("first_larger", [P, 3, CHUNK, PACK], F32, "wp_raw3")
+        maximum(0, first_larger[:, 0:2])
+        maximum(4, first_larger[:, 2:3])
+        wo_pair = sbuf("wo_pair", [P, 2, WO_PART, PACK], BF16, "magnitude_m0")
+        for part in range(2):
+            round_wo(part, wo_pair[:, part])
+        whole["m", 8] = sbuf("magnitude_m8", [P, 2, CHUNK, PACK], F32, "wp_bf")
+        value["m", 8], value["m", 9] = whole["m", 8][:, 0], whole["m", 8][:, 1]
+        project("p", 2)
+        project("p", 3)
+        transpose_sum(("h", 0), [larger[0], value["d", 0]])
+        for u, tag, role, emptied in ((5, "magnitude_p0", "p", 2), (2, "magnitude_p4", "p", 3), (3, "magnitude_p5", "m", 8)):
+            empty(role, emptied)
+            maximum(u, sbuf("larger%d" % u, [P, 1, CHUNK, PACK], F32, tag)[:])
+        round_sum(0)
+        for role, u in (("d", 1), ("p", 6), ("d", 2), ("p", 7), ("d", 3), ("d", 4), ("p", 8)):
+            project(role, u)
+        for u, emptied in ((1, [("p", 6)]), (2, [("p", 7)]), (3, [("m", 9), ("d", 4), ("p", 8)])):
+            subtract(u)
+            for role, other in emptied:
+                empty(role, other)
+        for role, u in (("p", 9), ("m", 10), ("d", 5), ("p", 10), ("d", 6), ("m", 11), ("d", 7), ("p", 11)):
+            project(role, u)
+        for role, u in (("p", 9), ("m", 10), ("p", 10), ("m", 11), ("p", 11)):
+            empty(role, u)
+
+        maximum(6)
+        wo_mx["codes"] = sbuf("wo_codes", [P, PASSES * N], U32, "magnitude_p4")
         wo_mx["scales"] = sbuf("wo_sc", [P, PASSES * N], U8)
+        pair = slice(0, 2 * WO_PART)
+        quantize(wo_mx["codes"][:, pair], wo_mx["scales"][:, pair], wo_pair[:].rearrange("p a c j -> p (a c j)"))
+        h_bf[1] = sbuf("h_bf1", [P, PASSES, GROUPS[1], PACK], BF16, "magnitude_m0")
+        quantize_h(0)
+        subtract_on_gpsimd(4, value["d", 4])
+        feed("d", 8)
+        decode_and_store(0, [0, 1])
+        for u in (5, 6, 7):
+            subtract(u)
 
-        take_maxima(0)
-        for part, tag in enumerate(("magnitude_m000", "magnitude_m100")):
-            round_wo(round_on_gpsimd, part, sbuf("wo_bf%d" % part, [P, WO_PART, PACK], BF16, tag)[:])
-        for bank, unit, tag, copied in zip(backs, own(0)[2:], ("magnitude_p000", "magnitude_p100"), GPSIMD_UNITS):
-            take_maximum_from(bank, unit, tag)
-            devices[units[len(devices)]] = project("d", units[len(devices)], "vector")
-            feed([("d", copied)])
-        subtract(nc.vector, units[0], slice(0, CHUNK), devices[units[0]])
-        devices[units[3]] = project("d", units[3], "vector")
-        feed(magnitudes("m", own(2)[2:3]) + magnitudes("p", own(2)[:2]))
-        for unit in own(0)[1:]:
-            subtract(nc.vector, unit, slice(0, CHUNK), devices[unit])
+        maximum(8)
+        maximum(10)
+        quantize_h(1)
+        wo_last = sbuf("wo_last", [P, WO_PART, PACK], BF16, "magnitude_m10")
+        round_wo(2, wo_last[:])
+        feed("mp", 12)
+        feed("m", 13)
+        for u in (9, 10, 11):
+            project("d", u)
+        feed("p", 13)
+        transpose_sum(("h", 8), [larger[8], value["d", 8]])
+        round_sum(8)
+        for role, u in (("d", 12), ("m", 14), ("m", 15)):
+            project(role, u)
+        subtract(9)
+        decode(1, [0, 1])
+        subtract(10)
+        subtract(11)
+        for role, u in (("p", 14), ("p", 15), ("d", 13)):
+            project(role, u)
+        empty("d", 12)
+        project("d", 15)
+        empty("m", 14)
+        empty("m", 15)
 
-        backs = [turn_back(unit) for unit in own(1)[2:]]
-        wo_mx["codes"] = sbuf("wo_codes", [P, PASSES * N], U32, "magnitude_p000")
-        quantize_wo([0])
-        quantize_h(0, slice(0, PASSES))
-        h_bf[1] = sbuf("h_bf1", [P, PASSES, GROUPS[1], PACK], BF16, "h_bf0")
-        quantize_wo([1])
-        for unit in GPSIMD_UNITS:
-            subtract(nc.gpsimd, unit, slice(0, CHUNK), device_copy[unit])
-        feed(magnitudes("p", own(2)[2:3]))
-        devices[units[6]] = project("d", units[6], "vector")
-        feed(magnitudes("mp", own(2)[3:]))
-        for bank, unit in zip(backs, own(1)[2:]):
-            take_maximum_from(bank, unit)
-        devices[units[7]] = project("d", units[7], "vector")
-        feed(turned[0][:1] + [("decode", (0, [0, 1]))])
-        for unit in own(1)[2:]:
-            subtract(nc.vector, unit, slice(0, CHUNK), devices[unit])
+        last = slice(2 * WO_PART, 3 * WO_PART)
+        quantize(wo_mx["codes"][:, last], wo_mx["scales"][:, last], wo_last[:].rearrange("p c j -> p (c j)"))
+        maximum(12)
+        quantize_h(2)
+        subtract_on_gpsimd(12, value["d", 12])
+        turn_back(14, 15)
+        empty("p", 14)
+        project("d", 14)
+        empty("p", 15)
+        subtract(13)
+        add_bias(1, [0, 1])
+        device_rest = sbuf("device_rest", [P, CHUNK - VECTOR_SHARE, PACK], F32)
+        nc.scalar.copy(out=device_rest[:], in_=filled["d", 15][:, VECTOR_SHARE:CHUNK])
+        decode_and_store(0, [2])
+        decode_and_store(1, [2])
+        decode_and_store(2, [0, 1])
+        maximum(14)
+        maximum(15)
+        decode_and_store(2, [2])
+        quantize_h(3)
+        decode_and_store(3, range(N_TILES))
+        subtract(14)
+        subtract(15, slice(0, VECTOR_SHARE))
+        subtract_on_gpsimd(15, device_rest[:], slice(VECTOR_SHARE, CHUNK))
 
-        take_maxima(2)
-        quantize_h(1, slice(0, PASSES))
-        round_wo(round_on_gpsimd, 2, sbuf("wo_last", [P, WO_PART, PACK], BF16, "magnitude_m210")[:])
-        feed(magnitudes("mp", own(3)[:1]) + magnitudes("m", own(3)[1:]))
-        for unit in own(2)[1:]:
-            devices[unit] = project("d", unit, "vector")
-        feed(magnitudes("p", own(3)[1:]) + turned[0][1:] + [("d", units[12])] + magnitudes("m", own(4)) + [("decode", (1, [0, 1]))])
-        for unit in own(2)[1:]:
-            subtract(nc.vector, unit, slice(0, CHUNK), devices[unit])
-
-        quantize_wo([2])
-        take_maxima(3)
-        quantize_h(2, slice(0, PASSES))
-        subtract(nc.gpsimd, units[12], slice(0, CHUNK), device_copy[units[12]])
-        devices[units[13]] = project("d", units[13], "vector")
-        feed(magnitudes("p", own(4)[:1]))
-        backs = [turn_back(unit) for unit in own(4)]
-        feed(magnitudes("p", own(4)[1:]) + [("decode", (0, [2])), ("decode", (1, [2]))])
-        sums = multiply(2, [0, 1])
-        subtract(nc.vector, units[13], slice(0, CHUNK), devices[units[13]])
-        devices[units[15]] = project("d", units[15], "vector")
-        feed([("rest", units[15])])
-        add_bias(2, [0, 1], sums)
-        take_maximum_from(backs[0], units[14])
-        devices[units[14]] = project("d", units[14], "vector")
-        feed([("decode", (2, [2]))])
-        take_maximum_from(backs[1], units[15])
-        quantize_h(3, slice(0, PASSES))
-        feed([("decode", (3, range(N_TILES)))])
-        subtract(nc.vector, units[14], slice(0, CHUNK), devices[units[14]])
-        subtract(nc.vector, units[15], slice(0, SHARED), devices[units[15]][:, 0:SHARED])
-        subtract(nc.gpsimd, units[15], slice(SHARED, CHUNK), device_rest[:])
+        g = len(GROUPS) - 1
+        sums = [take_bank(("y", g, n))[:, 0 : GROUPS[g]] for n in range(N_TILES)]
         for b in range(PASSES):
-            quantize_h(last_group, slice(b, b + 1))
-        decode(last_group, range(N_TILES))
+            quantize_h(g, slice(b, b + 1))
+        for b in range(PASSES):
+            for n in range(N_TILES):
+                multiply(g, b, n, sums[n])
+        result = sbuf("result_last", [P, N_TILES, GROUPS[g]], F32)
+        for n in range(N_TILES):
+            if n == 1:
+                nc.vector.tensor_scalar(
+                    out=result[:, n, :], in0=sums[n], scalar1=bias[:, n : n + 1], scalar2=None, op0=ALU.add
+                )
+            else:
+                nc.scalar.activation(out=result[:, n, :], in_=sums[n], func=ACT.Identity, bias=bias[:, n : n + 1])
+            nc.sync.dma_start(out=rows_of(g, range(N_TILES))[:, n, :], in_=result[:, n, :])

@@ -35,7 +35,7 @@ WO_TILES = (((0, 0), (0, 1)), ((1, 0), (1, 1)), ((0, 2), (1, 2)))
 WO_PART = PASSES * N // len(WO_TILES)
 TURNED = (0, 8)
 RETURNED = (2, 3, 5, 14, 15)
-VECTOR_SHARE = 64
+VECTOR_SHARE = 72
 BANKS = 8
 EARLY_BANKS = 4
 
@@ -275,7 +275,7 @@ def tile_list_payment_fraud_decoder_kernel(
 
         def h_of(u):
             g, b, c0 = units[u]
-            return h_bf[g][:, b, c0 : c0 + CHUNK, :]
+            return h_bf[g, b][:] if (g, b) in h_bf else h_bf[g][:, b, c0 : c0 + CHUNK, :]
 
         def round_sum(u):
             nc.scalar.copy(out=h_of(u), in_=filled["h", u])
@@ -327,7 +327,10 @@ def tile_list_payment_fraud_decoder_kernel(
                 nc.scalar.activation(
                     out=result[:, i, :], in_=bank[:, i * width : (i + 1) * width], func=ACT.Identity, bias=bias[:, n : n + 1]
                 )
-            nc.sync.dma_start(out=rows_of(g, tiles), in_=result[:])
+                if g == 2:
+                    nc.sync.dma_start(out=rows_of(g, tiles)[:, i, :], in_=result[:, i, :])
+            if g != 2:
+                nc.sync.dma_start(out=rows_of(g, tiles), in_=result[:])
             give_back(("y", g, tiles[0]))
 
         def decode_and_store(g, tiles):
@@ -364,9 +367,10 @@ def tile_list_payment_fraud_decoder_kernel(
             nc.sync.dma_start(out=bias[:], in_=bo.rearrange("(c p) -> p c", p=P))
 
         for g, width in enumerate(GROUPS):
-            if g != 1:
+            if g in (0, 2):
                 h_bf[g] = sbuf("h_bf%d" % g, [P, PASSES, width, PACK], BF16)
-            h_codes[g] = sbuf("h_codes%d" % g, [P, PASSES, width], U32)
+            if g != 3:
+                h_codes[g] = sbuf("h_codes%d" % g, [P, PASSES, width], U32)
             h_sc[g] = sbuf("h_sc%d" % g, [P, PASSES, width], U8)
 
         feed("m", 0, 2, 3, 1)
@@ -410,8 +414,8 @@ def tile_list_payment_fraud_decoder_kernel(
                 empty(role, other)
         for role, u in (("p", 9), ("m", 10), ("d", 5), ("p", 10), ("d", 6), ("m", 11), ("d", 7), ("p", 11)):
             project(role, u)
-        for role, u in (("p", 9), ("m", 10), ("p", 10), ("m", 11), ("p", 11)):
-            empty(role, u)
+        empty("p", 9)
+        empty("m", 10)
 
         maximum(6)
         wo_mx["codes"] = sbuf("wo_codes", [P, PASSES * N], U32, "magnitude_p4")
@@ -421,56 +425,69 @@ def tile_list_payment_fraud_decoder_kernel(
         h_bf[1] = sbuf("h_bf1", [P, PASSES, GROUPS[1], PACK], BF16, "magnitude_m0")
         quantize_h(0)
         subtract_on_gpsimd(4, value["d", 4])
-        feed("d", 8)
-        decode_and_store(0, [0, 1])
-        for u in (5, 6, 7):
+        project("d", 8)
+        decode(0, [0, 1])
+        for u, emptied, following in ((5, ("p", 10), ("m", 12)), (6, ("m", 11), ("p", 12)), (7, ("p", 11), ("m", 13))):
             subtract(u)
+            empty(*emptied)
+            project("d", u + 4)
+            project(*following)
+        empty("d", 8)
+        add_bias(0, [0, 1])
+        project("p", 13)
 
         maximum(8)
         maximum(10)
         quantize_h(1)
         wo_last = sbuf("wo_last", [P, WO_PART, PACK], BF16, "magnitude_m10")
         round_wo(2, wo_last[:])
-        feed("mp", 12)
-        feed("m", 13)
-        for u in (9, 10, 11):
-            project("d", u)
-        feed("p", 13)
         transpose_sum(("h", 8), [larger[8], value["d", 8]])
-        round_sum(8)
-        for role, u in (("d", 12), ("m", 14), ("m", 15)):
-            project(role, u)
+        for emptied, following in ((("m", 12), ("d", 12)), (("p", 12), ("m", 14)), (("m", 13), ("m", 15))):
+            empty(*emptied)
+            project(*following)
         subtract(9)
         decode(1, [0, 1])
+        empty("p", 13)
         subtract(10)
+        round_sum(8)
         subtract(11)
-        for role, u in (("p", 14), ("p", 15), ("d", 13)):
-            project(role, u)
         empty("d", 12)
-        project("d", 15)
+        for role, u in (("p", 14), ("p", 15), ("d", 13), ("d", 15), ("d", 14)):
+            project(role, u)
         empty("m", 14)
         empty("m", 15)
 
+        maximum(12)
         last = slice(2 * WO_PART, 3 * WO_PART)
         quantize(wo_mx["codes"][:, last], wo_mx["scales"][:, last], wo_last[:].rearrange("p c j -> p (c j)"))
-        maximum(12)
+        h_bf[3, 0] = sbuf("h_bf30", [P, CHUNK, PACK], BF16, "magnitude_m10")
+        h_bf[3, 1] = sbuf("h_bf31", [P, CHUNK, PACK], BF16)
         quantize_h(2)
         subtract_on_gpsimd(12, value["d", 12])
         turn_back(14, 15)
         empty("p", 14)
-        project("d", 14)
         empty("p", 15)
         subtract(13)
         add_bias(1, [0, 1])
         device_rest = sbuf("device_rest", [P, CHUNK - VECTOR_SHARE, PACK], F32)
         nc.scalar.copy(out=device_rest[:], in_=filled["d", 15][:, VECTOR_SHARE:CHUNK])
-        decode_and_store(0, [2])
-        decode_and_store(1, [2])
+        n = N_TILES - 1
+        bank = take_bank("third rows")
+        for g in range(2):
+            for b in range(PASSES):
+                multiply(g, b, n, bank[:, starts[g] : starts[g + 1]])
+        result = sbuf("result_third_rows", [P, HALF], F32)
+        nc.scalar.activation(out=result[:], in_=bank[:], func=ACT.Identity, bias=bias[:, n : n + 1])
+        nc.sync.dma_start(out=out[n * P : (n + 1) * P, 0:HALF], in_=result[:])
+        give_back("third rows")
         decode_and_store(2, [0, 1])
-        maximum(14)
+        maximum(14, sbuf("larger14", [P, 1, CHUNK, PACK], F32)[:])
+        h_codes[3] = sbuf("h_codes3", [P, PASSES, GROUPS[3]], U32, "magnitude_p14")
         maximum(15)
         decode_and_store(2, [2])
-        quantize_h(3)
+        for b in range(PASSES):
+            quantize(h_codes[3][:, b], h_sc[3][:, b], h_bf[3, b][:].rearrange("p c j -> p (c j)"))
+        h_bf[4] = sbuf("h_bf4", [P, PASSES, GROUPS[4], PACK], BF16, "magnitude_m10")
         decode_and_store(3, range(N_TILES))
         subtract(14)
         subtract(15, slice(0, VECTOR_SHARE))

@@ -337,7 +337,7 @@ def tile_list_payment_fraud_decoder_kernel(
             decode(g, tiles)
             add_bias(g, tiles)
 
-        nc.sync.dma_start(out=tab_sc[P - SCALE_ROWS : P, :].bitcast(I32), in_=tab_scales[0].bitcast(I32))
+        nc.scalar.dma_start(out=tab_sc[P - SCALE_ROWS : P, :].bitcast(I32), in_=tab_scales[0].bitcast(I32))
         nc.sync.dma_start(lists["m"][:], offs2)
         nc.sync.dma_start(lists["p"][:], offs)
         nc.sync.dma_start(lists["d"][:], offs3)
@@ -357,7 +357,7 @@ def tile_list_payment_fraud_decoder_kernel(
         carry_scales(second, "second", gather_scales(second, "second"))
         load_wp(3)
         nc.sync.dma_start(out=wd_raw[:], in_=wd_words[0].rearrange("p n t -> p (n t)").bitcast(I32))
-        gather_words([("m", 0, QUARTER), ("m", QUARTER, HALF), ("p", 0, HALF), ("m", HALF, S)], "first")
+        gather_words([("m", 0, QUARTER), ("m", QUARTER, S), ("p", 0, HALF)], "first")
         third = [("d", HALF, S)]
         staged = gather_scales(third, "third", "staged_first")
         for n in range(PASSES * PACK):
@@ -375,7 +375,7 @@ def tile_list_payment_fraud_decoder_kernel(
 
         feed("m", 0, 2, 3, 1)
         quantize_wp(0)
-        gather_words([("d", 0, HALF), ("p", HALF, S), ("d", HALF, S)], "second", "wp_raw1")
+        gather_words([("d", 0, S), ("p", HALF, S)], "second", "wp_raw1")
         quantize_wp(1)
         feed("m", 5, 4, 6, 7)
         reorder(scales["d"][:], sc_raw["d"][:])

from contextlib import ExitStack

import concourse.mybir as mybir
from concourse.masks import make_identity

K, H, N, T, S = 512, 1024, 384, 4096, 1024
FLOPS = 2 * S * (3 * K * H + H * N)

F32 = mybir.dt.float32
BF16 = mybir.dt.bfloat16
I32 = mybir.dt.int32
U32 = mybir.dt.uint32
U16 = mybir.dt.uint16
U8 = mybir.dt.uint8
FP8X4 = mybir.dt.float8_e4m3fn_x4
FP4X4 = mybir.dt.float4_e2m1fn_x4
ALU = mybir.AluOpType
ACT = mybir.ActivationFunctionType

P = 128
PACK = 4
PASS = P * PACK
PASSES = H // PASS
RUN = 8
QUADRANT = 32
SCALE_ROWS = 16
LIST_ROWS = 16
HALF = S // 2
QUARTER = S // 4
CHUNK = 128
N_TILES = N // P
GROUPS = (256, 256, 256, 128, 128)
WP_LOADS = 4
WO_TILES = (((0, 0), (0, 1)), ((1, 0), (1, 1)), ((0, 2), (1, 2)))
WO_PART = PASSES * N // len(WO_TILES)
TURNED = (0, 8)
RETURNED = (2, 3, 5, 14, 15)
VECTOR_SHARE = 72
BANKS = 8
EARLY_BANKS = 4


def tile_list_payment_fraud_decoder_kernel(
    tc, tab_words, tab_scales, offs, offs2, offs3, wp, wm_words, wm_scales, wd_words, wd_scales, wo, bo, out
):
    nc = tc.nc
    with ExitStack() as ctx:
        keep = ctx.enter_context(tc.tile_pool(name="keep", bufs=1))
        psum = ctx.enter_context(tc.psum_pool(name="psum", bufs=1))

        def sbuf(name, shape, dtype, tag=None):
            return keep.tile(shape, dtype, align_bytes=64, name=name, tag=tag or name)

        lists = {role: keep.tile([P, S // LIST_ROWS], U16, name="list_" + role) for role in "pmd"}
        tab_sc = sbuf("tab_sc", [P, T], U8)
        tab = sbuf("tab", [P, T], I32)
        wp_raw = [sbuf("wp_raw%d" % n, [P, PACK, H // WP_LOADS], F32) for n in range(WP_LOADS)]
        wm_raw = sbuf("wm_raw", [P, 2 * H], U8)
        wd_raw = sbuf("wd_raw", [P, H], I32)
        sc_raw = {role: sbuf("sc_raw_" + role, [P, H], U8) for role in "md"}
        wo_raw = sbuf("wo_raw", [P, PASSES, PACK, N], F32)
        bias = sbuf("bias", [P, N_TILES], F32)
        identity = sbuf("identity", [P, P], F32)

        for role in "md":
            nc.vector.memset(sc_raw[role][:].bitcast(I32), 0)
        nc.vector.memset(tab_sc[0 : P - SCALE_ROWS, :].bitcast(I32), 0)
        nc.vector.memset(identity[:], 0.0)

        def load_scale_rows(queues, dst, src):
            rows = src[0].rearrange("(q r) n -> r q n", r=4)
            for r, queue in enumerate(queues):
                queue.dma_start(out=dst[r:P:QUADRANT, :].bitcast(I32), in_=rows[r].bitcast(I32))

        def load_wp(n):
            rows = wp.rearrange("(p j) (n c) -> n p j c", j=PACK, n=WP_LOADS)
            nc.sync.dma_start(out=wp_raw[n][:], in_=rows[n])

        def load_wo(b, t):
            rows = wo.rearrange("(b q t i) n -> b t q i n", b=PASSES, t=PACK, i=RUN)
            nc.sync.dma_start(out=wo_raw[:, b, t, :], in_=rows[b, t])

        picked, picked_sc = {}, {}

        def offsets(role, j0, j1):
            return lists[role][:, j0 // LIST_ROWS : j1 // LIST_ROWS]

        def by_chunk(into, tile, pieces):
            c0 = 0
            for role, j0, j1 in pieces:
                for j in range(j0, j1, CHUNK):
                    into[role, j] = tile[:, c0 + j - j0 : c0 + j - j0 + CHUNK]
                c0 = c0 + j1 - j0

        def gather(dst, window, pieces):
            c0 = 0
            for role, j0, j1 in pieces:
                nc.vector.tensor_copy(dst[:, c0 : c0 + j1 - j0], window.indirect(offsets(role, j0, j1)))
                c0 = c0 + j1 - j0

        def width_of(pieces):
            return sum(j1 - j0 for role, j0, j1 in pieces)

        def gather_scales(pieces, name, tag=None):
            staged = sbuf("staged_" + name, [P, width_of(pieces)], U8, tag)
            gather(staged, tab_sc[:], pieces)
            return staged

        def carry_scales(pieces, name, staged):
            plane = sbuf("plane_" + name, [P, width_of(pieces)], U8)
            for r in range(4):
                nc.sync.dma_start(
                    out=plane[r:P:QUADRANT, :].bitcast(I32),
                    in_=staged[P - SCALE_ROWS + r : P : 4, :].bitcast(I32),
                )
            by_chunk(picked_sc, plane, pieces)

        def gather_words(pieces, name, tag=None):
            words = sbuf("picked_" + name, [P, width_of(pieces)], U32, tag)
            gather(words, tab[:].bitcast(U32), pieces)
            by_chunk(picked, words, pieces)

        def reorder(dst, src):
            nc.scalar.copy(
                out=dst.bitcast(U32).rearrange("p (b t q i) -> p b t q i", b=PASSES, t=PACK, q=P // RUN),
                in_=src.bitcast(U32).rearrange("p (b q t i) -> p b t q i", b=PASSES, t=PACK, q=P // RUN),
            )

        codes = {"p": sbuf("wp_codes", [P, H], U32), "m": sbuf("wm_codes", [P, 2 * H], U8), "d": sbuf("wd_codes", [P, H], U32)}
        scales = {role: sbuf("w_sc_" + role, [P, H], U8) for role in "pmd"}
        raw_codes = {"m": wm_raw, "d": wd_raw}

        def round_to_bf16(dst, src):
            nc.gpsimd.tensor_scalar(out=dst, in0=src, scalar1=1.0, scalar2=0.0, op0=ALU.mult, op1=ALU.add)

        def quantize(dst_codes, dst_scales, src):
            nc.vector.quantize_mx(out=dst_codes.bitcast(FP8X4), scales=dst_scales, in_=src)

        def quantize_wp(b):
            rounded = sbuf("wp_bf%d" % b, [P, PACK, P, PACK], BF16, "wp_bf")
            width = P * PASSES // WP_LOADS
            for share in range(WP_LOADS // PASSES):
                round_to_bf16(
                    rounded[:, :, share * width : (share + 1) * width].rearrange("p t (q i) j -> p q t i j", i=RUN),
                    wp_raw[b * WP_LOADS // PASSES + share][:].rearrange("p j (q t i) -> p q t i j", t=PACK, i=RUN),
                )
            cols = slice(b * PASS, (b + 1) * PASS)
            quantize(codes["p"][:, cols], scales["p"][:, cols], rounded[:].rearrange("p t c j -> p (t c j)"))

        def round_wo(part, dst):
            (b0, n0), (b1, n1) = WO_TILES[part][0], WO_TILES[part][-1]
            round_to_bf16(
                dst.rearrange("p (b c) t -> p b c t", b=b1 + 1 - b0),
                wo_raw[:, b0 : b1 + 1, :, n0 * P : (n1 + 1) * P].rearrange("p b t c -> p b c t"),
            )

        def weights(role, cols, raw=False):
            words, plane = (raw_codes[role], sc_raw[role]) if raw else (codes[role], scales[role])
            if role == "m":
                return words[:, 2 * cols.start : 2 * cols.stop].bitcast(FP4X4), plane[:, cols]
            return words[:, cols].bitcast(FP8X4), plane[:, cols]

        banks = [psum.tile([P, PACK * CHUNK], F32, name="bank%d" % n) for n in range(BANKS)]
        free = list(range(EARLY_BANKS))
        held = {}

        def take_bank(what):
            held[what] = free.pop(0)
            return banks[held[what]]

        def give_back(what):
            free.append(held.pop(what))

        starts = [sum(GROUPS[:g]) for g in range(len(GROUPS))]
        units = [(g, b, c0) for g, width in enumerate(GROUPS) for b in range(PASSES) for c0 in range(0, width, CHUNK)]
        filled = {}

        def is_turned(role, u):
            return u in TURNED or (role == "m" and u in RETURNED)

        def by_slot(tile):
            return tile.rearrange("p n t -> p (n t)").rearrange("p (t q i) -> p t q i", t=PACK, i=RUN)

        def project(role, u):
            g, b, c0 = units[u]
            j = starts[g] + c0
            bank = take_bank((role, u))
            if is_turned(role, u):
                words, plane = weights(role, slice(b * PASS, (b + 1) * PASS), raw=role != "p")
                nc.tensor.matmul_mx(
                    out=bank[:],
                    lhsT=picked[role, j].bitcast(FP8X4),
                    lhsT_scale=picked_sc[role, j],
                    rhs=words,
                    rhs_scale=plane,
                    start=True,
                    stop=True,
                )
                order = "p (t q i) -> p t q i" if role == "p" else "p (q t i) -> p t q i"
                filled[role, u] = bank[:].rearrange(order, t=PACK, i=RUN)
                return
            for t in range(PACK):
                words, plane = weights(role, slice((b * PACK + t) * P, (b * PACK + t + 1) * P))
                nc.tensor.matmul_mx(
                    out=bank[:, t * CHUNK : (t + 1) * CHUNK],
                    lhsT=words,
                    lhsT_scale=plane,
                    rhs=picked[role, j].bitcast(FP8X4),
                    rhs_scale=picked_sc[role, j],
                    start=True,
                    stop=True,
                )
            filled[role, u] = bank[:].rearrange("p (t n) -> p n t", t=PACK)

        steps = ((0, 2), (2, 3), (3, 4), (4, 5), (5, 6), (6, 8), (8, 10), (10, 12), (12, 14), (14, 15), (15, 16))
        whole, value, larger = {}, {}, {}
        for first, end in steps:
            for role in "pm":
                if (role, first) == ("m", 8):
                    continue
                whole[role, first] = sbuf("magnitude_%s%d" % (role, first), [P, end - first, CHUNK, PACK], F32)
                for u in range(first, end):
                    value[role, u] = whole[role, first][:, u - first]

        def empty(role, u):
            if role == "d":
                value[role, u] = sbuf("device%d" % u, [P, CHUNK, PACK], F32)[:]
            dst = by_slot(value[role, u]) if is_turned(role, u) else value[role, u]
            if role != "d":
                nc.scalar.activation(out=dst, in_=filled[role, u], func=ACT.Abs)
            elif u in TURNED:
                nc.scalar.activation(out=dst, in_=filled[role, u], func=ACT.Copy, scale=-1.0)
            else:
                nc.scalar.copy(out=dst, in_=filled[role, u])
            give_back((role, u))

        def feed(roles, *some):
            for u in some:
                for role in roles:
                    project(role, u)
                    empty(role, u)

        def transpose_sum(what, terms):
            bank = take_bank(what)
            flat = [term.rearrange("p n t -> p (n t)") for term in terms]
            for t in range(PACK):
                cols = slice(t * P, (t + 1) * P)
                for n, term in enumerate(flat):
                    nc.tensor.matmul(
                        out=bank[:, cols],
                        lhsT=term[:, cols],
                        rhs=identity[:],
                        start=(n == 0),
                        stop=(n == len(flat) - 1),
                        is_transpose=True,
                    )
            filled[what] = bank[:].rearrange("p (t n) -> p n t", t=PACK)

        def turn_back(*some):
            for u in some:
                transpose_sum(("back", u), [value["m", u]])

        def maximum(first, dst=None):
            payer = whole["p", first][:]
            dst = payer if dst is None else dst
            if first in RETURNED:
                nc.vector.tensor_tensor(out=dst[:, 0], in0=payer[:, 0], in1=filled["back", first], op=ALU.max)
                give_back(("back", first))
            else:
                nc.vector.tensor_tensor(out=dst, in0=payer, in1=whole["m", first][:], op=ALU.max)
            for n in range(payer.shape[1]):
                larger[first + n] = dst[:, n]

        h_bf, h_codes, h_sc = {}, {}, {}

        def h_of(u):
            g, b, c0 = units[u]
            return h_bf[g, b][:] if (g, b) in h_bf else h_bf[g][:, b, c0 : c0 + CHUNK, :]

        def round_sum(u):
            nc.scalar.copy(out=h_of(u), in_=filled["h", u])
            give_back(("h", u))

        def subtract(u, cols=slice(0, CHUNK)):
            nc.vector.tensor_tensor(out=h_of(u)[:, cols], in0=larger[u][:, cols], in1=filled["d", u][:, cols], op=ALU.subtract)
            give_back(("d", u))

        def subtract_on_gpsimd(u, device, cols=slice(0, CHUNK)):
            nc.gpsimd.tensor_tensor(out=h_of(u)[:, cols], in0=larger[u][:, cols], in1=device, op=ALU.subtract)

        def quantize_h(g, which=slice(0, PASSES)):
            quantize(
                h_codes[g][:, which].rearrange("p b c -> p (b c)"),
                h_sc[g][:, which].rearrange("p b c -> p (b c)"),
                h_bf[g][:, which].rearrange("p b c j -> p (b c j)"),
            )

        wo_mx = {}

        def multiply(g, b, n, dst):
            place = sum(WO_TILES, ()).index((b, n))
            cols = slice(place * P, (place + 1) * P)
            nc.tensor.matmul_mx(
                out=dst,
                lhsT=wo_mx["codes"][:, cols].bitcast(FP8X4),
                lhsT_scale=wo_mx["scales"][:, cols],
                rhs=h_codes[g][:, b].bitcast(FP8X4),
                rhs_scale=h_sc[g][:, b],
                start=(b == 0),
                stop=(b == PASSES - 1),
            )

        def decode(g, tiles):
            bank = take_bank(("y", g, tiles[0]))
            for i, n in enumerate(tiles):
                for b in range(PASSES):
                    multiply(g, b, n, bank[:, i * GROUPS[g] : (i + 1) * GROUPS[g]])

        def rows_of(g, tiles):
            return out.rearrange("(c p) j -> p c j", p=P)[:, tiles[0] : tiles[-1] + 1, starts[g] : starts[g] + GROUPS[g]]

        def add_bias(g, tiles):
            width = GROUPS[g]
            bank = banks[held["y", g, tiles[0]]]
            result = sbuf("result%d%d" % (g, tiles[0]), [P, len(tiles), width], F32)
            for i, n in enumerate(tiles):
                nc.scalar.activation(
                    out=result[:, i, :], in_=bank[:, i * width : (i + 1) * width], func=ACT.Identity, bias=bias[:, n : n + 1]
                )
                if g == 2:
                    nc.sync.dma_start(out=rows_of(g, tiles)[:, i, :], in_=result[:, i, :])
            if g != 2:
                nc.sync.dma_start(out=rows_of(g, tiles), in_=result[:])
            give_back(("y", g, tiles[0]))

        def decode_and_store(g, tiles):
            decode(g, tiles)
            add_bias(g, tiles)

        nc.scalar.dma_start(out=tab_sc[P - SCALE_ROWS : P, :].bitcast(I32), in_=tab_scales[0].bitcast(I32))
        nc.sync.dma_start(lists["m"][:], offs2)
        nc.sync.dma_start(lists["p"][:], offs)
        nc.sync.dma_start(lists["d"][:], offs3)
        load_scale_rows([nc.sync, nc.sync, nc.gpsimd, nc.gpsimd], sc_raw["m"], wm_scales)
        nc.sync.dma_start(out=tab[:], in_=tab_words[0].rearrange("p n t -> p (n t)").bitcast(I32))
        make_identity(nc, identity[:], nomemset=True)
        first = [("m", 0, S)]
        carry_scales(first, "first", gather_scales(first, "first"))
        nc.sync.dma_start(out=wm_raw[:].bitcast(I32), in_=wm_words[0].bitcast(I32))
        reorder(scales["m"][:], sc_raw["m"][:])
        reorder(codes["m"][:], wm_raw[:])
        load_wp(0)
        load_wp(1)
        load_scale_rows([nc.sync] * 4, sc_raw["d"], wd_scales)
        load_wp(2)
        second = [("p", 0, S), ("d", 0, HALF)]
        carry_scales(second, "second", gather_scales(second, "second"))
        load_wp(3)
        nc.sync.dma_start(out=wd_raw[:], in_=wd_words[0].rearrange("p n t -> p (n t)").bitcast(I32))
        gather_words([("m", 0, QUARTER), ("m", QUARTER, S), ("p", 0, HALF)], "first")
        third = [("d", HALF, S)]
        staged = gather_scales(third, "third", "staged_first")
        for n in range(PASSES * PACK):
            load_wo(*divmod(n, PACK))
        carry_scales(third, "third", staged)
        with nc.allow_non_contiguous_dma(reason="one bias value a partition"):
            nc.sync.dma_start(out=bias[:], in_=bo.rearrange("(c p) -> p c", p=P))

        for g, width in enumerate(GROUPS):
            if g in (0, 2):
                h_bf[g] = sbuf("h_bf%d" % g, [P, PASSES, width, PACK], BF16)
            if g != 3:
                h_codes[g] = sbuf("h_codes%d" % g, [P, PASSES, width], U32)
            h_sc[g] = sbuf("h_sc%d" % g, [P, PASSES, width], U8)

        feed("m", 0, 2, 3, 1)
        quantize_wp(0)
        gather_words([("d", 0, S), ("p", HALF, S)], "second", "wp_raw1")
        quantize_wp(1)
        feed("m", 5, 4, 6, 7)
        reorder(scales["d"][:], sc_raw["d"][:])
        spare = list(range(EARLY_BANKS, BANKS))
        ring = list(free)
        free[:] = spare[:3]
        turn_back(5, 2, 3)
        free[:] = ring
        feed("p", 0, 1, 4, 5)
        feed("d", 0)
        project("m", 8)
        project("m", 9)
        free.insert(0, spare[3])
        reorder(codes["d"][:], wd_raw[:])

        first_larger = sbuf("first_larger", [P, 3, CHUNK, PACK], F32, "wp_raw3")
        maximum(0, first_larger[:, 0:2])
        maximum(4, first_larger[:, 2:3])
        wo_pair = sbuf("wo_pair", [P, 2, WO_PART, PACK], BF16, "magnitude_m0")
        for part in range(2):
            round_wo(part, wo_pair[:, part])
        whole["m", 8] = sbuf("magnitude_m8", [P, 2, CHUNK, PACK], F32, "wp_bf")
        value["m", 8], value["m", 9] = whole["m", 8][:, 0], whole["m", 8][:, 1]
        project("p", 2)
        project("p", 3)
        transpose_sum(("h", 0), [larger[0], value["d", 0]])
        for u, tag, role, emptied in ((5, "magnitude_p0", "p", 2), (2, "magnitude_p4", "p", 3), (3, "magnitude_p5", "m", 8)):
            empty(role, emptied)
            maximum(u, sbuf("larger%d" % u, [P, 1, CHUNK, PACK], F32, tag)[:])
        round_sum(0)
        for role, u in (("d", 1), ("p", 6), ("d", 2), ("p", 7), ("d", 3), ("d", 4), ("p", 8)):
            project(role, u)
        for u, emptied in ((1, [("p", 6)]), (2, [("p", 7)]), (3, [("m", 9), ("d", 4), ("p", 8)])):
            subtract(u)
            for role, other in emptied:
                empty(role, other)
        for role, u in (("p", 9), ("m", 10), ("d", 5), ("p", 10), ("d", 6), ("m", 11), ("d", 7), ("p", 11)):
            project(role, u)
        empty("p", 9)
        empty("m", 10)

        maximum(6)
        wo_mx["codes"] = sbuf("wo_codes", [P, PASSES * N], U32, "magnitude_p4")
        wo_mx["scales"] = sbuf("wo_sc", [P, PASSES * N], U8)
        pair = slice(0, 2 * WO_PART)
        quantize(wo_mx["codes"][:, pair], wo_mx["scales"][:, pair], wo_pair[:].rearrange("p a c j -> p (a c j)"))
        h_bf[1] = sbuf("h_bf1", [P, PASSES, GROUPS[1], PACK], BF16, "magnitude_m0")
        quantize_h(0)
        subtract_on_gpsimd(4, value["d", 4])
        project("d", 8)
        decode(0, [0, 1])
        for u, emptied, following in ((5, ("p", 10), ("m", 12)), (6, ("m", 11), ("p", 12)), (7, ("p", 11), ("m", 13))):
            subtract(u)
            empty(*emptied)
            project("d", u + 4)
            project(*following)
        empty("d", 8)
        add_bias(0, [0, 1])
        project("p", 13)

        maximum(8)
        maximum(10)
        quantize_h(1)
        wo_last = sbuf("wo_last", [P, WO_PART, PACK], BF16, "magnitude_m10")
        round_wo(2, wo_last[:])
        transpose_sum(("h", 8), [larger[8], value["d", 8]])
        for emptied, following in ((("m", 12), ("d", 12)), (("p", 12), ("m", 14)), (("m", 13), ("m", 15))):
            empty(*emptied)
            project(*following)
        subtract(9)
        decode(1, [0, 1])
        empty("p", 13)
        subtract(10)
        round_sum(8)
        subtract(11)
        empty("d", 12)
        for role, u in (("p", 14), ("p", 15), ("d", 13), ("d", 15), ("d", 14)):
            project(role, u)
        empty("m", 14)
        empty("m", 15)

        maximum(12)
        last = slice(2 * WO_PART, 3 * WO_PART)
        quantize(wo_mx["codes"][:, last], wo_mx["scales"][:, last], wo_last[:].rearrange("p c j -> p (c j)"))
        h_bf[3, 0] = sbuf("h_bf30", [P, CHUNK, PACK], BF16, "magnitude_m10")
        h_bf[3, 1] = sbuf("h_bf31", [P, CHUNK, PACK], BF16)
        quantize_h(2)
        subtract_on_gpsimd(12, value["d", 12])
        turn_back(14, 15)
        empty("p", 14)
        empty("p", 15)
        subtract(13)
        add_bias(1, [0, 1])
        device_rest = sbuf("device_rest", [P, CHUNK - VECTOR_SHARE, PACK], F32)
        nc.scalar.copy(out=device_rest[:], in_=filled["d", 15][:, VECTOR_SHARE:CHUNK])
        n = N_TILES - 1
        bank = take_bank("third rows")
        for g in range(2):
            for b in range(PASSES):
                multiply(g, b, n, bank[:, starts[g] : starts[g + 1]])
        result = sbuf("result_third_rows", [P, HALF], F32)
        nc.scalar.activation(out=result[:], in_=bank[:], func=ACT.Identity, bias=bias[:, n : n + 1])
        nc.sync.dma_start(out=out[n * P : (n + 1) * P, 0:HALF], in_=result[:])
        give_back("third rows")
        decode_and_store(2, [0, 1])
        maximum(14, sbuf("larger14", [P, 1, CHUNK, PACK], F32)[:])
        h_codes[3] = sbuf("h_codes3", [P, PASSES, GROUPS[3]], U32, "magnitude_p14")
        maximum(15)
        decode_and_store(2, [2])
        for b in range(PASSES):
            quantize(h_codes[3][:, b], h_sc[3][:, b], h_bf[3, b][:].rearrange("p c j -> p (c j)"))
        h_bf[4] = sbuf("h_bf4", [P, PASSES, GROUPS[4], PACK], BF16, "magnitude_m10")
        decode_and_store(3, range(N_TILES))
        subtract(14)
        subtract(15, slice(0, VECTOR_SHARE))
        subtract_on_gpsimd(15, device_rest[:], slice(VECTOR_SHARE, CHUNK))

        g = len(GROUPS) - 1
        sums = [take_bank(("y", g, n))[:, 0 : GROUPS[g]] for n in range(N_TILES)]
        for b in range(PASSES):
            quantize_h(g, slice(b, b + 1))
        for b in range(PASSES):
            for n in range(N_TILES):
                multiply(g, b, n, sums[n])
        result = sbuf("result_last", [P, N_TILES, GROUPS[g]], F32)
        for n in range(N_TILES):
            if n == 1:
                nc.vector.tensor_scalar(
                    out=result[:, n, :], in0=sums[n], scalar1=bias[:, n : n + 1], scalar2=None, op0=ALU.add
                )
            else:
                nc.scalar.activation(out=result[:, n, :], in_=sums[n], func=ACT.Identity, bias=bias[:, n : n + 1])
            nc.sync.dma_start(out=rows_of(g, range(N_TILES))[:, n, :], in_=result[:, n, :])
